import numpy as np
import ml_dtypes


def mxq(x, axis, fmt="e4m3"):
    dtype, down = {"e4m3": (ml_dtypes.float8_e4m3fn, 7), "e5m2": (ml_dtypes.float8_e5m2, 14)}[fmt]
    v = np.moveaxis(np.asarray(x, np.float32).astype(ml_dtypes.bfloat16).astype(np.float64), axis, -1)
    blocks = v.reshape(v.shape[:-1] + (-1, 32))
    amax = np.abs(blocks).max(-1, keepdims=True)
    byte = np.maximum(np.where(amax > 0, np.frexp(amax)[1] - 1 + 127, 0) - down, 1)
    scale = np.exp2(byte - 127.0)
    codes = (blocks / scale).astype(np.float32).astype(dtype).astype(np.float64)
    return np.moveaxis((codes * scale).reshape(v.shape), -1, axis)


WIDE = False


def mx_kscale(k):
    if not WIDE:
        return np.ones(k)
    levels = np.array([10, -10, 5, -5, 0])
    if k % 512:
        return np.exp2(np.random.permutation(np.resize(levels, k // 32))).repeat(32)
    a = np.empty((k // 512, 16))
    for p in range(k // 512):
        a[p, :8] = np.random.permutation(np.resize(levels, 8))
        for g in range(8):
            far = levels[np.abs(levels - a[p, g]) >= 10]
            a[p, g + 8] = far[np.random.randint(len(far))]
    return np.exp2(a.ravel()).repeat(32)


def f64(x):
    return np.asarray(x).astype(np.float64)


def striped(idx):
    return np.tile(idx.reshape(-1, 16).T, (8, 1)).astype(np.uint16)


def unstriped(offs):
    return offs[:16].T.reshape(-1).astype(np.int64)


def striped8(idx):
    return np.concatenate([x.reshape(-1, 16).T for x in idx]).astype(np.uint16)


def runs(offs, k):
    lists = np.stack([offs[16 * r : 16 * r + 16].T.reshape(-1) for r in range(8)]).astype(np.int64)
    return lists[np.arange(k) % 512 // 64]


def pack_weight(w):
    k, n = w.shape
    w = f64(np.asarray(w, np.float32).astype(ml_dtypes.bfloat16)).reshape(k // 32, 32, n)
    amax = np.abs(w).max(1)
    byte = np.clip(np.where(amax > 0, np.frexp(amax)[1] - 1 + 127 - 7, 1), 1, 254)
    scaled = (w * np.exp2(127.0 - byte)[:, None, :]).reshape(k, n).astype(np.float32)
    words = np.ascontiguousarray(scaled.reshape(k // 512, 128, 4, n).transpose(0, 1, 3, 2)).astype(ml_dtypes.float8_e4m3fn).view(np.uint8)
    return words, np.ascontiguousarray(byte.astype(np.uint8).reshape(k // 512, 16, n))


def unpack_weight(words, scales):
    g, p, n, _ = words.shape
    vals = np.ascontiguousarray(words).view(ml_dtypes.float8_e4m3fn).astype(np.float64) * np.repeat(np.exp2(scales.astype(np.float64) - 127.0), 8, axis=1)[..., None]
    return vals.transpose(0, 1, 3, 2).reshape(g * 512, n)

def planes(y):
    n, m = y.shape
    v = y.astype(np.float32).astype(ml_dtypes.bfloat16).astype(np.float64).reshape(n // 32, 32, m)
    top = np.abs(v).max(1)
    byte = np.clip(np.where(top > 0, np.frexp(top)[1] - 1 + 127 - 7, 1), 1, 254)
    codes = (v * np.exp2(127.0 - byte)[:, None, :]).reshape(n, m).astype(np.float32).astype(ml_dtypes.float8_e4m3fn).view(np.uint8)
    words = codes.reshape(n // 512, 128, 4, m).transpose(0, 1, 3, 2)
    return np.ascontiguousarray(words), np.ascontiguousarray(byte.astype(np.uint8).reshape(n // 512, 16, m))


K, T, S, N, H = 512, 2048, 512, 512, 512


def setup_inputs():
    n = np.random.standard_normal
    s = mx_kscale(K)[:, None]
    u = mx_kscale(H)
    packed_xT = pack_weight(n((K, T)) * s)
    packed_w1 = pack_weight(n((K, H)) / np.sqrt(K) / s)
    packed_w2 = pack_weight(n((H, N)) / np.sqrt(H) / u[:, None])
    return {
        "x_words": packed_xT[0],
        "x_scales": packed_xT[1],
        "w1_words": packed_w1[0],
        "w1_scales": packed_w1[1],
        "q": np.random.uniform(0.5, 1.5, (H, S)).astype(np.float32),
        "gn": (np.random.uniform(0.5, 1.5, (H, 1)) * u[:, None]).astype(np.float32),
        "w2_words": packed_w2[0],
        "w2_scales": packed_w2[1],
        "offs": striped(np.random.permutation(T)[:S]),
        "p1": striped8(np.stack([np.random.permutation(S) for _ in range(8)])),
        "p2": striped8(np.stack([np.random.permutation(S) for _ in range(8)])),
    }


def reference(x_words, x_scales, w1_words, w1_scales, q, gn, w2_words, w2_scales, offs, p1, p2):
    xq = unpack_weight(x_words, x_scales)[:, unstriped(offs)]
    y = unpack_weight(w1_words, w1_scales).T @ xq
    d1 = y[np.arange(H)[:, None], runs(p1, H)] - y
    s1 = f64(q) / ((d1) ** 2 + 1)
    d2 = y[np.arange(H)[:, None], runs(p2, H)] - y
    s2 = f64(q) / ((d2) ** 2 + 1)
    z = f64(gn) * (d1 * ((s1) ** 2 - s1) + d2 * ((s2) ** 2 - s2))
    out_0 = unpack_weight(w2_words, w2_scales).T @ mxq(z, 0, "e4m3")
    return (out_0,) + planes(out_0)

@@ -1,0 +1,175 @@
+from contextlib import ExitStack
+
+import concourse.mybir as mybir
+
+F32 = mybir.dt.float32
+BF16 = mybir.dt.bfloat16
+I32 = mybir.dt.int32
+U32 = mybir.dt.uint32
+U16 = mybir.dt.uint16
+U8 = mybir.dt.uint8
+FP8X4 = mybir.dt.float8_e4m3fn_x4
+ACT = mybir.ActivationFunctionType
+MULT = mybir.AluOpType.mult
+ADD = mybir.AluOpType.add
+SUBTRACT = mybir.AluOpType.subtract
+
+P = 128
+PACK = 4
+T = 2048
+S = 512
+CHUNK = 128
+CHUNKS = S // CHUNK
+LIST_COLS = CHUNK // 16
+SHRINK = 1.0
+FLOPS = 2 * 2 * 512 * 512 * 512
+
+
+def words_view(words):
+    return words[0].rearrange("p n t -> p (n t)").bitcast(I32)
+
+
+def load_scale_rows(queue, plane, scales, quads):
+    for quad in quads:
+        queue.dma_start(out=plane[32 * quad : 32 * quad + 4, :].bitcast(I32), in_=scales[0, 4 * quad : 4 * quad + 4, :].bitcast(I32))
+
+
+def deal(engine, dealt, raw):
+    engine.tensor_copy(out=dealt.rearrange("p (t m) -> p t m", t=PACK), in_=raw.rearrange("p (m t) -> p t m", t=PACK))
+
+
+def tile_picked_ljpot_none_po_kernel(
+    tc, x_words, x_scales, w1_words, w1_scales, q, gn, w2_words, w2_scales, offs, p1, p2, out_0, out_1, out_2
+):
+    nc = tc.nc
+    with ExitStack() as ctx:
+        keep = ctx.enter_context(tc.tile_pool(name="keep", bufs=1))
+        work = ctx.enter_context(tc.tile_pool(name="work", bufs=3))
+        psum = ctx.enter_context(tc.psum_pool(name="psum", bufs=1))
+
+        offs_sb = keep.tile([P, S // 16], U16, name="offs_sb")
+        p1_sb = keep.tile([P, S // 16], U16, name="p1_sb")
+        p2_sb = keep.tile([P, S // 16], U16, name="p2_sb")
+        x_table = keep.tile([P, T], I32, name="x_table", align_bytes=64)
+        x_plane = keep.tile([P, T], U8, name="x_plane", tag="x_plane_then_q", align_bytes=64)
+        w1_raw = keep.tile([P, S], I32, name="w1_raw", tag="raw_words", align_bytes=64)
+        raw_plane = keep.tile([P, S], U8, name="raw_plane", align_bytes=64)
+        gn_sb = keep.tile([P, PACK], F32, name="gn_sb", align_bytes=64)
+        gain = keep.tile([P, PACK], F32, name="gain", align_bytes=64)
+        warm_in = keep.tile([P, 1], F32, name="warm_in")
+        warm_out = keep.tile([P, 1], F32, name="warm_out")
+
+        nc.sync.dma_start(offs_sb[:], offs)
+        nc.sync.dma_start(p1_sb[:], p1)
+        nc.sync.dma_start(p2_sb[:], p2)
+        nc.sync.dma_start(out=x_table[:], in_=words_view(x_words))
+        nc.vector.memset(x_plane[:].bitcast(I32), 0)
+        nc.vector.memset(warm_in[:], 1.0)
+        nc.scalar.activation(out=warm_out[:], in_=warm_in[:], func=ACT.Abs_reciprocal_sqrt)
+        load_scale_rows(nc.sync, x_plane, x_scales, range(4))
+        nc.gpsimd.dma_start(out=w1_raw[:], in_=words_view(w1_words))
+        nc.vector.memset(raw_plane[:].bitcast(I32), 0)
+        load_scale_rows(nc.gpsimd, raw_plane, w1_scales, range(1))
+        load_scale_rows(nc.sync, raw_plane, w1_scales, range(1, 4))
+        nc.gpsimd.dma_start(out=gn_sb[:], in_=gn.rearrange("(p t) o -> p (t o)", t=PACK))
+        nc.gpsimd.tensor_scalar(gain[:], gn_sb[:], SHRINK * SHRINK, 0.0, MULT, ADD)
+
+        x_codes = keep.tile([P, S], I32, name="x_codes", align_bytes=64)
+        x_picked_plane = keep.tile([P, S], U8, name="x_picked_plane", align_bytes=64)
+        nc.vector.tensor_copy(x_picked_plane[:], x_plane[:].indirect(offs_sb[:]))
+        w1_codes = keep.tile([P, S], I32, name="w1_codes", align_bytes=64)
+        w1_plane = keep.tile([P, S], U8, name="w1_plane", align_bytes=64)
+        deal(nc.vector, w1_codes[:].bitcast(U32), w1_raw[:].bitcast(U32))
+        deal(nc.vector, w1_plane[:], raw_plane[:])
+        nc.vector.tensor_copy(x_codes[:].bitcast(U32), x_table[:].bitcast(U32).indirect(offs_sb[:]))
+
+        q_sb = keep.tile([P, PACK, S], F32, name="q_sb", tag="x_plane_then_q", align_bytes=64)
+        nc.sync.dma_start(out=q_sb[:], in_=q.rearrange("(p t) j -> p t j", t=PACK))
+        w2_raw = keep.tile([P, S], I32, name="w2_raw", tag="raw_words", align_bytes=64)
+        nc.sync.dma_start(out=w2_raw[:], in_=words_view(w2_words))
+        load_scale_rows(nc.sync, raw_plane, w2_scales, range(4))
+        w2_codes = keep.tile([P, S], I32, name="w2_codes", align_bytes=64)
+        w2_plane = keep.tile([P, S], U8, name="w2_plane", align_bytes=64)
+        deal(nc.vector, w2_codes[:].bitcast(U32), w2_raw[:].bitcast(U32))
+        deal(nc.vector, w2_plane[:], raw_plane[:])
+
+        y_window = []
+        y_own = []
+        for t in range(PACK):
+            cols = slice(P * t, P * (t + 1))
+            y_bank = psum.tile([P, S], F32, name="y_bank", bufs=4)
+            nc.tensor.matmul_mx(
+                out=y_bank[:],
+                lhsT=w1_codes[:, cols].bitcast(FP8X4),
+                lhsT_scale=w1_plane[:, cols],
+                rhs=x_codes[:].bitcast(FP8X4),
+                rhs_scale=x_picked_plane[:],
+                start=True,
+                stop=True,
+            )
+            window = keep.tile([P, S], F32, name="y_window%d" % t, align_bytes=64)
+            nc.scalar.copy(out=window[:], in_=y_bank[:])
+            y_window.append(window)
+            own = keep.tile([P, S], F32, name="y_own%d" % t, align_bytes=64)
+            nc.scalar.copy(out=own[:], in_=y_bank[:])
+            y_own.append(own)
+
+        out_plane = keep.tile([P, S], U8, name="out_plane", align_bytes=64)
+        out_rows = out_0.rearrange("(p t) j -> p t j", t=PACK)
+        out_words = words_view(out_1)
+
+        for c in range(CHUNKS):
+            js = slice(CHUNK * c, CHUNK * (c + 1))
+            z_planes = work.tile([P, PACK, CHUNK], BF16, name="z_planes", bufs=2, align_bytes=64)
+            for half in range(2):
+                ts = slice(2 * half, 2 * half + 2)
+                d = work.tile([P, 2, 2, CHUNK], F32, name="d", bufs=8, align_bytes=64)
+                for u in range(2):
+                    for k, partners in enumerate((p1_sb, p2_sb)):
+                        t = 2 * half + u
+                        nc.vector.tensor_tensor(
+                            d[:, u, k, :], y_window[t][:].indirect(partners[:, LIST_COLS * c : LIST_COLS * (c + 1)]), y_own[t][:, js], SUBTRACT
+                        )
+                flat = "p u k j -> p (u k j)"
+                d2 = work.tile([P, S], F32, name="d2", align_bytes=64)
+                nc.scalar.activation(out=d2[:], in_=d[:].rearrange(flat), func=ACT.Square)
+                denom2 = work.tile([P, S], F32, name="denom2", align_bytes=64)
+                nc.scalar.activation(out=denom2[:], in_=d2[:], func=ACT.Square, scale=SHRINK, bias=SHRINK)
+                soft = work.tile([P, 2, 2, CHUNK], F32, name="soft", bufs=4, align_bytes=64)
+                nc.scalar.activation(out=soft[:].rearrange(flat), in_=denom2[:], func=ACT.Abs_reciprocal_sqrt)
+                s = work.tile([P, 2, 2, CHUNK], F32, name="s", align_bytes=64)
+                nc.vector.tensor_tensor(s[:], soft[:], q_sb[:, ts, js].unsqueeze(2).to_broadcast([P, 2, 2, CHUNK]), MULT)
+                poly = work.tile([P, 2, 2, CHUNK], F32, name="poly", align_bytes=64)
+                nc.vector.scalar_tensor_tensor(poly[:].rearrange(flat), s[:].rearrange(flat), 1.0 / SHRINK, s[:].rearrange(flat), SUBTRACT, MULT)
+                force = work.tile([P, 2, 2, CHUNK], F32, name="force", align_bytes=64)
+                for u in range(2):
+                    t = 2 * half + u
+                    nc.vector.scalar_tensor_tensor(force[:, u], poly[:, u], gain[:, t : t + 1], d[:, u], MULT, MULT)
+                nc.vector.tensor_tensor(z_planes[:, ts, :], force[:, :, 0, :], force[:, :, 1, :], ADD)
+            z16 = work.tile([P, CHUNK, PACK], BF16, name="z16", bufs=2, align_bytes=64)
+            nc.scalar.copy(out=z16[:].rearrange("p (c i) t -> p c t i", i=4), in_=z_planes[:].rearrange("p t (c i) -> p c t i", i=4))
+            z_codes = work.tile([P, CHUNK], I32, name="z_codes", bufs=2, align_bytes=64)
+            z_plane = work.tile([P, CHUNK], U8, name="z_plane", bufs=2, align_bytes=64)
+            nc.vector.quantize_mx(out=z_codes[:].bitcast(FP8X4), scales=z_plane[:], in_=z16[:].rearrange("p j t -> p (j t)"))
+            out_bank = psum.tile([P, S], F32, name="out_bank", bufs=2)
+            for t in range(PACK):
+                cols = slice(P * t, P * (t + 1))
+                nc.tensor.matmul_mx(
+                    out=out_bank[:, cols],
+                    lhsT=w2_codes[:, cols].bitcast(FP8X4),
+                    lhsT_scale=w2_plane[:, cols],
+                    rhs=z_codes[:].bitcast(FP8X4),
+                    rhs_scale=z_plane[:],
+                    start=True,
+                    stop=True,
+                )
+            result16 = work.tile([P, CHUNK, PACK], BF16, name="result16", bufs=2, align_bytes=64)
+            nc.scalar.copy(out=result16[:], in_=out_bank[:].rearrange("p (t j) -> p j t", t=PACK))
+            result = work.tile([P, PACK, CHUNK], F32, name="result", bufs=4, align_bytes=64)
+            nc.scalar.copy(out=result[:].rearrange("p t j -> p (t j)"), in_=out_bank[:])
+            nc.sync.dma_start(out=out_rows[:, :, js], in_=result[:])
+            out_codes = work.tile([P, CHUNK], I32, name="out_codes", bufs=4, align_bytes=64)
+            nc.vector.quantize_mx(out=out_codes[:].bitcast(FP8X4), scales=out_plane[:, js], in_=result16[:].rearrange("p j t -> p (j t)"))
+            nc.sync.dma_start(out=out_words[:, js], in_=out_codes[:])
+        for quad in range(4):
+            nc.sync.dma_start(out=out_2[0, 4 * quad : 4 * quad + 4, :].bitcast(I32), in_=out_plane[32 * quad : 32 * quad + 4, :].bitcast(I32))

@@ -21,7 +21,7 @@ S = 512
 CHUNK = 128
 CHUNKS = S // CHUNK
 LIST_COLS = CHUNK // 16
-SHRINK = 1.0
+HALF = S // 2
 FLOPS = 2 * 2 * 512 * 512 * 512
 
 
@@ -54,8 +54,8 @@ def tile_picked_ljpot_none_po_kernel(
         x_plane = keep.tile([P, T], U8, name="x_plane", tag="x_plane_then_q", align_bytes=64)
         w1_raw = keep.tile([P, S], I32, name="w1_raw", tag="raw_words", align_bytes=64)
         raw_plane = keep.tile([P, S], U8, name="raw_plane", align_bytes=64)
+        w2_raw_plane = keep.tile([P, S], U8, name="w2_raw_plane", align_bytes=64)
         gn_sb = keep.tile([P, PACK], F32, name="gn_sb", align_bytes=64)
-        gain = keep.tile([P, PACK], F32, name="gain", align_bytes=64)
         warm_in = keep.tile([P, 1], F32, name="warm_in")
         warm_out = keep.tile([P, 1], F32, name="warm_out")
 
@@ -71,87 +71,123 @@ def tile_picked_ljpot_none_po_kernel(
         nc.vector.memset(raw_plane[:].bitcast(I32), 0)
         load_scale_rows(nc.gpsimd, raw_plane, w1_scales, range(1))
         load_scale_rows(nc.sync, raw_plane, w1_scales, range(1, 4))
+        nc.vector.memset(w2_raw_plane[:].bitcast(I32), 0)
+        load_scale_rows(nc.sync, w2_raw_plane, w2_scales, range(4))
         nc.gpsimd.dma_start(out=gn_sb[:], in_=gn.rearrange("(p t) o -> p (t o)", t=PACK))
-        nc.gpsimd.tensor_scalar(gain[:], gn_sb[:], SHRINK * SHRINK, 0.0, MULT, ADD)
 
-        x_codes = keep.tile([P, S], I32, name="x_codes", align_bytes=64)
-        x_picked_plane = keep.tile([P, S], U8, name="x_picked_plane", align_bytes=64)
-        nc.vector.tensor_copy(x_picked_plane[:], x_plane[:].indirect(offs_sb[:]))
         w1_codes = keep.tile([P, S], I32, name="w1_codes", align_bytes=64)
         w1_plane = keep.tile([P, S], U8, name="w1_plane", align_bytes=64)
-        deal(nc.vector, w1_codes[:].bitcast(U32), w1_raw[:].bitcast(U32))
-        deal(nc.vector, w1_plane[:], raw_plane[:])
-        nc.vector.tensor_copy(x_codes[:].bitcast(U32), x_table[:].bitcast(U32).indirect(offs_sb[:]))
+        deal(nc.gpsimd, w1_codes[:].bitcast(U32), w1_raw[:].bitcast(U32))
+        deal(nc.gpsimd, w1_plane[:], raw_plane[:])
+        x_codes = []
+        x_picked_plane = []
+        for h in range(2):
+            picked = keep.tile([P, HALF], U8, name="x_picked_plane%d" % h, align_bytes=64)
+            nc.vector.tensor_copy(picked[:], x_plane[:].indirect(offs_sb[:, 16 * h : 16 * (h + 1)]))
+            x_picked_plane.append(picked)
+            codes = keep.tile([P, HALF], I32, name="x_codes%d" % h, align_bytes=64)
+            nc.vector.tensor_copy(codes[:].bitcast(U32), x_table[:].bitcast(U32).indirect(offs_sb[:, 16 * h : 16 * (h + 1)]))
+            x_codes.append(codes)
 
         q_sb = keep.tile([P, PACK, S], F32, name="q_sb", tag="x_plane_then_q", align_bytes=64)
         nc.sync.dma_start(out=q_sb[:], in_=q.rearrange("(p t) j -> p t j", t=PACK))
         w2_raw = keep.tile([P, S], I32, name="w2_raw", tag="raw_words", align_bytes=64)
         nc.sync.dma_start(out=w2_raw[:], in_=words_view(w2_words))
-        load_scale_rows(nc.sync, raw_plane, w2_scales, range(4))
         w2_codes = keep.tile([P, S], I32, name="w2_codes", align_bytes=64)
         w2_plane = keep.tile([P, S], U8, name="w2_plane", align_bytes=64)
         deal(nc.vector, w2_codes[:].bitcast(U32), w2_raw[:].bitcast(U32))
-        deal(nc.vector, w2_plane[:], raw_plane[:])
+        deal(nc.vector, w2_plane[:], w2_raw_plane[:])
 
         y_window = []
         y_own = []
+        late_banks = []
         for t in range(PACK):
             cols = slice(P * t, P * (t + 1))
-            y_bank = psum.tile([P, S], F32, name="y_bank", bufs=4)
-            nc.tensor.matmul_mx(
-                out=y_bank[:],
-                lhsT=w1_codes[:, cols].bitcast(FP8X4),
-                lhsT_scale=w1_plane[:, cols],
-                rhs=x_codes[:].bitcast(FP8X4),
-                rhs_scale=x_picked_plane[:],
-                start=True,
-                stop=True,
-            )
             window = keep.tile([P, S], F32, name="y_window%d" % t, align_bytes=64)
-            nc.scalar.copy(out=window[:], in_=y_bank[:])
-            y_window.append(window)
             own = keep.tile([P, S], F32, name="y_own%d" % t, align_bytes=64)
-            nc.scalar.copy(out=own[:], in_=y_bank[:])
+            banks = []
+            for h in range(2):
+                bank = psum.tile([P, S], F32, name="bank", bufs=8)
+                nc.tensor.matmul_mx(
+                    out=bank[:, :HALF],
+                    lhsT=w1_codes[:, cols].bitcast(FP8X4),
+                    lhsT_scale=w1_plane[:, cols],
+                    rhs=x_codes[h][:].bitcast(FP8X4),
+                    rhs_scale=x_picked_plane[h][:],
+                    start=True,
+                    stop=True,
+                )
+                banks.append(bank)
+            nc.scalar.copy(out=window[:, :HALF], in_=banks[0][:, :HALF])
+            nc.scalar.copy(out=own[:, :HALF], in_=banks[0][:, :HALF])
+            nc.scalar.copy(out=window[:, HALF:], in_=banks[1][:, :HALF])
+            y_window.append(window)
             y_own.append(own)
+            late_banks.append(banks[1])
+        for t in range(PACK):
+            nc.scalar.copy(out=y_own[t][:, HALF:], in_=late_banks[t][:, :HALF])
 
         out_plane = keep.tile([P, S], U8, name="out_plane", align_bytes=64)
         out_rows = out_0.rearrange("(p t) j -> p t j", t=PACK)
         out_words = words_view(out_1)
+        flat = "p u k j -> p (u k j)"
+        pair_shape = [P, 2, 2, CHUNK]
+        pairs = range(2)
 
-        for c in range(CHUNKS):
+        def differences(h):
+            js = slice(HALF * h, HALF * (h + 1))
+            d = [work.tile([P, 2, 2, HALF], F32, name="d", bufs=4, align_bytes=64) for a in pairs]
+            for t in range(PACK):
+                for k, partners in enumerate((p1_sb, p2_sb)):
+                    nc.vector.tensor_tensor(
+                        d[t // 2][:, t % 2, k, :], y_window[t][:].indirect(partners[:, 16 * h : 16 * (h + 1)]), y_own[t][:, js], SUBTRACT
+                    )
+            return [[d[a][:, :, :, CHUNK * c : CHUNK * (c + 1)] for a in pairs] for c in range(2)]
+
+        def softened(d):
+            d2 = [work.tile(pair_shape, F32, name="d2", bufs=2, align_bytes=64) for a in pairs]
+            denom2 = [work.tile(pair_shape, F32, name="denom2", bufs=2, align_bytes=64) for a in pairs]
+            soft = [work.tile(pair_shape, F32, name="soft", bufs=8, align_bytes=64) for a in pairs]
+            for a in pairs:
+                nc.scalar.activation(out=d2[a][:], in_=d[a], func=ACT.Square)
+            for a in pairs:
+                nc.scalar.activation(out=denom2[a][:], in_=d2[a][:], func=ACT.Square, bias=1.0)
+            for a in pairs:
+                nc.scalar.activation(out=soft[a][:], in_=denom2[a][:], func=ACT.Abs_reciprocal_sqrt)
+            return soft
+
+        def forces(c, d, soft):
             js = slice(CHUNK * c, CHUNK * (c + 1))
-            z_planes = work.tile([P, PACK, CHUNK], BF16, name="z_planes", bufs=2, align_bytes=64)
-            for half in range(2):
-                ts = slice(2 * half, 2 * half + 2)
-                d = work.tile([P, 2, 2, CHUNK], F32, name="d", bufs=8, align_bytes=64)
-                for u in range(2):
-                    for k, partners in enumerate((p1_sb, p2_sb)):
-                        t = 2 * half + u
-                        nc.vector.tensor_tensor(
-                            d[:, u, k, :], y_window[t][:].indirect(partners[:, LIST_COLS * c : LIST_COLS * (c + 1)]), y_own[t][:, js], SUBTRACT
-                        )
-                flat = "p u k j -> p (u k j)"
-                d2 = work.tile([P, S], F32, name="d2", align_bytes=64)
-                nc.scalar.activation(out=d2[:], in_=d[:].rearrange(flat), func=ACT.Square)
-                denom2 = work.tile([P, S], F32, name="denom2", align_bytes=64)
-                nc.scalar.activation(out=denom2[:], in_=d2[:], func=ACT.Square, scale=SHRINK, bias=SHRINK)
-                soft = work.tile([P, 2, 2, CHUNK], F32, name="soft", bufs=4, align_bytes=64)
-                nc.scalar.activation(out=soft[:].rearrange(flat), in_=denom2[:], func=ACT.Abs_reciprocal_sqrt)
-                s = work.tile([P, 2, 2, CHUNK], F32, name="s", align_bytes=64)
-                nc.vector.tensor_tensor(s[:], soft[:], q_sb[:, ts, js].unsqueeze(2).to_broadcast([P, 2, 2, CHUNK]), MULT)
-                poly = work.tile([P, 2, 2, CHUNK], F32, name="poly", align_bytes=64)
-                nc.vector.scalar_tensor_tensor(poly[:].rearrange(flat), s[:].rearrange(flat), 1.0 / SHRINK, s[:].rearrange(flat), SUBTRACT, MULT)
-                force = work.tile([P, 2, 2, CHUNK], F32, name="force", align_bytes=64)
-                for u in range(2):
-                    t = 2 * half + u
-                    nc.vector.scalar_tensor_tensor(force[:, u], poly[:, u], gain[:, t : t + 1], d[:, u], MULT, MULT)
-                nc.vector.tensor_tensor(z_planes[:, ts, :], force[:, :, 0, :], force[:, :, 1, :], ADD)
+            s = [work.tile(pair_shape, F32, name="s", bufs=2, align_bytes=64) for a in pairs]
+            poly = [work.tile(pair_shape, F32, name="poly", bufs=2, align_bytes=64) for a in pairs]
+            force = work.tile([P, PACK, 2, CHUNK], F32, name="force", bufs=2, align_bytes=64)
+            for a in pairs:
+                nc.vector.tensor_tensor(s[a][:], soft[a][:], q_sb[:, 2 * a : 2 * a + 2, js].unsqueeze(2).to_broadcast(pair_shape), MULT)
+            for a in pairs:
+                nc.vector.scalar_tensor_tensor(poly[a][:].rearrange(flat), s[a][:].rearrange(flat), 1.0, s[a][:].rearrange(flat), SUBTRACT, MULT)
+            for t in range(PACK):
+                nc.vector.scalar_tensor_tensor(force[:, t], poly[t // 2][:, t % 2], gn_sb[:, t : t + 1], d[t // 2][:, t % 2], MULT, MULT)
+            return force
+
+        def summed(c, force):
             z16 = work.tile([P, CHUNK, PACK], BF16, name="z16", bufs=2, align_bytes=64)
-            nc.scalar.copy(out=z16[:].rearrange("p (c i) t -> p c t i", i=4), in_=z_planes[:].rearrange("p t (c i) -> p c t i", i=4))
+            if c == CHUNKS - 1:
+                nc.vector.tensor_tensor(z16[:], force[:, :, 0, :].rearrange("p t j -> p j t"), force[:, :, 1, :].rearrange("p t j -> p j t"), ADD)
+                return z16
+            z_planes = work.tile([P, PACK, CHUNK], BF16, name="z_planes", bufs=2, align_bytes=64)
+            nc.vector.tensor_tensor(z_planes[:], force[:, :, 0, :], force[:, :, 1, :], ADD)
+            woven = z16[:].rearrange("p (c i) t -> p c t i", i=4)
+            planar = z_planes[:].rearrange("p t (c i) -> p c t i", i=4)
+            nc.scalar.copy(out=woven, in_=planar)
+            return z16
+
+        def layer(c, z16):
+            js = slice(CHUNK * c, CHUNK * (c + 1))
+            last = c == CHUNKS - 1
             z_codes = work.tile([P, CHUNK], I32, name="z_codes", bufs=2, align_bytes=64)
             z_plane = work.tile([P, CHUNK], U8, name="z_plane", bufs=2, align_bytes=64)
             nc.vector.quantize_mx(out=z_codes[:].bitcast(FP8X4), scales=z_plane[:], in_=z16[:].rearrange("p j t -> p (j t)"))
-            out_bank = psum.tile([P, S], F32, name="out_bank", bufs=2)
+            out_bank = psum.tile([P, S], F32, name="bank", bufs=8)
             for t in range(PACK):
                 cols = slice(P * t, P * (t + 1))
                 nc.tensor.matmul_mx(
@@ -167,9 +203,17 @@ def tile_picked_ljpot_none_po_kernel(
             nc.scalar.copy(out=result16[:], in_=out_bank[:].rearrange("p (t j) -> p j t", t=PACK))
             result = work.tile([P, PACK, CHUNK], F32, name="result", bufs=4, align_bytes=64)
             nc.scalar.copy(out=result[:].rearrange("p t j -> p (t j)"), in_=out_bank[:])
-            nc.sync.dma_start(out=out_rows[:, :, js], in_=result[:])
+            (nc.scalar if last else nc.sync).dma_start(out=out_rows[:, :, js], in_=result[:])
             out_codes = work.tile([P, CHUNK], I32, name="out_codes", bufs=4, align_bytes=64)
             nc.vector.quantize_mx(out=out_codes[:].bitcast(FP8X4), scales=out_plane[:, js], in_=result16[:].rearrange("p j t -> p (j t)"))
             nc.sync.dma_start(out=out_words[:, js], in_=out_codes[:])
+
+        diffs = differences(0) + differences(1)
+        softs = [softened(diffs[c]) for c in range(2)]
+        for c in range(CHUNKS):
+            force = forces(c, diffs[c], softs[c])
+            if c + 2 < CHUNKS:
+                softs.append(softened(diffs[c + 2]))
+            layer(c, summed(c, force))
         for quad in range(4):
-            nc.sync.dma_start(out=out_2[0, 4 * quad : 4 * quad + 4, :].bitcast(I32), in_=out_plane[32 * quad : 32 * quad + 4, :].bitcast(I32))
+            (nc.sync if quad < 2 else nc.scalar).dma_start(out=out_2[0, 4 * quad : 4 * quad + 4, :].bitcast(I32), in_=out_plane[32 * quad : 32 * quad + 4, :].bitcast(I32))

@@ -59,25 +59,30 @@ def tile_picked_ljpot_none_po_kernel(
         warm_in = keep.tile([P, 1], F32, name="warm_in")
         warm_out = keep.tile([P, 1], F32, name="warm_out")
 
+        x_rows = keep.tile([P, T // 4], I32, name="x_rows", align_bytes=64)
+        for quad in range(4):
+            nc.sync.dma_start(out=x_rows[32 * quad : 32 * quad + 4, :], in_=x_scales[0, 4 * quad : 4 * quad + 4, :].bitcast(I32))
         nc.sync.dma_start(offs_sb[:], offs)
-        nc.sync.dma_start(p1_sb[:], p1)
-        nc.sync.dma_start(p2_sb[:], p2)
+        nc.vector.memset(raw_plane[:].bitcast(I32), 0)
+        load_scale_rows(nc.sync, raw_plane, w1_scales, range(2))
         nc.sync.dma_start(out=x_table[:], in_=words_view(x_words))
-        nc.vector.memset(x_plane[:].bitcast(I32), 0)
         nc.vector.memset(warm_in[:], 1.0)
         nc.scalar.activation(out=warm_out[:], in_=warm_in[:], func=ACT.Abs_reciprocal_sqrt)
-        load_scale_rows(nc.sync, x_plane, x_scales, range(4))
         nc.gpsimd.dma_start(out=w1_raw[:], in_=words_view(w1_words))
-        nc.vector.memset(raw_plane[:].bitcast(I32), 0)
-        load_scale_rows(nc.gpsimd, raw_plane, w1_scales, range(1))
-        load_scale_rows(nc.sync, raw_plane, w1_scales, range(1, 4))
+        load_scale_rows(nc.gpsimd, raw_plane, w1_scales, range(2, 4))
+        nc.sync.dma_start(p1_sb[:], p1)
+        nc.sync.dma_start(p2_sb[:], p2)
+        nc.vector.memset(x_plane[:].bitcast(I32), 0)
+        for quad in range(4):
+            rows = slice(32 * quad, 32 * quad + 4)
+            nc.vector.tensor_copy(out=x_plane[rows, :].bitcast(I32), in_=x_rows[rows, :])
         nc.vector.memset(w2_raw_plane[:].bitcast(I32), 0)
         load_scale_rows(nc.sync, w2_raw_plane, w2_scales, range(4))
         nc.gpsimd.dma_start(out=gn_sb[:], in_=gn.rearrange("(p t) o -> p (t o)", t=PACK))
 
         w1_codes = keep.tile([P, S], I32, name="w1_codes", align_bytes=64)
         w1_plane = keep.tile([P, S], U8, name="w1_plane", align_bytes=64)
-        deal(nc.gpsimd, w1_codes[:].bitcast(U32), w1_raw[:].bitcast(U32))
+        deal(nc.vector, w1_codes[:].bitcast(U32), w1_raw[:].bitcast(U32))
         deal(nc.gpsimd, w1_plane[:], raw_plane[:])
         x_codes = []
         x_picked_plane = []
@@ -131,7 +136,6 @@ def tile_picked_ljpot_none_po_kernel(
         out_rows = out_0.rearrange("(p t) j -> p t j", t=PACK)
         out_words = words_view(out_1)
         flat = "p u k j -> p (u k j)"
-        pair_shape = [P, 2, 2, CHUNK]
         pairs = range(2)
 
         def differences(h):
@@ -142,12 +146,13 @@ def tile_picked_ljpot_none_po_kernel(
                     nc.vector.tensor_tensor(
                         d[t // 2][:, t % 2, k, :], y_window[t][:].indirect(partners[:, 16 * h : 16 * (h + 1)]), y_own[t][:, js], SUBTRACT
                     )
-            return [[d[a][:, :, :, CHUNK * c : CHUNK * (c + 1)] for a in pairs] for c in range(2)]
+            return d
 
-        def softened(d):
-            d2 = [work.tile(pair_shape, F32, name="d2", bufs=2, align_bytes=64) for a in pairs]
-            denom2 = [work.tile(pair_shape, F32, name="denom2", bufs=2, align_bytes=64) for a in pairs]
-            soft = [work.tile(pair_shape, F32, name="soft", bufs=8, align_bytes=64) for a in pairs]
+        def pair_tiles(name, width, bufs):
+            return [work.tile([P, 2, 2, width], F32, name=name, bufs=bufs, align_bytes=64) for a in pairs]
+
+        def softened(d, width):
+            d2, denom2, soft = pair_tiles("d2", width, 2), pair_tiles("denom2", width, 2), pair_tiles("soft", width, 8)
             for a in pairs:
                 nc.scalar.activation(out=d2[a][:], in_=d[a], func=ACT.Square)
             for a in pairs:
@@ -156,42 +161,37 @@ def tile_picked_ljpot_none_po_kernel(
                 nc.scalar.activation(out=soft[a][:], in_=denom2[a][:], func=ACT.Abs_reciprocal_sqrt)
             return soft
 
-        def forces(c, d, soft):
-            js = slice(CHUNK * c, CHUNK * (c + 1))
-            s = [work.tile(pair_shape, F32, name="s", bufs=2, align_bytes=64) for a in pairs]
-            poly = [work.tile(pair_shape, F32, name="poly", bufs=2, align_bytes=64) for a in pairs]
-            force = work.tile([P, PACK, 2, CHUNK], F32, name="force", bufs=2, align_bytes=64)
+        def forces(js, width, d, soft):
+            s, poly = pair_tiles("s", width, 2), pair_tiles("poly", width, 2)
+            force = work.tile([P, PACK, 2, width], F32, name="force", bufs=2, align_bytes=64)
             for a in pairs:
-                nc.vector.tensor_tensor(s[a][:], soft[a][:], q_sb[:, 2 * a : 2 * a + 2, js].unsqueeze(2).to_broadcast(pair_shape), MULT)
+                nc.vector.tensor_tensor(s[a][:], soft[a], q_sb[:, 2 * a : 2 * a + 2, js].unsqueeze(2).to_broadcast([P, 2, 2, width]), MULT)
             for a in pairs:
                 nc.vector.scalar_tensor_tensor(poly[a][:].rearrange(flat), s[a][:].rearrange(flat), 1.0, s[a][:].rearrange(flat), SUBTRACT, MULT)
             for t in range(PACK):
                 nc.vector.scalar_tensor_tensor(force[:, t], poly[t // 2][:, t % 2], gn_sb[:, t : t + 1], d[t // 2][:, t % 2], MULT, MULT)
             return force
 
-        def summed(c, force):
-            z16 = work.tile([P, CHUNK, PACK], BF16, name="z16", bufs=2, align_bytes=64)
-            if c == CHUNKS - 1:
+        def summed(force, width):
+            z16 = work.tile([P, width, PACK], BF16, name="z16", bufs=2, align_bytes=64)
+            if width < CHUNK:
                 nc.vector.tensor_tensor(z16[:], force[:, :, 0, :].rearrange("p t j -> p j t"), force[:, :, 1, :].rearrange("p t j -> p j t"), ADD)
                 return z16
             z_planes = work.tile([P, PACK, CHUNK], BF16, name="z_planes", bufs=2, align_bytes=64)
             nc.vector.tensor_tensor(z_planes[:], force[:, :, 0, :], force[:, :, 1, :], ADD)
-            woven = z16[:].rearrange("p (c i) t -> p c t i", i=4)
-            planar = z_planes[:].rearrange("p t (c i) -> p c t i", i=4)
-            nc.scalar.copy(out=woven, in_=planar)
+            nc.scalar.copy(out=z16[:].rearrange("p (c i) t -> p c t i", i=4), in_=z_planes[:].rearrange("p t (c i) -> p c t i", i=4))
             return z16
 
-        def layer(c, z16):
-            js = slice(CHUNK * c, CHUNK * (c + 1))
-            last = c == CHUNKS - 1
-            z_codes = work.tile([P, CHUNK], I32, name="z_codes", bufs=2, align_bytes=64)
-            z_plane = work.tile([P, CHUNK], U8, name="z_plane", bufs=2, align_bytes=64)
+        def layer(js, width, z16):
+            z_codes = work.tile([P, width], I32, name="z_codes", bufs=2, align_bytes=64)
+            z_plane = work.tile([P, width], U8, name="z_plane", bufs=2, align_bytes=64)
             nc.vector.quantize_mx(out=z_codes[:].bitcast(FP8X4), scales=z_plane[:], in_=z16[:].rearrange("p j t -> p (j t)"))
             out_bank = psum.tile([P, S], F32, name="bank", bufs=8)
+            sums = out_bank[:, : PACK * width].rearrange("p (t j) -> p t j", t=PACK)
             for t in range(PACK):
                 cols = slice(P * t, P * (t + 1))
                 nc.tensor.matmul_mx(
-                    out=out_bank[:, cols],
+                    out=sums[:, t, :],
                     lhsT=w2_codes[:, cols].bitcast(FP8X4),
                     lhsT_scale=w2_plane[:, cols],
                     rhs=z_codes[:].bitcast(FP8X4),
@@ -199,21 +199,31 @@ def tile_picked_ljpot_none_po_kernel(
                     start=True,
                     stop=True,
                 )
-            result16 = work.tile([P, CHUNK, PACK], BF16, name="result16", bufs=2, align_bytes=64)
-            nc.scalar.copy(out=result16[:], in_=out_bank[:].rearrange("p (t j) -> p j t", t=PACK))
-            result = work.tile([P, PACK, CHUNK], F32, name="result", bufs=4, align_bytes=64)
-            nc.scalar.copy(out=result[:].rearrange("p t j -> p (t j)"), in_=out_bank[:])
-            (nc.scalar if last else nc.sync).dma_start(out=out_rows[:, :, js], in_=result[:])
-            out_codes = work.tile([P, CHUNK], I32, name="out_codes", bufs=4, align_bytes=64)
+            result16 = work.tile([P, width, PACK], BF16, name="result16", bufs=2, align_bytes=64)
+            nc.scalar.copy(out=result16[:], in_=sums.rearrange("p t j -> p j t"))
+            result = work.tile([P, PACK, width], F32, name="result", bufs=4, align_bytes=64)
+            nc.scalar.copy(out=result[:], in_=sums)
+            (nc.scalar if js.stop == S else nc.sync).dma_start(out=out_rows[:, :, js], in_=result[:])
+            out_codes = work.tile([P, width], I32, name="out_codes", bufs=4, align_bytes=64)
             nc.vector.quantize_mx(out=out_codes[:].bitcast(FP8X4), scales=out_plane[:, js], in_=result16[:].rearrange("p j t -> p (j t)"))
             nc.sync.dma_start(out=out_words[:, js], in_=out_codes[:])
 
-        diffs = differences(0) + differences(1)
-        softs = [softened(diffs[c]) for c in range(2)]
+        halves = [differences(h) for h in range(2)]
+
+        def columns(tiles, start, width):
+            return [tiles[a][:, :, :, start : start + width] for a in pairs]
+
+        def soften_chunk(c):
+            return softened(columns(halves[c // 2], CHUNK * (c % 2), CHUNK), CHUNK)
+
+        softs = [soften_chunk(c) for c in range(3)]
         for c in range(CHUNKS):
-            force = forces(c, diffs[c], softs[c])
-            if c + 2 < CHUNKS:
-                softs.append(softened(diffs[c + 2]))
-            layer(c, summed(c, force))
+            width = CHUNK if c + 1 < CHUNKS else CHUNK // 2
+            for start in range(0, CHUNK, width):
+                js = slice(CHUNK * c + start, CHUNK * c + start + width)
+                force = forces(js, width, columns(halves[c // 2], CHUNK * (c % 2) + start, width), columns(softs[c], start, width))
+                if c + 3 < CHUNKS:
+                    softs.append(soften_chunk(c + 3))
+                layer(js, width, summed(force, width))
         for quad in range(4):
             (nc.sync if quad < 2 else nc.scalar).dma_start(out=out_2[0, 4 * quad : 4 * quad + 4, :].bitcast(I32), in_=out_plane[32 * quad : 32 * quad + 4, :].bitcast(I32))

@@ -50,9 +50,9 @@ def tile_picked_ljpot_none_po_kernel(
         offs_sb = keep.tile([P, S // 16], U16, name="offs_sb")
         p1_sb = keep.tile([P, S // 16], U16, name="p1_sb")
         p2_sb = keep.tile([P, S // 16], U16, name="p2_sb")
-        x_table = keep.tile([P, T], I32, name="x_table", align_bytes=64)
+        x_table = keep.tile([P, T], I32, name="x_table", tag="x_table_then_w2", align_bytes=64)
         x_plane = keep.tile([P, T], U8, name="x_plane", tag="x_plane_then_q", align_bytes=64)
-        w1_raw = keep.tile([P, S], I32, name="w1_raw", tag="raw_words", align_bytes=64)
+        w1_raw = keep.tile([P, S], I32, name="w1_raw", align_bytes=64)
         raw_plane = keep.tile([P, S], U8, name="raw_plane", align_bytes=64)
         w2_raw_plane = keep.tile([P, S], U8, name="w2_raw_plane", align_bytes=64)
         gn_sb = keep.tile([P, PACK], F32, name="gn_sb", align_bytes=64)
@@ -63,13 +63,12 @@ def tile_picked_ljpot_none_po_kernel(
         for quad in range(4):
             nc.sync.dma_start(out=x_rows[32 * quad : 32 * quad + 4, :], in_=x_scales[0, 4 * quad : 4 * quad + 4, :].bitcast(I32))
         nc.sync.dma_start(offs_sb[:], offs)
-        nc.vector.memset(raw_plane[:].bitcast(I32), 0)
-        load_scale_rows(nc.sync, raw_plane, w1_scales, range(2))
+        nc.sync.dma_start(out=w1_raw[:], in_=words_view(w1_words))
         nc.sync.dma_start(out=x_table[:], in_=words_view(x_words))
+        nc.vector.memset(raw_plane[:].bitcast(I32), 0)
+        load_scale_rows(nc.sync, raw_plane, w1_scales, range(4))
         nc.vector.memset(warm_in[:], 1.0)
         nc.scalar.activation(out=warm_out[:], in_=warm_in[:], func=ACT.Abs_reciprocal_sqrt)
-        nc.gpsimd.dma_start(out=w1_raw[:], in_=words_view(w1_words))
-        load_scale_rows(nc.gpsimd, raw_plane, w1_scales, range(2, 4))
         nc.sync.dma_start(p1_sb[:], p1)
         nc.sync.dma_start(p2_sb[:], p2)
         nc.vector.memset(x_plane[:].bitcast(I32), 0)
@@ -96,12 +95,12 @@ def tile_picked_ljpot_none_po_kernel(
 
         q_sb = keep.tile([P, PACK, S], F32, name="q_sb", tag="x_plane_then_q", align_bytes=64)
         nc.sync.dma_start(out=q_sb[:], in_=q.rearrange("(p t) j -> p t j", t=PACK))
-        w2_raw = keep.tile([P, S], I32, name="w2_raw", tag="raw_words", align_bytes=64)
+        w2_raw = keep.tile([P, S], I32, name="w2_raw", tag="x_table_then_w2", align_bytes=64)
         nc.sync.dma_start(out=w2_raw[:], in_=words_view(w2_words))
         w2_codes = keep.tile([P, S], I32, name="w2_codes", align_bytes=64)
         w2_plane = keep.tile([P, S], U8, name="w2_plane", align_bytes=64)
         deal(nc.vector, w2_codes[:].bitcast(U32), w2_raw[:].bitcast(U32))
-        deal(nc.vector, w2_plane[:], w2_raw_plane[:])
+        deal(nc.gpsimd, w2_plane[:], w2_raw_plane[:])
 
         y_window = []
         y_own = []
@@ -133,6 +132,7 @@ def tile_picked_ljpot_none_po_kernel(
             nc.scalar.copy(out=y_own[t][:, HALF:], in_=late_banks[t][:, :HALF])
 
         out_plane = keep.tile([P, S], U8, name="out_plane", align_bytes=64)
+        out_codes = keep.tile([P, S], I32, name="out_codes", align_bytes=64)
         out_rows = out_0.rearrange("(p t) j -> p t j", t=PACK)
         out_words = words_view(out_1)
         flat = "p u k j -> p (u k j)"
@@ -172,14 +172,12 @@ def tile_picked_ljpot_none_po_kernel(
                 nc.vector.scalar_tensor_tensor(force[:, t], poly[t // 2][:, t % 2], gn_sb[:, t : t + 1], d[t // 2][:, t % 2], MULT, MULT)
             return force
 
-        def summed(force, width):
-            z16 = work.tile([P, width, PACK], BF16, name="z16", bufs=2, align_bytes=64)
-            if width < CHUNK:
-                nc.vector.tensor_tensor(z16[:], force[:, :, 0, :].rearrange("p t j -> p j t"), force[:, :, 1, :].rearrange("p t j -> p j t"), ADD)
-                return z16
-            z_planes = work.tile([P, PACK, CHUNK], BF16, name="z_planes", bufs=2, align_bytes=64)
+        def summed(force, width, last):
+            z_planes = work.tile([P, PACK, width], BF16, name="z_planes", bufs=2, align_bytes=64)
             nc.vector.tensor_tensor(z_planes[:], force[:, :, 0, :], force[:, :, 1, :], ADD)
-            nc.scalar.copy(out=z16[:].rearrange("p (c i) t -> p c t i", i=4), in_=z_planes[:].rearrange("p t (c i) -> p c t i", i=4))
+            z16 = work.tile([P, width, PACK], BF16, name="z16", bufs=2, align_bytes=64)
+            weave = nc.vector.tensor_copy if last else nc.scalar.copy
+            weave(out=z16[:].rearrange("p (c i) t -> p c t i", i=4), in_=z_planes[:].rearrange("p t (c i) -> p c t i", i=4))
             return z16
 
         def layer(js, width, z16):
@@ -204,9 +202,10 @@ def tile_picked_ljpot_none_po_kernel(
             result = work.tile([P, PACK, width], F32, name="result", bufs=4, align_bytes=64)
             nc.scalar.copy(out=result[:], in_=sums)
             (nc.scalar if js.stop == S else nc.sync).dma_start(out=out_rows[:, :, js], in_=result[:])
-            out_codes = work.tile([P, width], I32, name="out_codes", bufs=4, align_bytes=64)
-            nc.vector.quantize_mx(out=out_codes[:].bitcast(FP8X4), scales=out_plane[:, js], in_=result16[:].rearrange("p j t -> p (j t)"))
-            nc.sync.dma_start(out=out_words[:, js], in_=out_codes[:])
+            nc.vector.quantize_mx(out=out_codes[:, js].bitcast(FP8X4), scales=out_plane[:, js], in_=result16[:].rearrange("p j t -> p (j t)"))
+            if js.stop % CHUNK == 0:
+                done = slice(js.stop - CHUNK, js.stop)
+                nc.sync.dma_start(out=out_words[:, done], in_=out_codes[:, done])
 
         halves = [differences(h) for h in range(2)]
 
@@ -224,6 +223,6 @@ def tile_picked_ljpot_none_po_kernel(
                 force = forces(js, width, columns(halves[c // 2], CHUNK * (c % 2) + start, width), columns(softs[c], start, width))
                 if c + 3 < CHUNKS:
                     softs.append(soften_chunk(c + 3))
-                layer(js, width, summed(force, width))
+                layer(js, width, summed(force, width, js.stop == S))
         for quad in range(4):
             (nc.sync if quad < 2 else nc.scalar).dma_start(out=out_2[0, 4 * quad : 4 * quad + 4, :].bitcast(I32), in_=out_plane[32 * quad : 32 * quad + 4, :].bitcast(I32))

@@ -56,8 +56,6 @@ def tile_picked_ljpot_none_po_kernel(
         raw_plane = keep.tile([P, S], U8, name="raw_plane", align_bytes=64)
         w2_raw_plane = keep.tile([P, S], U8, name="w2_raw_plane", align_bytes=64)
         gn_sb = keep.tile([P, PACK], F32, name="gn_sb", align_bytes=64)
-        warm_in = keep.tile([P, 1], F32, name="warm_in")
-        warm_out = keep.tile([P, 1], F32, name="warm_out")
 
         x_rows = keep.tile([P, T // 4], I32, name="x_rows", align_bytes=64)
         for quad in range(4):
@@ -67,8 +65,6 @@ def tile_picked_ljpot_none_po_kernel(
         nc.sync.dma_start(out=x_table[:], in_=words_view(x_words))
         nc.vector.memset(raw_plane[:].bitcast(I32), 0)
         load_scale_rows(nc.sync, raw_plane, w1_scales, range(4))
-        nc.vector.memset(warm_in[:], 1.0)
-        nc.scalar.activation(out=warm_out[:], in_=warm_in[:], func=ACT.Abs_reciprocal_sqrt)
         nc.sync.dma_start(p1_sb[:], p1)
         nc.sync.dma_start(p2_sb[:], p2)
         nc.vector.memset(x_plane[:].bitcast(I32), 0)

@@ -18,24 +18,22 @@ P = 128
 PACK = 4
 T = 2048
 S = 512
-CHUNK = 128
-CHUNKS = S // CHUNK
-LIST_COLS = CHUNK // 16
 HALF = S // 2
+BLOCK = 128
 FLOPS = 2 * 2 * 512 * 512 * 512
+
+SCALAR_FETCHES = ((2, 1), (3, 1))
 
 
 def words_view(words):
     return words[0].rearrange("p n t -> p (n t)").bitcast(I32)
 
 
-def load_scale_rows(queue, plane, scales, quads):
-    for quad in quads:
-        queue.dma_start(out=plane[32 * quad : 32 * quad + 4, :].bitcast(I32), in_=scales[0, 4 * quad : 4 * quad + 4, :].bitcast(I32))
-
-
-def deal(engine, dealt, raw):
-    engine.tensor_copy(out=dealt.rearrange("p (t m) -> p t m", t=PACK), in_=raw.rearrange("p (m t) -> p t m", t=PACK))
+def load_plane(queue, plane, scales):
+    rows = scales[0].bitcast(I32)
+    for quad in range(4):
+        four = rows[4 * quad : 4 * quad + 4, :]
+        queue.dma_start(out=plane[32 * quad : 32 * quad + 32, :].bitcast(I32), in_=four.unsqueeze(0).to_broadcast([8, 4, four.shape[1]]))
 
 
 def tile_picked_ljpot_none_po_kernel(
@@ -44,181 +42,200 @@ def tile_picked_ljpot_none_po_kernel(
     nc = tc.nc
     with ExitStack() as ctx:
         keep = ctx.enter_context(tc.tile_pool(name="keep", bufs=1))
-        work = ctx.enter_context(tc.tile_pool(name="work", bufs=3))
+        work = ctx.enter_context(tc.tile_pool(name="work", bufs=2))
         psum = ctx.enter_context(tc.psum_pool(name="psum", bufs=1))
 
         offs_sb = keep.tile([P, S // 16], U16, name="offs_sb")
         p1_sb = keep.tile([P, S // 16], U16, name="p1_sb")
         p2_sb = keep.tile([P, S // 16], U16, name="p2_sb")
-        x_table = keep.tile([P, T], I32, name="x_table", tag="x_table_then_w2", align_bytes=64)
-        x_plane = keep.tile([P, T], U8, name="x_plane", tag="x_plane_then_q", align_bytes=64)
+        x_table = keep.tile([P, T], I32, name="x_table", align_bytes=64)
+        x_plane = keep.tile([P, T], U8, name="x_plane", align_bytes=64)
         w1_raw = keep.tile([P, S], I32, name="w1_raw", align_bytes=64)
-        raw_plane = keep.tile([P, S], U8, name="raw_plane", align_bytes=64)
+        w2_raw = keep.tile([P, S], I32, name="w2_raw", align_bytes=64)
+        w1_raw_plane = keep.tile([P, S], U8, name="w1_raw_plane", align_bytes=64)
         w2_raw_plane = keep.tile([P, S], U8, name="w2_raw_plane", align_bytes=64)
         gn_sb = keep.tile([P, PACK], F32, name="gn_sb", align_bytes=64)
+        q_sb = keep.tile([P, PACK, S], F32, name="q_sb", align_bytes=64)
 
-        x_rows = keep.tile([P, T // 4], I32, name="x_rows", align_bytes=64)
-        for quad in range(4):
-            nc.sync.dma_start(out=x_rows[32 * quad : 32 * quad + 4, :], in_=x_scales[0, 4 * quad : 4 * quad + 4, :].bitcast(I32))
+        load_plane(nc.sync, x_plane, x_scales)
         nc.sync.dma_start(offs_sb[:], offs)
-        nc.sync.dma_start(out=w1_raw[:], in_=words_view(w1_words))
         nc.sync.dma_start(out=x_table[:], in_=words_view(x_words))
-        nc.vector.memset(raw_plane[:].bitcast(I32), 0)
-        load_scale_rows(nc.sync, raw_plane, w1_scales, range(4))
+        load_plane(nc.sync, w1_raw_plane, w1_scales)
+        nc.sync.dma_start(out=w1_raw[:], in_=words_view(w1_words))
         nc.sync.dma_start(p1_sb[:], p1)
         nc.sync.dma_start(p2_sb[:], p2)
-        nc.vector.memset(x_plane[:].bitcast(I32), 0)
-        for quad in range(4):
-            rows = slice(32 * quad, 32 * quad + 4)
-            nc.vector.tensor_copy(out=x_plane[rows, :].bitcast(I32), in_=x_rows[rows, :])
-        nc.vector.memset(w2_raw_plane[:].bitcast(I32), 0)
-        load_scale_rows(nc.sync, w2_raw_plane, w2_scales, range(4))
-        nc.gpsimd.dma_start(out=gn_sb[:], in_=gn.rearrange("(p t) o -> p (t o)", t=PACK))
-
-        w1_codes = keep.tile([P, S], I32, name="w1_codes", align_bytes=64)
-        w1_plane = keep.tile([P, S], U8, name="w1_plane", align_bytes=64)
-        deal(nc.vector, w1_codes[:].bitcast(U32), w1_raw[:].bitcast(U32))
-        deal(nc.gpsimd, w1_plane[:], raw_plane[:])
-        x_codes = []
-        x_picked_plane = []
-        for h in range(2):
-            picked = keep.tile([P, HALF], U8, name="x_picked_plane%d" % h, align_bytes=64)
-            nc.vector.tensor_copy(picked[:], x_plane[:].indirect(offs_sb[:, 16 * h : 16 * (h + 1)]))
-            x_picked_plane.append(picked)
-            codes = keep.tile([P, HALF], I32, name="x_codes%d" % h, align_bytes=64)
-            nc.vector.tensor_copy(codes[:].bitcast(U32), x_table[:].bitcast(U32).indirect(offs_sb[:, 16 * h : 16 * (h + 1)]))
-            x_codes.append(codes)
-
-        q_sb = keep.tile([P, PACK, S], F32, name="q_sb", tag="x_plane_then_q", align_bytes=64)
-        nc.sync.dma_start(out=q_sb[:], in_=q.rearrange("(p t) j -> p t j", t=PACK))
-        w2_raw = keep.tile([P, S], I32, name="w2_raw", tag="x_table_then_w2", align_bytes=64)
         nc.sync.dma_start(out=w2_raw[:], in_=words_view(w2_words))
-        w2_codes = keep.tile([P, S], I32, name="w2_codes", align_bytes=64)
-        w2_plane = keep.tile([P, S], U8, name="w2_plane", align_bytes=64)
-        deal(nc.vector, w2_codes[:].bitcast(U32), w2_raw[:].bitcast(U32))
-        deal(nc.gpsimd, w2_plane[:], w2_raw_plane[:])
+        load_plane(nc.sync, w2_raw_plane, w2_scales)
+        nc.sync.dma_start(out=gn_sb[:], in_=gn.rearrange("(p t) o -> p (t o)", t=PACK))
+        nc.sync.dma_start(out=q_sb[:], in_=q.rearrange("(p t) j -> p t j", t=PACK))
 
-        y_window = []
-        y_own = []
-        late_banks = []
+        warm = keep.tile([P, 2], F32, name="warm", align_bytes=64)
+        nc.gpsimd.memset(warm[:, 0:1], 1.0)
+        nc.scalar.activation(out=warm[:, 1:2], in_=warm[:, 0:1], func=ACT.Abs_reciprocal_sqrt)
+
+        def deal(name, raw_words, raw_plane, first, count):
+            codes = keep.tile([P, count * P], I32, name=name + "_codes", align_bytes=64)
+            plane = keep.tile([P, count * P], U8, name=name + "_plane", align_bytes=64)
+            slabs = slice(first, first + count)
+            nc.vector.tensor_copy(out=plane[:].rearrange("p (t m) -> p t m", t=count), in_=raw_plane[:].rearrange("p (m t) -> p t m", t=PACK)[:, slabs, :])
+            nc.vector.tensor_copy(
+                out=codes[:].bitcast(U32).rearrange("p (t m) -> p m t", t=count), in_=raw_words[:].bitcast(U32).rearrange("p (m t) -> p m t", t=PACK)[:, :, slabs]
+            )
+            return [(codes[:, P * t : P * (t + 1)].bitcast(FP8X4), plane[:, P * t : P * (t + 1)]) for t in range(count)]
+
+        x_codes = [keep.tile([P, HALF], I32, name="x_codes%d" % h, align_bytes=64) for h in range(2)]
+        x_picked_plane = [keep.tile([P, HALF], U8, name="x_picked_plane%d" % h, align_bytes=64) for h in range(2)]
+        for h in range(2):
+            nc.vector.tensor_copy(x_picked_plane[h][:], x_plane[:].indirect(offs_sb[:, 16 * h : 16 * (h + 1)]))
+        nc.vector.tensor_copy(x_codes[0][:].bitcast(U32), x_table[:].bitcast(U32).indirect(offs_sb[:, 0:16]))
+        w1 = deal("w1_first", w1_raw, w1_raw_plane, 0, 1)
+        nc.vector.tensor_copy(x_codes[1][:].bitcast(U32), x_table[:].bitcast(U32).indirect(offs_sb[:, 16:32]))
+        w1 = w1 + deal("w1_rest", w1_raw, w1_raw_plane, 1, 3)
+
+        y_window = [keep.tile([P, S], F32, name="y_window%d" % t, align_bytes=64) for t in range(PACK)]
+        y_own = {}
+        banks = {}
         for t in range(PACK):
-            cols = slice(P * t, P * (t + 1))
-            window = keep.tile([P, S], F32, name="y_window%d" % t, align_bytes=64)
-            own = keep.tile([P, S], F32, name="y_own%d" % t, align_bytes=64)
-            banks = []
             for h in range(2):
                 bank = psum.tile([P, S], F32, name="bank", bufs=8)
                 nc.tensor.matmul_mx(
                     out=bank[:, :HALF],
-                    lhsT=w1_codes[:, cols].bitcast(FP8X4),
-                    lhsT_scale=w1_plane[:, cols],
+                    lhsT=w1[t][0],
+                    lhsT_scale=w1[t][1],
                     rhs=x_codes[h][:].bitcast(FP8X4),
                     rhs_scale=x_picked_plane[h][:],
                     start=True,
                     stop=True,
                 )
-                banks.append(bank)
-            nc.scalar.copy(out=window[:, :HALF], in_=banks[0][:, :HALF])
-            nc.scalar.copy(out=own[:, :HALF], in_=banks[0][:, :HALF])
-            nc.scalar.copy(out=window[:, HALF:], in_=banks[1][:, :HALF])
-            y_window.append(window)
-            y_own.append(own)
-            late_banks.append(banks[1])
+                banks[t, h] = bank
+
+        def own_copy(t, h):
+            if (t, h) not in SCALAR_FETCHES:
+                y_own[t, h] = keep.tile([P, HALF], F32, name="y_own%d_%d" % (t, h), align_bytes=64)
+                nc.scalar.copy(out=y_own[t, h][:], in_=banks[t, h][:, :HALF])
+
         for t in range(PACK):
-            nc.scalar.copy(out=y_own[t][:, HALF:], in_=late_banks[t][:, :HALF])
+            nc.scalar.copy(out=y_window[t][:, :HALF], in_=banks[t, 0][:, :HALF])
+            own_copy(t, 0)
+            nc.scalar.copy(out=y_window[t][:, HALF:], in_=banks[t, 1][:, :HALF])
+        for t in range(PACK):
+            own_copy(t, 1)
 
         out_plane = keep.tile([P, S], U8, name="out_plane", align_bytes=64)
         out_codes = keep.tile([P, S], I32, name="out_codes", align_bytes=64)
         out_rows = out_0.rearrange("(p t) j -> p t j", t=PACK)
         out_words = words_view(out_1)
-        flat = "p u k j -> p (u k j)"
-        pairs = range(2)
+        lists = (p1_sb, p2_sb)
 
-        def differences(h):
-            js = slice(HALF * h, HALF * (h + 1))
-            d = [work.tile([P, 2, 2, HALF], F32, name="d", bufs=4, align_bytes=64) for a in pairs]
+        d = {}
+        soft = {}
+        fetched = {}
+        force = [keep.tile([P, PACK, 2, HALF], F32, name="force%d" % h, align_bytes=64) for h in range(2)]
+        for h in range(2):
             for t in range(PACK):
-                for k, partners in enumerate((p1_sb, p2_sb)):
-                    nc.vector.tensor_tensor(
-                        d[t // 2][:, t % 2, k, :], y_window[t][:].indirect(partners[:, 16 * h : 16 * (h + 1)]), y_own[t][:, js], SUBTRACT
-                    )
-            return d
+                d[t, h] = keep.tile([P, 2, HALF], F32, name="d%d_%d" % (t, h), align_bytes=64)
+                soft[t, h] = keep.tile([P, 2, HALF], F32, name="soft%d_%d" % (t, h), align_bytes=64)
+                if (t, h) not in SCALAR_FETCHES:
+                    for k in range(2):
+                        nc.vector.tensor_tensor(d[t, h][:, k, :], y_window[t][:].indirect(lists[k][:, 16 * h : 16 * (h + 1)]), y_own[t, h][:], SUBTRACT)
+        w2 = deal("w2", w2_raw, w2_raw_plane, 0, 4)
 
-        def pair_tiles(name, width, bufs):
-            return [work.tile([P, 2, 2, width], F32, name=name, bufs=bufs, align_bytes=64) for a in pairs]
+        def fetch(t, h):
+            fetched[t, h] = keep.tile([P, 2, HALF], F32, name="fetched%d_%d" % (t, h), align_bytes=64)
+            for k in range(2):
+                nc.scalar.activation(out=fetched[t, h][:, k, :], in_=y_window[t][:].indirect(lists[k][:, 16 * h : 16 * (h + 1)]), func=ACT.Copy)
 
-        def softened(d, width):
-            d2, denom2, soft = pair_tiles("d2", width, 2), pair_tiles("denom2", width, 2), pair_tiles("soft", width, 8)
-            for a in pairs:
-                nc.scalar.activation(out=d2[a][:], in_=d[a], func=ACT.Square)
-            for a in pairs:
-                nc.scalar.activation(out=denom2[a][:], in_=d2[a][:], func=ACT.Square, bias=1.0)
-            for a in pairs:
-                nc.scalar.activation(out=soft[a][:], in_=denom2[a][:], func=ACT.Abs_reciprocal_sqrt)
-            return soft
+        def subtract(t, h):
+            own = y_window[t][:, HALF * h : HALF * (h + 1)].unsqueeze(1).to_broadcast([P, 2, HALF])
+            nc.vector.tensor_tensor(d[t, h][:], fetched[t, h][:], own, SUBTRACT)
 
-        def forces(js, width, d, soft):
-            s, poly = pair_tiles("s", width, 2), pair_tiles("poly", width, 2)
-            force = work.tile([P, PACK, 2, width], F32, name="force", bufs=2, align_bytes=64)
-            for a in pairs:
-                nc.vector.tensor_tensor(s[a][:], soft[a], q_sb[:, 2 * a : 2 * a + 2, js].unsqueeze(2).to_broadcast([P, 2, 2, width]), MULT)
-            for a in pairs:
-                nc.vector.scalar_tensor_tensor(poly[a][:].rearrange(flat), s[a][:].rearrange(flat), 1.0, s[a][:].rearrange(flat), SUBTRACT, MULT)
-            for t in range(PACK):
-                nc.vector.scalar_tensor_tensor(force[:, t], poly[t // 2][:, t % 2], gn_sb[:, t : t + 1], d[t // 2][:, t % 2], MULT, MULT)
-            return force
+        def soften(slabs, h, cols):
+            width = cols.stop - cols.start
+            d2 = [work.tile([P, 2, width], F32, name="d2", bufs=2, align_bytes=64) for t in slabs]
+            denom2 = [work.tile([P, 2, width], F32, name="denom2", bufs=2, align_bytes=64) for t in slabs]
+            for i, t in enumerate(slabs):
+                nc.scalar.activation(out=d2[i][:], in_=d[t, h][:, :, cols], func=ACT.Square)
+            for i, t in enumerate(slabs):
+                nc.scalar.activation(out=denom2[i][:], in_=d2[i][:], func=ACT.Square, bias=1.0)
+            for i, t in enumerate(slabs):
+                nc.scalar.activation(out=soft[t, h][:, :, cols], in_=denom2[i][:], func=ACT.Abs_reciprocal_sqrt)
 
-        def summed(force, width, last):
-            z_planes = work.tile([P, PACK, width], BF16, name="z_planes", bufs=2, align_bytes=64)
-            nc.vector.tensor_tensor(z_planes[:], force[:, :, 0, :], force[:, :, 1, :], ADD)
+        def forces(slabs, h, cols):
+            width = cols.stop - cols.start
+            js = slice(HALF * h + cols.start, HALF * h + cols.stop)
+            s = [work.tile([P, 2, width], F32, name="s", bufs=4, align_bytes=64) for t in slabs]
+            poly = [work.tile([P, 2, width], F32, name="poly", bufs=4, align_bytes=64) for t in slabs]
+            for i, t in enumerate(slabs):
+                nc.vector.tensor_tensor(s[i][:], soft[t, h][:, :, cols], q_sb[:, t, js].unsqueeze(1).to_broadcast([P, 2, width]), MULT)
+            for i, t in enumerate(slabs):
+                nc.vector.scalar_tensor_tensor(poly[i][:], s[i][:], 1.0, s[i][:], SUBTRACT, MULT)
+            for i, t in enumerate(slabs):
+                nc.vector.scalar_tensor_tensor(force[h][:, t, :, cols], poly[i][:], gn_sb[:, t : t + 1], d[t, h][:, :, cols], MULT, MULT)
+
+        def quantized(h, cols):
+            width = cols.stop - cols.start
             z16 = work.tile([P, width, PACK], BF16, name="z16", bufs=2, align_bytes=64)
-            weave = nc.vector.tensor_copy if last else nc.scalar.copy
-            weave(out=z16[:].rearrange("p (c i) t -> p c t i", i=4), in_=z_planes[:].rearrange("p t (c i) -> p c t i", i=4))
-            return z16
-
-        def layer(js, width, z16):
+            nc.vector.tensor_tensor(
+                z16[:].rearrange("p (c i) t -> p c t i", i=2),
+                force[h][:, :, 0, cols].rearrange("p t (c i) -> p c t i", i=2),
+                force[h][:, :, 1, cols].rearrange("p t (c i) -> p c t i", i=2),
+                ADD,
+            )
             z_codes = work.tile([P, width], I32, name="z_codes", bufs=2, align_bytes=64)
             z_plane = work.tile([P, width], U8, name="z_plane", bufs=2, align_bytes=64)
             nc.vector.quantize_mx(out=z_codes[:].bitcast(FP8X4), scales=z_plane[:], in_=z16[:].rearrange("p j t -> p (j t)"))
-            out_bank = psum.tile([P, S], F32, name="bank", bufs=8)
-            sums = out_bank[:, : PACK * width].rearrange("p (t j) -> p t j", t=PACK)
-            for t in range(PACK):
-                cols = slice(P * t, P * (t + 1))
-                nc.tensor.matmul_mx(
-                    out=sums[:, t, :],
-                    lhsT=w2_codes[:, cols].bitcast(FP8X4),
-                    lhsT_scale=w2_plane[:, cols],
-                    rhs=z_codes[:].bitcast(FP8X4),
-                    rhs_scale=z_plane[:],
-                    start=True,
-                    stop=True,
-                )
-            result16 = work.tile([P, width, PACK], BF16, name="result16", bufs=2, align_bytes=64)
-            nc.scalar.copy(out=result16[:], in_=sums.rearrange("p t j -> p j t"))
-            result = work.tile([P, PACK, width], F32, name="result", bufs=4, align_bytes=64)
-            nc.scalar.copy(out=result[:], in_=sums)
-            (nc.scalar if js.stop == S else nc.sync).dma_start(out=out_rows[:, :, js], in_=result[:])
+            return z_codes, z_plane
+
+        def layer(h, cols, z_codes, z_plane):
+            width = cols.stop - cols.start
+            start = HALF * h + cols.start
+            result16 = work.tile([P, width, PACK], BF16, name="result16", bufs=3, align_bytes=64)
+            n = min(width, BLOCK)
+            for b in range(0, width, n):
+                out_bank = psum.tile([P, S], F32, name="bank", bufs=8)
+                sums = out_bank[:, : PACK * n].rearrange("p (t j) -> p t j", t=PACK)
+                for t in range(PACK):
+                    nc.tensor.matmul_mx(
+                        out=sums[:, t, :],
+                        lhsT=w2[t][0],
+                        lhsT_scale=w2[t][1],
+                        rhs=z_codes[:, b : b + n].bitcast(FP8X4),
+                        rhs_scale=z_plane[:, b : b + n],
+                        start=True,
+                        stop=True,
+                    )
+                nc.scalar.copy(out=result16[:, b : b + n, :], in_=sums.rearrange("p t j -> p j t"))
+                result = work.tile([P, PACK, n], F32, name="result", bufs=4, align_bytes=64)
+                nc.scalar.copy(out=result[:], in_=sums)
+                js = slice(start + b, start + b + n)
+                (nc.scalar if js.stop == S else nc.sync).dma_start(out=out_rows[:, :, js], in_=result[:])
+            return start, width, result16
+
+        def planes(start, width, result16):
+            js = slice(start, start + width)
             nc.vector.quantize_mx(out=out_codes[:, js].bitcast(FP8X4), scales=out_plane[:, js], in_=result16[:].rearrange("p j t -> p (j t)"))
-            if js.stop % CHUNK == 0:
-                done = slice(js.stop - CHUNK, js.stop)
-                nc.sync.dma_start(out=out_words[:, done], in_=out_codes[:, done])
+            nc.sync.dma_start(out=out_words[:, js], in_=out_codes[:, js])
 
-        halves = [differences(h) for h in range(2)]
-
-        def columns(tiles, start, width):
-            return [tiles[a][:, :, :, start : start + width] for a in pairs]
-
-        def soften_chunk(c):
-            return softened(columns(halves[c // 2], CHUNK * (c % 2), CHUNK), CHUNK)
-
-        softs = [soften_chunk(c) for c in range(3)]
-        for c in range(CHUNKS):
-            width = CHUNK if c + 1 < CHUNKS else CHUNK // 2
-            for start in range(0, CHUNK, width):
-                js = slice(CHUNK * c + start, CHUNK * c + start + width)
-                force = forces(js, width, columns(halves[c // 2], CHUNK * (c % 2) + start, width), columns(softs[c], start, width))
-                if c + 3 < CHUNKS:
-                    softs.append(soften_chunk(c + 3))
-                layer(js, width, summed(force, width, js.stop == S))
+        whole = slice(0, HALF)
+        soften((0, 1), 0, whole)
+        soften((2, 3), 0, whole)
+        for t, h in SCALAR_FETCHES:
+            fetch(t, h)
+        forces((0, 1), 0, whole)
+        forces((2, 3), 0, whole)
+        for t, h in SCALAR_FETCHES:
+            subtract(t, h)
+        soften((0, 1), 1, whole)
+        soften((2, 3), 1, slice(0, 128))
+        soften((2, 3), 1, slice(128, 256))
+        z = quantized(0, whole)
+        forces((0, 1), 1, whole)
+        waiting = layer(0, whole, *z)
+        for cols in (slice(0, 128), slice(128, 192), slice(192, 256)):
+            forces((2, 3), 1, cols)
+            z = quantized(1, cols)
+            planes(*waiting)
+            waiting = layer(1, cols, *z)
+        planes(*waiting)
         for quad in range(4):
             (nc.sync if quad < 2 else nc.scalar).dma_start(out=out_2[0, 4 * quad : 4 * quad + 4, :].bitcast(I32), in_=out_plane[32 * quad : 32 * quad + 4, :].bitcast(I32))

@@ -22,8 +22,6 @@ HALF = S // 2
 BLOCK = 128
 FLOPS = 2 * 2 * 512 * 512 * 512
 
-SCALAR_FETCHES = ((2, 1), (3, 1))
-
 
 def words_view(words):
     return words[0].rearrange("p n t -> p (n t)").bitcast(I32)
@@ -45,54 +43,56 @@ def tile_picked_ljpot_none_po_kernel(
         work = ctx.enter_context(tc.tile_pool(name="work", bufs=2))
         psum = ctx.enter_context(tc.psum_pool(name="psum", bufs=1))
 
+        def tile(name, shape, dtype, tag=None):
+            return keep.tile([P] + shape, dtype, name=name, tag=tag or name, align_bytes=64)
+
         offs_sb = keep.tile([P, S // 16], U16, name="offs_sb")
         p1_sb = keep.tile([P, S // 16], U16, name="p1_sb")
         p2_sb = keep.tile([P, S // 16], U16, name="p2_sb")
-        x_table = keep.tile([P, T], I32, name="x_table", align_bytes=64)
-        x_plane = keep.tile([P, T], U8, name="x_plane", align_bytes=64)
-        w1_raw = keep.tile([P, S], I32, name="w1_raw", align_bytes=64)
-        w2_raw = keep.tile([P, S], I32, name="w2_raw", align_bytes=64)
-        w1_raw_plane = keep.tile([P, S], U8, name="w1_raw_plane", align_bytes=64)
-        w2_raw_plane = keep.tile([P, S], U8, name="w2_raw_plane", align_bytes=64)
-        gn_sb = keep.tile([P, PACK], F32, name="gn_sb", align_bytes=64)
-        q_sb = keep.tile([P, PACK, S], F32, name="q_sb", align_bytes=64)
+        x_table = tile("x_table", [T], I32)
+        x_plane = tile("x_plane", [T], U8)
+        w1_raw = tile("w1_raw", [S], I32)
+        w2_raw = tile("w2_raw", [S], I32)
+        w1_raw_plane = tile("w1_raw_plane", [S], U8)
+        w2_raw_plane = tile("w2_raw_plane", [S], U8)
+        gn_sb = tile("gn_sb", [PACK], F32)
+        q_rows = q.rearrange("(p t) j -> p t j", t=PACK)
+        q_sb = [tile("q0", [PACK, HALF], F32)]
 
         load_plane(nc.sync, x_plane, x_scales)
         nc.sync.dma_start(offs_sb[:], offs)
         nc.sync.dma_start(out=x_table[:], in_=words_view(x_words))
         load_plane(nc.sync, w1_raw_plane, w1_scales)
         nc.sync.dma_start(out=w1_raw[:], in_=words_view(w1_words))
+        nc.sync.dma_start(out=w2_raw[:], in_=words_view(w2_words))
         nc.sync.dma_start(p1_sb[:], p1)
         nc.sync.dma_start(p2_sb[:], p2)
-        nc.sync.dma_start(out=w2_raw[:], in_=words_view(w2_words))
         load_plane(nc.sync, w2_raw_plane, w2_scales)
         nc.sync.dma_start(out=gn_sb[:], in_=gn.rearrange("(p t) o -> p (t o)", t=PACK))
-        nc.sync.dma_start(out=q_sb[:], in_=q.rearrange("(p t) j -> p t j", t=PACK))
+        nc.sync.dma_start(out=q_sb[0][:], in_=q_rows[:, :, :HALF])
 
-        warm = keep.tile([P, 2], F32, name="warm", align_bytes=64)
+        warm = tile("warm", [2], F32)
         nc.gpsimd.memset(warm[:, 0:1], 1.0)
         nc.scalar.activation(out=warm[:, 1:2], in_=warm[:, 0:1], func=ACT.Abs_reciprocal_sqrt)
 
-        def deal(name, raw_words, raw_plane, first, count):
-            codes = keep.tile([P, count * P], I32, name=name + "_codes", align_bytes=64)
-            plane = keep.tile([P, count * P], U8, name=name + "_plane", align_bytes=64)
-            slabs = slice(first, first + count)
-            nc.vector.tensor_copy(out=plane[:].rearrange("p (t m) -> p t m", t=count), in_=raw_plane[:].rearrange("p (m t) -> p t m", t=PACK)[:, slabs, :])
-            nc.vector.tensor_copy(
-                out=codes[:].bitcast(U32).rearrange("p (t m) -> p m t", t=count), in_=raw_words[:].bitcast(U32).rearrange("p (m t) -> p m t", t=PACK)[:, :, slabs]
-            )
-            return [(codes[:, P * t : P * (t + 1)].bitcast(FP8X4), plane[:, P * t : P * (t + 1)]) for t in range(count)]
+        def deal(engine, name, raw, dtype, first, count, order):
+            dealt = tile(name, [count * P], I32 if dtype == U32 else U8)
+            source = raw[:].bitcast(dtype).rearrange("p (m t) -> p m t", t=PACK)[:, :, first : first + count]
+            engine.tensor_copy(out=dealt[:].bitcast(dtype).rearrange("p (t m) -> " + order, t=count), in_=source.rearrange("p m t -> " + order))
+            return [dealt[:, P * t : P * (t + 1)] for t in range(count)]
 
-        x_codes = [keep.tile([P, HALF], I32, name="x_codes%d" % h, align_bytes=64) for h in range(2)]
-        x_picked_plane = [keep.tile([P, HALF], U8, name="x_picked_plane%d" % h, align_bytes=64) for h in range(2)]
+        x_codes = [tile("x_codes%d" % h, [HALF], I32) for h in range(2)]
+        x_picked_plane = tile("x_picked_plane", [S], U8, tag="w2_plane")
+        nc.vector.tensor_copy(x_picked_plane[:], x_plane[:].indirect(offs_sb[:]))
         for h in range(2):
-            nc.vector.tensor_copy(x_picked_plane[h][:], x_plane[:].indirect(offs_sb[:, 16 * h : 16 * (h + 1)]))
-        nc.vector.tensor_copy(x_codes[0][:].bitcast(U32), x_table[:].bitcast(U32).indirect(offs_sb[:, 0:16]))
-        w1 = deal("w1_first", w1_raw, w1_raw_plane, 0, 1)
-        nc.vector.tensor_copy(x_codes[1][:].bitcast(U32), x_table[:].bitcast(U32).indirect(offs_sb[:, 16:32]))
-        w1 = w1 + deal("w1_rest", w1_raw, w1_raw_plane, 1, 3)
+            nc.vector.tensor_copy(x_codes[h][:].bitcast(U32), x_table[:].bitcast(U32).indirect(offs_sb[:, 16 * h : 16 * (h + 1)]))
+        w1_plane = deal(nc.gpsimd, "w1_first_plane", w1_raw_plane, U8, 0, 1, "p t m")
+        w1_codes = deal(nc.gpsimd, "w1_first_codes", w1_raw, U32, 0, 1, "p t m")
+        w1_plane = w1_plane + deal(nc.vector, "w1_rest_plane", w1_raw_plane, U8, 1, 3, "p t m")
+        w1_codes = w1_codes + deal(nc.vector, "w1_rest_codes", w1_raw, U32, 1, 3, "p m t")
+        w2_codes = deal(nc.gpsimd, "w2_codes", w2_raw, U32, 0, 4, "p t m")
 
-        y_window = [keep.tile([P, S], F32, name="y_window%d" % t, align_bytes=64) for t in range(PACK)]
+        y_window = [tile("y_window%d" % t, [S], F32) for t in range(PACK)]
         y_own = {}
         banks = {}
         for t in range(PACK):
@@ -100,29 +100,31 @@ def tile_picked_ljpot_none_po_kernel(
                 bank = psum.tile([P, S], F32, name="bank", bufs=8)
                 nc.tensor.matmul_mx(
                     out=bank[:, :HALF],
-                    lhsT=w1[t][0],
-                    lhsT_scale=w1[t][1],
+                    lhsT=w1_codes[t].bitcast(FP8X4),
+                    lhsT_scale=w1_plane[t],
                     rhs=x_codes[h][:].bitcast(FP8X4),
-                    rhs_scale=x_picked_plane[h][:],
+                    rhs_scale=x_picked_plane[:, HALF * h : HALF * (h + 1)],
                     start=True,
                     stop=True,
                 )
                 banks[t, h] = bank
 
-        def own_copy(t, h):
-            if (t, h) not in SCALAR_FETCHES:
-                y_own[t, h] = keep.tile([P, HALF], F32, name="y_own%d_%d" % (t, h), align_bytes=64)
-                nc.scalar.copy(out=y_own[t, h][:], in_=banks[t, h][:, :HALF])
-
         for t in range(PACK):
-            nc.scalar.copy(out=y_window[t][:, :HALF], in_=banks[t, 0][:, :HALF])
-            own_copy(t, 0)
-            nc.scalar.copy(out=y_window[t][:, HALF:], in_=banks[t, 1][:, :HALF])
-        for t in range(PACK):
-            own_copy(t, 1)
+            for h in range(2):
+                cols = slice(HALF * h, HALF * (h + 1))
+                (nc.vector.tensor_copy if (t, h) == (0, 1) else nc.scalar.copy)(out=y_window[t][:, cols], in_=banks[t, h][:, :HALF])
+                if (t, h) in ((0, 0), (1, 0), (2, 0), (3, 0)):
+                    y_own[t, h] = tile("y_own%d_%d" % (t, h), [HALF], F32)
+                    nc.scalar.copy(out=y_own[t, h][:], in_=banks[t, h][:, :HALF])
+                if (t, h) in ():
+                    y_own[t, h] = tile("y_own%d_%d" % (t, h), [HALF], F32)
+                    nc.sync.dma_start(out=y_own[t, h][:], in_=y_window[t][:, cols])
+        for t in range(2):
+            y_own[t, 1] = tile("y_own%d_1" % t, [HALF], F32)
+            nc.scalar.copy(out=y_own[t, 1][:], in_=banks[t, 1][:, :HALF])
 
-        out_plane = keep.tile([P, S], U8, name="out_plane", align_bytes=64)
-        out_codes = keep.tile([P, S], I32, name="out_codes", align_bytes=64)
+        out_plane = tile("out_plane", [S], U8)
+        out_codes = tile("out_codes", [S], I32)
         out_rows = out_0.rearrange("(p t) j -> p t j", t=PACK)
         out_words = words_view(out_1)
         lists = (p1_sb, p2_sb)
@@ -130,47 +132,48 @@ def tile_picked_ljpot_none_po_kernel(
         d = {}
         soft = {}
         fetched = {}
-        force = [keep.tile([P, PACK, 2, HALF], F32, name="force%d" % h, align_bytes=64) for h in range(2)]
-        for h in range(2):
-            for t in range(PACK):
-                d[t, h] = keep.tile([P, 2, HALF], F32, name="d%d_%d" % (t, h), align_bytes=64)
-                soft[t, h] = keep.tile([P, 2, HALF], F32, name="soft%d_%d" % (t, h), align_bytes=64)
-                if (t, h) not in SCALAR_FETCHES:
-                    for k in range(2):
-                        nc.vector.tensor_tensor(d[t, h][:, k, :], y_window[t][:].indirect(lists[k][:, 16 * h : 16 * (h + 1)]), y_own[t, h][:], SUBTRACT)
-        w2 = deal("w2", w2_raw, w2_raw_plane, 0, 4)
+        force = [tile("force%d" % h, [PACK, 2, HALF], F32) for h in range(2)]
 
-        def fetch(t, h):
-            fetched[t, h] = keep.tile([P, 2, HALF], F32, name="fetched%d_%d" % (t, h), align_bytes=64)
+        def gather(t, h):
+            d[t, h] = tile("d%d_%d" % (t, h), [2, HALF], F32)
+            for k in range(2):
+                nc.vector.tensor_tensor(d[t, h][:, k, :], y_window[t][:].indirect(lists[k][:, 16 * h : 16 * (h + 1)]), y_own[t, h][:], SUBTRACT)
+
+        def fetch(t, h, tag):
+            fetched[t, h] = tile("fetched%d_%d" % (t, h), [2, HALF], F32, tag)
             for k in range(2):
                 nc.scalar.activation(out=fetched[t, h][:, k, :], in_=y_window[t][:].indirect(lists[k][:, 16 * h : 16 * (h + 1)]), func=ACT.Copy)
 
-        def subtract(t, h):
+        def subtract(t, h, tag):
+            d[t, h] = tile("d%d_%d" % (t, h), [2, HALF], F32, tag)
             own = y_window[t][:, HALF * h : HALF * (h + 1)].unsqueeze(1).to_broadcast([P, 2, HALF])
             nc.vector.tensor_tensor(d[t, h][:], fetched[t, h][:], own, SUBTRACT)
 
-        def soften(slabs, h, cols):
-            width = cols.stop - cols.start
-            d2 = [work.tile([P, 2, width], F32, name="d2", bufs=2, align_bytes=64) for t in slabs]
-            denom2 = [work.tile([P, 2, width], F32, name="denom2", bufs=2, align_bytes=64) for t in slabs]
-            for i, t in enumerate(slabs):
-                nc.scalar.activation(out=d2[i][:], in_=d[t, h][:, :, cols], func=ACT.Square)
-            for i, t in enumerate(slabs):
-                nc.scalar.activation(out=denom2[i][:], in_=d2[i][:], func=ACT.Square, bias=1.0)
-            for i, t in enumerate(slabs):
-                nc.scalar.activation(out=soft[t, h][:, :, cols], in_=denom2[i][:], func=ACT.Abs_reciprocal_sqrt)
+        def label(name, t, h, cols):
+            return "%s%d_%d_%d" % (name, t, h, cols.start)
 
-        def forces(slabs, h, cols):
-            width = cols.stop - cols.start
-            js = slice(HALF * h + cols.start, HALF * h + cols.stop)
-            s = [work.tile([P, 2, width], F32, name="s", bufs=4, align_bytes=64) for t in slabs]
-            poly = [work.tile([P, 2, width], F32, name="poly", bufs=4, align_bytes=64) for t in slabs]
-            for i, t in enumerate(slabs):
-                nc.vector.tensor_tensor(s[i][:], soft[t, h][:, :, cols], q_sb[:, t, js].unsqueeze(1).to_broadcast([P, 2, width]), MULT)
-            for i, t in enumerate(slabs):
+        def soften(items):
+            d2 = [work.tile([P, 2, c.stop - c.start], F32, name="d2", bufs=2, align_bytes=64) for t, h, c in items]
+            denom2 = [tile(label("denom2_", t, h, c), [2, c.stop - c.start], F32) for t, h, c in items]
+            for t, h, c in items:
+                if (t, h) not in soft:
+                    soft[t, h] = tile("soft%d_%d" % (t, h), [2, HALF], F32)
+            for i, (t, h, c) in enumerate(items):
+                nc.scalar.activation(out=d2[i][:], in_=d[t, h][:, :, c], func=ACT.Square)
+            for i, (t, h, c) in enumerate(items):
+                nc.scalar.activation(out=denom2[i][:], in_=d2[i][:], func=ACT.Square, bias=1.0)
+            for i, (t, h, c) in enumerate(items):
+                nc.scalar.activation(out=soft[t, h][:, :, c], in_=denom2[i][:], func=ACT.Abs_reciprocal_sqrt)
+
+        def forces(items):
+            s = [work.tile([P, 2, c.stop - c.start], F32, name="s", bufs=4, align_bytes=64) for t, h, c in items]
+            poly = [tile(label("poly", t, h, c), [2, c.stop - c.start], F32) for t, h, c in items]
+            for i, (t, h, c) in enumerate(items):
+                nc.vector.tensor_tensor(s[i][:], soft[t, h][:, :, c], q_sb[h][:, t, c].unsqueeze(1).to_broadcast([P, 2, c.stop - c.start]), MULT)
+            for i, (t, h, c) in enumerate(items):
                 nc.vector.scalar_tensor_tensor(poly[i][:], s[i][:], 1.0, s[i][:], SUBTRACT, MULT)
-            for i, t in enumerate(slabs):
-                nc.vector.scalar_tensor_tensor(force[h][:, t, :, cols], poly[i][:], gn_sb[:, t : t + 1], d[t, h][:, :, cols], MULT, MULT)
+            for i, (t, h, c) in enumerate(items):
+                nc.vector.scalar_tensor_tensor(force[h][:, t, :, c], poly[i][:], gn_sb[:, t : t + 1], d[t, h][:, :, c], MULT, MULT)
 
         def quantized(h, cols):
             width = cols.stop - cols.start
@@ -186,10 +189,11 @@ def tile_picked_ljpot_none_po_kernel(
             nc.vector.quantize_mx(out=z_codes[:].bitcast(FP8X4), scales=z_plane[:], in_=z16[:].rearrange("p j t -> p (j t)"))
             return z_codes, z_plane
 
-        def layer(h, cols, z_codes, z_plane):
+        def layer(h, cols, z, tags=(None, None, None)):
+            z_codes, z_plane = z
             width = cols.stop - cols.start
             start = HALF * h + cols.start
-            result16 = work.tile([P, width, PACK], BF16, name="result16", bufs=3, align_bytes=64)
+            result16 = tile("result16_%d" % start, [width, PACK], BF16, tags[0])
             n = min(width, BLOCK)
             for b in range(0, width, n):
                 out_bank = psum.tile([P, S], F32, name="bank", bufs=8)
@@ -197,17 +201,17 @@ def tile_picked_ljpot_none_po_kernel(
                 for t in range(PACK):
                     nc.tensor.matmul_mx(
                         out=sums[:, t, :],
-                        lhsT=w2[t][0],
-                        lhsT_scale=w2[t][1],
+                        lhsT=w2_codes[t].bitcast(FP8X4),
+                        lhsT_scale=w2_plane[t],
                         rhs=z_codes[:, b : b + n].bitcast(FP8X4),
                         rhs_scale=z_plane[:, b : b + n],
                         start=True,
                         stop=True,
                     )
-                nc.scalar.copy(out=result16[:, b : b + n, :], in_=sums.rearrange("p t j -> p j t"))
-                result = work.tile([P, PACK, n], F32, name="result", bufs=4, align_bytes=64)
-                nc.scalar.copy(out=result[:], in_=sums)
                 js = slice(start + b, start + b + n)
+                (nc.vector.tensor_copy if js.stop == S and True else nc.scalar.copy)(out=result16[:, b : b + n, :], in_=sums.rearrange("p t j -> p j t"))
+                result = tile("result%d" % js.start, [PACK, n], F32, tags[1 + b // n])
+                nc.scalar.copy(out=result[:], in_=sums)
                 (nc.scalar if js.stop == S else nc.sync).dma_start(out=out_rows[:, :, js], in_=result[:])
             return start, width, result16
 
@@ -216,26 +220,31 @@ def tile_picked_ljpot_none_po_kernel(
             nc.vector.quantize_mx(out=out_codes[:, js].bitcast(FP8X4), scales=out_plane[:, js], in_=result16[:].rearrange("p j t -> p (j t)"))
             nc.sync.dma_start(out=out_words[:, js], in_=out_codes[:, js])
 
-        whole = slice(0, HALF)
-        soften((0, 1), 0, whole)
-        soften((2, 3), 0, whole)
-        for t, h in SCALAR_FETCHES:
-            fetch(t, h)
-        forces((0, 1), 0, whole)
-        forces((2, 3), 0, whole)
-        for t, h in SCALAR_FETCHES:
-            subtract(t, h)
-        soften((0, 1), 1, whole)
-        soften((2, 3), 1, slice(0, 128))
-        soften((2, 3), 1, slice(128, 256))
+        whole, low, high = slice(0, HALF), slice(0, 128), slice(128, 256)
+        for t, h in ((0, 0), (1, 0), (2, 0), (3, 0), (0, 1), (1, 1)):
+            gather(t, h)
+        q_sb.append(tile("q1", [PACK, HALF], F32))
+        nc.sync.dma_start(out=q_sb[1][:], in_=q_rows[:, :, HALF:])
+        w2_plane = deal(nc.vector, "w2_plane", w2_raw_plane, U8, 0, 4, "p t m")
+        soften([(0, 0, whole), (1, 0, whole)])
+        soften([(2, 0, whole), (3, 0, whole)])
+        fetch(2, 1, "denom2_2_0_0")
+        fetch(3, 1, "denom2_3_0_0")
+        forces([(0, 0, whole), (1, 0, whole)])
+        forces([(2, 0, whole), (3, 0, whole)])
+        subtract(2, 1, None)
+        subtract(3, 1, None)
+        soften([(0, 1, whole), (1, 1, whole)])
+        soften([(2, 1, low), (3, 1, low)])
+        soften([(2, 1, high), (3, 1, high)])
         z = quantized(0, whole)
-        forces((0, 1), 1, whole)
-        waiting = layer(0, whole, *z)
-        for cols in (slice(0, 128), slice(128, 192), slice(192, 256)):
-            forces((2, 3), 1, cols)
+        forces([(0, 1, whole), (1, 1, whole)])
+        waiting = layer(0, whole, z)
+        for cols in (low, slice(128, 192), slice(192, 256)):
+            forces([(2, 1, cols), (3, 1, cols)])
             z = quantized(1, cols)
             planes(*waiting)
-            waiting = layer(1, cols, *z)
+            waiting = layer(1, cols, z)
         planes(*waiting)
         for quad in range(4):
             (nc.sync if quad < 2 else nc.scalar).dma_start(out=out_2[0, 4 * quad : 4 * quad + 4, :].bitcast(I32), in_=out_plane[32 * quad : 32 * quad + 4, :].bitcast(I32))

@@ -81,16 +81,15 @@ def tile_picked_ljpot_none_po_kernel(
             engine.tensor_copy(out=dealt[:].bitcast(dtype).rearrange("p (t m) -> " + order, t=count), in_=source.rearrange("p m t -> " + order))
             return [dealt[:, P * t : P * (t + 1)] for t in range(count)]
 
-        x_codes = [tile("x_codes%d" % h, [HALF], I32) for h in range(2)]
         x_picked_plane = tile("x_picked_plane", [S], U8, tag="w2_plane")
         nc.vector.tensor_copy(x_picked_plane[:], x_plane[:].indirect(offs_sb[:]))
-        for h in range(2):
-            nc.vector.tensor_copy(x_codes[h][:].bitcast(U32), x_table[:].bitcast(U32).indirect(offs_sb[:, 16 * h : 16 * (h + 1)]))
-        w1_plane = deal(nc.gpsimd, "w1_first_plane", w1_raw_plane, U8, 0, 1, "p t m")
-        w1_codes = deal(nc.gpsimd, "w1_first_codes", w1_raw, U32, 0, 1, "p t m")
-        w1_plane = w1_plane + deal(nc.vector, "w1_rest_plane", w1_raw_plane, U8, 1, 3, "p t m")
-        w1_codes = w1_codes + deal(nc.vector, "w1_rest_codes", w1_raw, U32, 1, 3, "p m t")
-        w2_codes = deal(nc.gpsimd, "w2_codes", w2_raw, U32, 0, 4, "p t m")
+        x_codes = [tile("x_codes0", [HALF], I32)]
+        nc.vector.tensor_copy(x_codes[0][:].bitcast(U32), x_table[:].bitcast(U32).indirect(offs_sb[:, 0:16]))
+        w1_plane = deal(nc.vector, "w1_plane", w1_raw_plane, U8, 0, 4, "p t m")
+        w1_codes = deal(nc.vector, "w1_codes", w1_raw, U32, 0, 4, "p m t")
+        x_codes.append(tile("x_codes1", [HALF], I32, "w1_raw"))
+        nc.vector.tensor_copy(x_codes[1][:].bitcast(U32), x_table[:].bitcast(U32).indirect(offs_sb[:, 16:32]))
+        w2_codes = deal(nc.vector, "w2_codes", w2_raw, U32, 0, 4, "p m t")
 
         y_window = [tile("y_window%d" % t, [S], F32) for t in range(PACK)]
         y_own = {}
@@ -119,12 +118,10 @@ def tile_picked_ljpot_none_po_kernel(
                 if (t, h) in ():
                     y_own[t, h] = tile("y_own%d_%d" % (t, h), [HALF], F32)
                     nc.sync.dma_start(out=y_own[t, h][:], in_=y_window[t][:, cols])
-        for t in range(2):
-            y_own[t, 1] = tile("y_own%d_1" % t, [HALF], F32)
-            nc.scalar.copy(out=y_own[t, 1][:], in_=banks[t, 1][:, :HALF])
+        y_own[0, 1] = tile("y_own0_1", [HALF], F32)
+        nc.scalar.copy(out=y_own[0, 1][:], in_=banks[0, 1][:, :HALF])
 
         out_plane = tile("out_plane", [S], U8)
-        out_codes = tile("out_codes", [S], I32)
         out_rows = out_0.rearrange("(p t) j -> p t j", t=PACK)
         out_words = words_view(out_1)
         lists = (p1_sb, p2_sb)
@@ -152,8 +149,11 @@ def tile_picked_ljpot_none_po_kernel(
         def label(name, t, h, cols):
             return "%s%d_%d_%d" % (name, t, h, cols.start)
 
-        def soften(items):
-            d2 = [work.tile([P, 2, c.stop - c.start], F32, name="d2", bufs=2, align_bytes=64) for t, h, c in items]
+        def soften(items, tags=None):
+            if tags:
+                d2 = [tile(label("d2_", t, h, c), [2, c.stop - c.start], F32, tag) for (t, h, c), tag in zip(items, tags)]
+            else:
+                d2 = [work.tile([P, 2, c.stop - c.start], F32, name="d2", bufs=2, align_bytes=64) for t, h, c in items]
             denom2 = [tile(label("denom2_", t, h, c), [2, c.stop - c.start], F32) for t, h, c in items]
             for t, h, c in items:
                 if (t, h) not in soft:
@@ -165,13 +165,17 @@ def tile_picked_ljpot_none_po_kernel(
             for i, (t, h, c) in enumerate(items):
                 nc.scalar.activation(out=soft[t, h][:, :, c], in_=denom2[i][:], func=ACT.Abs_reciprocal_sqrt)
 
-        def forces(items):
+        def forces(items, between=None, later=None):
             s = [work.tile([P, 2, c.stop - c.start], F32, name="s", bufs=4, align_bytes=64) for t, h, c in items]
             poly = [tile(label("poly", t, h, c), [2, c.stop - c.start], F32) for t, h, c in items]
             for i, (t, h, c) in enumerate(items):
                 nc.vector.tensor_tensor(s[i][:], soft[t, h][:, :, c], q_sb[h][:, t, c].unsqueeze(1).to_broadcast([P, 2, c.stop - c.start]), MULT)
+            if between:
+                between()
             for i, (t, h, c) in enumerate(items):
                 nc.vector.scalar_tensor_tensor(poly[i][:], s[i][:], 1.0, s[i][:], SUBTRACT, MULT)
+            if later:
+                later()
             for i, (t, h, c) in enumerate(items):
                 nc.vector.scalar_tensor_tensor(force[h][:, t, :, c], poly[i][:], gn_sb[:, t : t + 1], d[t, h][:, :, c], MULT, MULT)
 
@@ -189,12 +193,11 @@ def tile_picked_ljpot_none_po_kernel(
             nc.vector.quantize_mx(out=z_codes[:].bitcast(FP8X4), scales=z_plane[:], in_=z16[:].rearrange("p j t -> p (j t)"))
             return z_codes, z_plane
 
-        def layer(h, cols, z, tags=(None, None, None)):
+        def products(h, cols, z):
             z_codes, z_plane = z
             width = cols.stop - cols.start
-            start = HALF * h + cols.start
-            result16 = tile("result16_%d" % start, [width, PACK], BF16, tags[0])
             n = min(width, BLOCK)
+            blocks = []
             for b in range(0, width, n):
                 out_bank = psum.tile([P, S], F32, name="bank", bufs=8)
                 sums = out_bank[:, : PACK * n].rearrange("p (t j) -> p t j", t=PACK)
@@ -208,43 +211,64 @@ def tile_picked_ljpot_none_po_kernel(
                         start=True,
                         stop=True,
                     )
-                js = slice(start + b, start + b + n)
-                (nc.vector.tensor_copy if js.stop == S and True else nc.scalar.copy)(out=result16[:, b : b + n, :], in_=sums.rearrange("p t j -> p j t"))
-                result = tile("result%d" % js.start, [PACK, n], F32, tags[1 + b // n])
-                nc.scalar.copy(out=result[:], in_=sums)
-                (nc.scalar if js.stop == S else nc.sync).dma_start(out=out_rows[:, :, js], in_=result[:])
+                blocks.append((slice(b, b + n), sums))
+            return HALF * h + cols.start, width, blocks
+
+        def rounded(start, width, blocks, tag=None):
+            result16 = tile("result16_%d" % start, [width, PACK], BF16, tag)
+            for cols, sums in blocks:
+                (nc.vector.tensor_copy if start + width == S else nc.scalar.copy)(out=result16[:, cols, :], in_=sums.rearrange("p t j -> p j t"))
             return start, width, result16
+
+        def stored(start, width, blocks, tag=None):
+            result = tile("result%d" % start, [PACK, width], F32, tag)
+            for cols, sums in blocks:
+                nc.scalar.copy(out=result[:, :, cols], in_=sums)
+            (nc.scalar if start + width == S else nc.sync).dma_start(out=out_rows[:, :, start : start + width], in_=result[:])
+
+        def layer(h, cols, z):
+            made = products(h, cols, z)
+            result16 = rounded(*made)
+            stored(*made)
+            return result16
 
         def planes(start, width, result16):
             js = slice(start, start + width)
             nc.vector.quantize_mx(out=out_codes[:, js].bitcast(FP8X4), scales=out_plane[:, js], in_=result16[:].rearrange("p j t -> p (j t)"))
-            nc.sync.dma_start(out=out_words[:, js], in_=out_codes[:, js])
+            if start + width >= S - 64:
+                done = slice(0 if start + width < S else start, start + width)
+                nc.sync.dma_start(out=out_words[:, done], in_=out_codes[:, done])
 
         whole, low, high = slice(0, HALF), slice(0, 128), slice(128, 256)
-        for t, h in ((0, 0), (1, 0), (2, 0), (3, 0), (0, 1), (1, 1)):
+        for t, h in ((0, 0), (1, 0), (2, 0), (3, 0), (0, 1)):
             gather(t, h)
         q_sb.append(tile("q1", [PACK, HALF], F32))
         nc.sync.dma_start(out=q_sb[1][:], in_=q_rows[:, :, HALF:])
         w2_plane = deal(nc.vector, "w2_plane", w2_raw_plane, U8, 0, 4, "p t m")
-        soften([(0, 0, whole), (1, 0, whole)])
-        soften([(2, 0, whole), (3, 0, whole)])
-        fetch(2, 1, "denom2_2_0_0")
-        fetch(3, 1, "denom2_3_0_0")
-        forces([(0, 0, whole), (1, 0, whole)])
-        forces([(2, 0, whole), (3, 0, whole)])
-        subtract(2, 1, None)
-        subtract(3, 1, None)
-        soften([(0, 1, whole), (1, 1, whole)])
-        soften([(2, 1, low), (3, 1, low)])
-        soften([(2, 1, high), (3, 1, high)])
+        soften([(0, 0, low), (0, 0, high)])
+        fetch(1, 1, "denom2_0_0_0")
+        soften([(1, 0, whole), (2, 0, whole)])
+        soften([(3, 0, whole), (0, 1, whole)])
+        fetch(2, 1, "denom2_3_0_0")
+        forces([(0, 0, low), (0, 0, high)])
+        subtract(1, 1, "poly0_0_0")
+        soften([(1, 1, whole)])
+        fetch(3, 1, "denom2_0_1_0")
+        forces([(1, 0, whole), (2, 0, whole)])
+        forces([(3, 0, whole), (0, 1, whole)], None, lambda: subtract(2, 1, "soft0_1"))
+        subtract(3, 1, "poly3_0_0")
+        soften([(2, 1, low), (2, 1, high)])
+        soften([(3, 1, low), (3, 1, high)])
         z = quantized(0, whole)
-        forces([(0, 1, whole), (1, 1, whole)])
-        waiting = layer(0, whole, z)
+        forces([(1, 1, low), (1, 1, high)])
+        made = products(0, whole, z)
+        stored(*made)
+        late = [rounded(*made)]
         for cols in (low, slice(128, 192), slice(192, 256)):
             forces([(2, 1, cols), (3, 1, cols)])
-            z = quantized(1, cols)
-            planes(*waiting)
-            waiting = layer(1, cols, z)
-        planes(*waiting)
+            late.append(layer(1, cols, quantized(1, cols)))
+        out_codes = tile("out_codes", [S], I32, "force1")
+        for piece in late:
+            planes(*piece)
         for quad in range(4):
             (nc.sync if quad < 2 else nc.scalar).dma_start(out=out_2[0, 4 * quad : 4 * quad + 4, :].bitcast(I32), in_=out_plane[32 * quad : 32 * quad + 4, :].bitcast(I32))

@@ -59,11 +59,17 @@ def tile_picked_ljpot_none_po_kernel(
         q_rows = q.rearrange("(p t) j -> p t j", t=PACK)
         q_sb = [tile("q0", [PACK, HALF], F32)]
 
-        load_plane(nc.sync, x_plane, x_scales)
+        x_rows = tile("x_rows", [T // 4], I32)
+        for r in range(4):
+            nc.sync.dma_start(out=x_rows[r:P:32, :], in_=x_scales[0].bitcast(I32)[r:16:4, :])
+        nc.vector.memset(x_plane[:].bitcast(I32), 0)
+        for quad in range(4):
+            rows = slice(32 * quad, 32 * quad + 4)
+            nc.vector.tensor_copy(out=x_plane[rows, :].bitcast(I32), in_=x_rows[rows, :])
         nc.sync.dma_start(offs_sb[:], offs)
         nc.sync.dma_start(out=x_table[:], in_=words_view(x_words))
-        load_plane(nc.sync, w1_raw_plane, w1_scales)
         nc.sync.dma_start(out=w1_raw[:], in_=words_view(w1_words))
+        load_plane(nc.sync, w1_raw_plane, w1_scales)
         nc.sync.dma_start(out=w2_raw[:], in_=words_view(w2_words))
         nc.sync.dma_start(p1_sb[:], p1)
         nc.sync.dma_start(p2_sb[:], p2)
@@ -87,15 +93,15 @@ def tile_picked_ljpot_none_po_kernel(
         nc.vector.tensor_copy(x_codes[0][:].bitcast(U32), x_table[:].bitcast(U32).indirect(offs_sb[:, 0:16]))
         w1_plane = deal(nc.vector, "w1_plane", w1_raw_plane, U8, 0, 4, "p t m")
         w1_codes = deal(nc.vector, "w1_codes", w1_raw, U32, 0, 4, "p m t")
-        x_codes.append(tile("x_codes1", [HALF], I32, "w1_raw"))
+        x_codes.append(tile("x_codes1", [HALF], I32, "w1_raw_plane"))
         nc.vector.tensor_copy(x_codes[1][:].bitcast(U32), x_table[:].bitcast(U32).indirect(offs_sb[:, 16:32]))
         w2_codes = deal(nc.vector, "w2_codes", w2_raw, U32, 0, 4, "p m t")
 
         y_window = [tile("y_window%d" % t, [S], F32) for t in range(PACK)]
         y_own = {}
         banks = {}
-        for t in range(PACK):
-            for h in range(2):
+        for t, h in ((0, 0), (1, 0), (0, 1), (1, 1), (2, 0), (2, 1), (3, 0), (3, 1)):
+            if True:
                 bank = psum.tile([P, S], F32, name="bank", bufs=8)
                 nc.tensor.matmul_mx(
                     out=bank[:, :HALF],
@@ -114,7 +120,10 @@ def tile_picked_ljpot_none_po_kernel(
                 (nc.vector.tensor_copy if (t, h) == (0, 1) else nc.scalar.copy)(out=y_window[t][:, cols], in_=banks[t, h][:, :HALF])
                 if (t, h) in ((0, 0), (1, 0), (2, 0), (3, 0)):
                     y_own[t, h] = tile("y_own%d_%d" % (t, h), [HALF], F32)
-                    nc.scalar.copy(out=y_own[t, h][:], in_=banks[t, h][:, :HALF])
+                    if t == 0:
+                        nc.vector.tensor_copy(out=y_own[t, h][:], in_=y_window[t][:, cols])
+                    else:
+                        nc.scalar.copy(out=y_own[t, h][:], in_=banks[t, h][:, :HALF])
                 if (t, h) in ():
                     y_own[t, h] = tile("y_own%d_%d" % (t, h), [HALF], F32)
                     nc.sync.dma_start(out=y_own[t, h][:], in_=y_window[t][:, cols])

@@ -1,6 +1,7 @@
 from contextlib import ExitStack
 
 import concourse.mybir as mybir
+from concourse.masks import make_identity
 
 F32 = mybir.dt.float32
 BF16 = mybir.dt.bfloat16
@@ -19,7 +20,6 @@ PACK = 4
 T = 2048
 S = 512
 HALF = S // 2
-BLOCK = 128
 FLOPS = 2 * 2 * 512 * 512 * 512
 
 
@@ -40,11 +40,13 @@ def tile_picked_ljpot_none_po_kernel(
     nc = tc.nc
     with ExitStack() as ctx:
         keep = ctx.enter_context(tc.tile_pool(name="keep", bufs=1))
-        work = ctx.enter_context(tc.tile_pool(name="work", bufs=2))
         psum = ctx.enter_context(tc.psum_pool(name="psum", bufs=1))
 
         def tile(name, shape, dtype, tag=None):
             return keep.tile([P] + shape, dtype, name=name, tag=tag or name, align_bytes=64)
+
+        def bank(name, number):
+            return psum.tile([P, S], F32, name=name, tag="bank%d" % number)
 
         offs_sb = keep.tile([P, S // 16], U16, name="offs_sb")
         p1_sb = keep.tile([P, S // 16], U16, name="p1_sb")
@@ -57,7 +59,7 @@ def tile_picked_ljpot_none_po_kernel(
         w2_raw_plane = tile("w2_raw_plane", [S], U8)
         gn_sb = tile("gn_sb", [PACK], F32)
         q_rows = q.rearrange("(p t) j -> p t j", t=PACK)
-        q_sb = [tile("q0", [PACK, HALF], F32)]
+        q_sb = [tile("q%d" % h, [PACK, HALF], F32) for h in range(2)]
 
         x_rows = tile("x_rows", [T // 4], I32)
         for r in range(4):
@@ -68,216 +70,262 @@ def tile_picked_ljpot_none_po_kernel(
             nc.vector.tensor_copy(out=x_plane[rows, :].bitcast(I32), in_=x_rows[rows, :])
         nc.sync.dma_start(offs_sb[:], offs)
         nc.sync.dma_start(out=x_table[:], in_=words_view(x_words))
-        nc.sync.dma_start(out=w1_raw[:], in_=words_view(w1_words))
         load_plane(nc.sync, w1_raw_plane, w1_scales)
+        nc.sync.dma_start(out=w1_raw[:], in_=words_view(w1_words))
         nc.sync.dma_start(out=w2_raw[:], in_=words_view(w2_words))
         nc.sync.dma_start(p1_sb[:], p1)
         nc.sync.dma_start(p2_sb[:], p2)
         load_plane(nc.sync, w2_raw_plane, w2_scales)
         nc.sync.dma_start(out=gn_sb[:], in_=gn.rearrange("(p t) o -> p (t o)", t=PACK))
-        nc.sync.dma_start(out=q_sb[0][:], in_=q_rows[:, :, :HALF])
+        for h in range(2):
+            nc.sync.dma_start(out=q_sb[h][:], in_=q_rows[:, :, HALF * h : HALF * (h + 1)])
 
         warm = tile("warm", [2], F32)
         nc.gpsimd.memset(warm[:, 0:1], 1.0)
         nc.scalar.activation(out=warm[:, 1:2], in_=warm[:, 0:1], func=ACT.Abs_reciprocal_sqrt)
+        identity = tile("identity", [P], F32)
+        make_identity(nc, identity[:])
 
-        def deal(engine, name, raw, dtype, first, count, order):
-            dealt = tile(name, [count * P], I32 if dtype == U32 else U8)
+        def deal(name, raw, dtype, first, count, order, tag=None):
+            dealt = tile(name, [count * P], I32 if dtype == U32 else U8, tag)
             source = raw[:].bitcast(dtype).rearrange("p (m t) -> p m t", t=PACK)[:, :, first : first + count]
-            engine.tensor_copy(out=dealt[:].bitcast(dtype).rearrange("p (t m) -> " + order, t=count), in_=source.rearrange("p m t -> " + order))
+            nc.vector.tensor_copy(out=dealt[:].bitcast(dtype).rearrange("p (t m) -> " + order, t=count), in_=source.rearrange("p m t -> " + order))
             return [dealt[:, P * t : P * (t + 1)] for t in range(count)]
+
+        def turn(out, block, start=True, stop=True):
+            nc.tensor.matmul(out=out, lhsT=block, rhs=identity[:], start=start, stop=stop, is_transpose=True)
+
+        def product(out, codes, plane, moving, moving_plane):
+            nc.tensor.matmul_mx(
+                out=out, lhsT=codes.bitcast(FP8X4), lhsT_scale=plane, rhs=moving.bitcast(FP8X4), rhs_scale=moving_plane, start=True, stop=True
+            )
 
         x_picked_plane = tile("x_picked_plane", [S], U8, tag="w2_plane")
         nc.vector.tensor_copy(x_picked_plane[:], x_plane[:].indirect(offs_sb[:]))
-        x_codes = [tile("x_codes0", [HALF], I32)]
-        nc.vector.tensor_copy(x_codes[0][:].bitcast(U32), x_table[:].bitcast(U32).indirect(offs_sb[:, 0:16]))
-        w1_plane = deal(nc.vector, "w1_plane", w1_raw_plane, U8, 0, 4, "p t m")
-        w1_codes = deal(nc.vector, "w1_codes", w1_raw, U32, 0, 4, "p m t")
-        x_codes.append(tile("x_codes1", [HALF], I32, "w1_raw_plane"))
-        nc.vector.tensor_copy(x_codes[1][:].bitcast(U32), x_table[:].bitcast(U32).indirect(offs_sb[:, 16:32]))
-        w2_codes = deal(nc.vector, "w2_codes", w2_raw, U32, 0, 4, "p m t")
+        x_codes = tile("x_codes", [S], I32)
+        for h in range(2):
+            nc.vector.tensor_copy(x_codes[:, HALF * h : HALF * (h + 1)].bitcast(U32), x_table[:].bitcast(U32).indirect(offs_sb[:, 16 * h : 16 * (h + 1)]))
+        w1_plane = deal("w1_plane0", w1_raw_plane, U8, 0, 1, "p t m")
+        w1_codes = deal("w1_codes0", w1_raw, U32, 0, 1, "p m t")
+        w1_codes = w1_codes + deal("w1_codes", w1_raw, U32, 1, 3, "p m t")
+        w1_plane = w1_plane + deal("w1_plane", w1_raw_plane, U8, 1, 3, "p t m", "w1_raw")
+        w2_codes = deal("w2_codes", w2_raw, U32, 0, 4, "p m t", "w1_raw_plane")
 
         y_window = [tile("y_window%d" % t, [S], F32) for t in range(PACK)]
-        y_own = {}
-        banks = {}
-        for t, h in ((0, 0), (1, 0), (0, 1), (1, 1), (2, 0), (2, 1), (3, 0), (3, 1)):
-            if True:
-                bank = psum.tile([P, S], F32, name="bank", bufs=8)
-                nc.tensor.matmul_mx(
-                    out=bank[:, :HALF],
-                    lhsT=w1_codes[t].bitcast(FP8X4),
-                    lhsT_scale=w1_plane[t],
-                    rhs=x_codes[h][:].bitcast(FP8X4),
-                    rhs_scale=x_picked_plane[:, HALF * h : HALF * (h + 1)],
-                    start=True,
-                    stop=True,
-                )
-                banks[t, h] = bank
+        y_own = {(t, h): tile("y_own%d_%d" % (t, h), [HALF], F32) for t in range(PACK) for h in range(2) if (t, h) != (3, 0)}
+        halves = [slice(0, HALF), slice(HALF, S)]
+        y_banks = [bank("y%d" % n, n) for n in range(5)]
+        for h in range(2):
+            product(y_banks[h][:, :HALF], w1_codes[0], w1_plane[0], x_codes[:, halves[h]], x_picked_plane[:, halves[h]])
+        for t in range(1, PACK):
+            product(y_banks[t + 1][:], w1_codes[t], w1_plane[t], x_codes[:], x_picked_plane[:])
+        nc.scalar.copy(out=y_window[0][:, halves[0]], in_=y_banks[0][:, :HALF])
+        nc.scalar.copy(out=y_own[0, 0][:], in_=y_banks[0][:, :HALF])
+        nc.vector.tensor_copy(out=y_window[0][:, halves[1]], in_=y_banks[1][:, :HALF])
+        for t in range(1, PACK):
+            nc.scalar.copy(out=y_window[t][:], in_=y_banks[t + 1][:])
+            if t < PACK - 1:
+                nc.scalar.copy(out=y_own[t, 0][:], in_=y_banks[t + 1][:, :HALF])
 
-        for t in range(PACK):
-            for h in range(2):
-                cols = slice(HALF * h, HALF * (h + 1))
-                (nc.vector.tensor_copy if (t, h) == (0, 1) else nc.scalar.copy)(out=y_window[t][:, cols], in_=banks[t, h][:, :HALF])
-                if (t, h) in ((0, 0), (1, 0), (2, 0), (3, 0)):
-                    y_own[t, h] = tile("y_own%d_%d" % (t, h), [HALF], F32)
-                    if t == 0:
-                        nc.vector.tensor_copy(out=y_own[t, h][:], in_=y_window[t][:, cols])
-                    else:
-                        nc.scalar.copy(out=y_own[t, h][:], in_=banks[t, h][:, :HALF])
-                if (t, h) in ():
-                    y_own[t, h] = tile("y_own%d_%d" % (t, h), [HALF], F32)
-                    nc.sync.dma_start(out=y_own[t, h][:], in_=y_window[t][:, cols])
-        y_own[0, 1] = tile("y_own0_1", [HALF], F32)
-        nc.scalar.copy(out=y_own[0, 1][:], in_=banks[0, 1][:, :HALF])
-
-        out_plane = tile("out_plane", [S], U8)
-        out_rows = out_0.rearrange("(p t) j -> p t j", t=PACK)
-        out_words = words_view(out_1)
         lists = (p1_sb, p2_sb)
+        d_bank, q_bank, soft, s, m, force = {}, {}, {}, {}, {}, {}
+
+        def blocks(view):
+            return view.rearrange("j (c k p) -> j c k p", c=2, k=2)
 
         d = {}
-        soft = {}
-        fetched = {}
-        force = [tile("force%d" % h, [PACK, 2, HALF], F32) for h in range(2)]
 
-        def gather(t, h):
-            d[t, h] = tile("d%d_%d" % (t, h), [2, HALF], F32)
+        def gather(t, h, tag=None):
+            d[t, h] = tile("d%d_%d" % (t, h), [2, HALF], F32, tag)
             for k in range(2):
                 nc.vector.tensor_tensor(d[t, h][:, k, :], y_window[t][:].indirect(lists[k][:, 16 * h : 16 * (h + 1)]), y_own[t, h][:], SUBTRACT)
 
-        def fetch(t, h, tag):
-            fetched[t, h] = tile("fetched%d_%d" % (t, h), [2, HALF], F32, tag)
+        def turn_over(t, h, number):
+            d_bank[t, h] = bank("d_bank%d_%d" % (t, h), number)
             for k in range(2):
-                nc.scalar.activation(out=fetched[t, h][:, k, :], in_=y_window[t][:].indirect(lists[k][:, 16 * h : 16 * (h + 1)]), func=ACT.Copy)
+                for c in range(2):
+                    turn(blocks(d_bank[t, h][:])[:, c, k, :], d[t, h][:, k, P * c : P * (c + 1)])
 
-        def subtract(t, h, tag):
-            d[t, h] = tile("d%d_%d" % (t, h), [2, HALF], F32, tag)
-            own = y_window[t][:, HALF * h : HALF * (h + 1)].unsqueeze(1).to_broadcast([P, 2, HALF])
-            nc.vector.tensor_tensor(d[t, h][:], fetched[t, h][:], own, SUBTRACT)
+        def fetch(t, h, number, tag=None):
+            fetched = tile("fetched%d_%d" % (t, h), [2, HALF], F32, tag)
+            for k in range(2):
+                nc.scalar.activation(out=fetched[:, k, :], in_=y_window[t][:].indirect(lists[k][:, 16 * h : 16 * (h + 1)]), func=ACT.Copy, scale=-1.0)
+            d_bank[t, h] = bank("d_bank%d_%d" % (t, h), number)
+            for k in range(2):
+                for c in range(2):
+                    out = blocks(d_bank[t, h][:])[:, c, k, :]
+                    turn(out, y_window[t][:, HALF * h + P * c : HALF * h + P * (c + 1)], True, False)
+                    turn(out, fetched[:, k, P * c : P * (c + 1)], False, True)
 
-        def label(name, t, h, cols):
-            return "%s%d_%d_%d" % (name, t, h, cols.start)
+        def strengths(units, number):
+            held = bank("q_bank%d_%d" % units[0], number)
+            for i, (t, h) in enumerate(units):
+                q_bank[t, h] = held[:, HALF * i : HALF * (i + 1)].rearrange("j (c p) -> j c p", c=2)
+                for c in range(2):
+                    turn(q_bank[t, h][:, c, :], q_sb[h][:, t, P * c : P * (c + 1)])
 
-        def soften(items, tags=None):
-            if tags:
-                d2 = [tile(label("d2_", t, h, c), [2, c.stop - c.start], F32, tag) for (t, h, c), tag in zip(items, tags)]
-            else:
-                d2 = [work.tile([P, 2, c.stop - c.start], F32, name="d2", bufs=2, align_bytes=64) for t, h, c in items]
-            denom2 = [tile(label("denom2_", t, h, c), [2, c.stop - c.start], F32) for t, h, c in items]
-            for t, h, c in items:
-                if (t, h) not in soft:
-                    soft[t, h] = tile("soft%d_%d" % (t, h), [2, HALF], F32)
-            for i, (t, h, c) in enumerate(items):
-                nc.scalar.activation(out=d2[i][:], in_=d[t, h][:, :, c], func=ACT.Square)
-            for i, (t, h, c) in enumerate(items):
+        def label(name, t, h, cs):
+            return "%s%d_%d_%d" % (name, t, h, cs.start)
+
+        def span(cs):
+            return slice(HALF * cs.start, HALF * cs.stop)
+
+        def fresh(name, items, tags=None):
+            return [tile(label(name, t, h, cs), [HALF * (cs.stop - cs.start)], F32, tag) for (t, h, cs), tag in zip(items, tags or [None] * len(items))]
+
+        def soften(items, tags=None, between=None):
+            d2, denom2 = fresh("d2_", items, tags), fresh("denom2_", items)
+            for item, made in zip(items, fresh("soft", items)):
+                soft[item[0], item[1], item[2].start] = made
+            for i, (t, h, cs) in enumerate(items):
+                nc.scalar.activation(out=d2[i][:], in_=d_bank[t, h][:, span(cs)], func=ACT.Square)
+                if between and i == 0:
+                    between()
+            for i, (t, h, cs) in enumerate(items):
                 nc.scalar.activation(out=denom2[i][:], in_=d2[i][:], func=ACT.Square, bias=1.0)
-            for i, (t, h, c) in enumerate(items):
-                nc.scalar.activation(out=soft[t, h][:, :, c], in_=denom2[i][:], func=ACT.Abs_reciprocal_sqrt)
+            for i, (t, h, cs) in enumerate(items):
+                nc.scalar.activation(out=soft[t, h, cs.start][:], in_=denom2[i][:], func=ACT.Abs_reciprocal_sqrt)
 
-        def forces(items, between=None, later=None):
-            s = [work.tile([P, 2, c.stop - c.start], F32, name="s", bufs=4, align_bytes=64) for t, h, c in items]
-            poly = [tile(label("poly", t, h, c), [2, c.stop - c.start], F32) for t, h, c in items]
-            for i, (t, h, c) in enumerate(items):
-                nc.vector.tensor_tensor(s[i][:], soft[t, h][:, :, c], q_sb[h][:, t, c].unsqueeze(1).to_broadcast([P, 2, c.stop - c.start]), MULT)
-            if between:
-                between()
-            for i, (t, h, c) in enumerate(items):
-                nc.vector.scalar_tensor_tensor(poly[i][:], s[i][:], 1.0, s[i][:], SUBTRACT, MULT)
-            if later:
-                later()
-            for i, (t, h, c) in enumerate(items):
-                nc.vector.scalar_tensor_tensor(force[h][:, t, :, c], poly[i][:], gn_sb[:, t : t + 1], d[t, h][:, :, c], MULT, MULT)
+        def factors(items):
+            for item, made, other in zip(items, fresh("s", items), fresh("m", items)):
+                s[item[0], item[1], item[2].start] = made
+                m[item[0], item[1], item[2].start] = other
+            for t, h, cs in items:
+                n = cs.stop - cs.start
+                shaped = lambda view: view.rearrange("j (c k p) -> j c k p", c=n, k=2)
+                nc.vector.tensor_tensor(shaped(s[t, h, cs.start][:]), shaped(soft[t, h, cs.start][:]), q_bank[t, h][:, cs, :].unsqueeze(2).to_broadcast([P, n, 2, P]), MULT)
+            for t, h, cs in items:
+                nc.vector.scalar_tensor_tensor(m[t, h, cs.start][:], s[t, h, cs.start][:], 1.0, d_bank[t, h][:, span(cs)], SUBTRACT, MULT)
 
-        def quantized(h, cols):
-            width = cols.stop - cols.start
-            z16 = work.tile([P, width, PACK], BF16, name="z16", bufs=2, align_bytes=64)
-            nc.vector.tensor_tensor(
-                z16[:].rearrange("p (c i) t -> p c t i", i=2),
-                force[h][:, :, 0, cols].rearrange("p t (c i) -> p c t i", i=2),
-                force[h][:, :, 1, cols].rearrange("p t (c i) -> p c t i", i=2),
-                ADD,
-            )
-            z_codes = work.tile([P, width], I32, name="z_codes", bufs=2, align_bytes=64)
-            z_plane = work.tile([P, width], U8, name="z_plane", bufs=2, align_bytes=64)
+        def forces(engine, items, tiles=None):
+            tiles = tiles or [made[:] for made in fresh("force", items)]
+            for (t, h, cs), made in zip(items, tiles):
+                engine.tensor_tensor(made, m[t, h, cs.start][:], s[t, h, cs.start][:], MULT)
+                for c in range(cs.start, cs.stop):
+                    force[t, h, c] = made[:, HALF * (c - cs.start) : HALF * (c - cs.start + 1)]
+
+        def turn_back(z_bank, t, h, c):
+            for k in range(2):
+                turn(z_bank[:, P * t : P * (t + 1)], force[t, h, c][:, P * k : P * (k + 1)], k == 0, k == 1)
+
+        out_plane = tile("out_plane", [S], U8)
+        out_codes = tile("out_codes", [S], I32)
+        out_rows = out_0.rearrange("(p t) j -> p t j", t=PACK)
+        out_words = words_view(out_1)
+
+        gain = [tile("gain0", [PACK], F32), gn_sb]
+        nc.gpsimd.tensor_copy(out=gain[0][:, 0:3], in_=gn_sb[:, 0:3])
+        nc.gpsimd.tensor_scalar(out=gain[0][:, 3:4], in0=gn_sb[:, 3:4], scalar1=-1.0, scalar2=0.0, op0=MULT, op1=ADD)
+
+        def weighted(start, width, z_bank, tag=None):
+            cols = slice(start % P, start % P + width)
+            z16 = tile("z16_%d" % start, [width, PACK], BF16, tag)
+            sums = z_bank[:].rearrange("p (t j) -> p j t", t=PACK)[:, cols, :]
+            nc.vector.tensor_tensor(z16[:], sums, gain[start // HALF][:].unsqueeze(1).to_broadcast([P, width, PACK]), MULT)
+            return z16
+
+        def quantized(start, width, z16, tag=None):
+            z_codes = tile("z_codes%d" % start, [width], I32, tag)
+            z_plane = tile("z_plane%d" % start, [width], U8)
             nc.vector.quantize_mx(out=z_codes[:].bitcast(FP8X4), scales=z_plane[:], in_=z16[:].rearrange("p j t -> p (j t)"))
             return z_codes, z_plane
 
-        def products(h, cols, z):
-            z_codes, z_plane = z
-            width = cols.stop - cols.start
-            n = min(width, BLOCK)
-            blocks = []
-            for b in range(0, width, n):
-                out_bank = psum.tile([P, S], F32, name="bank", bufs=8)
-                sums = out_bank[:, : PACK * n].rearrange("p (t j) -> p t j", t=PACK)
-                for t in range(PACK):
-                    nc.tensor.matmul_mx(
-                        out=sums[:, t, :],
-                        lhsT=w2_codes[t].bitcast(FP8X4),
-                        lhsT_scale=w2_plane[t],
-                        rhs=z_codes[:, b : b + n].bitcast(FP8X4),
-                        rhs_scale=z_plane[:, b : b + n],
-                        start=True,
-                        stop=True,
-                    )
-                blocks.append((slice(b, b + n), sums))
-            return HALF * h + cols.start, width, blocks
+        def layer(start, width, z, number):
+            sums = bank("out_bank%d" % start, number)[:, : PACK * width].rearrange("p (t j) -> p t j", t=PACK)
+            for t in range(PACK):
+                product(sums[:, t, :], w2_codes[t], w2_plane[t], z[0][:], z[1][:])
+            return sums
 
-        def rounded(start, width, blocks, tag=None):
-            result16 = tile("result16_%d" % start, [width, PACK], BF16, tag)
-            for cols, sums in blocks:
-                (nc.vector.tensor_copy if start + width == S else nc.scalar.copy)(out=result16[:, cols, :], in_=sums.rearrange("p t j -> p j t"))
+        def rounded(engine_copy, start, width, sums):
+            result16 = tile("result16_%d" % start, [width, PACK], BF16)
+            engine_copy(out=result16[:], in_=sums.rearrange("p t j -> p j t"))
             return start, width, result16
-
-        def stored(start, width, blocks, tag=None):
-            result = tile("result%d" % start, [PACK, width], F32, tag)
-            for cols, sums in blocks:
-                nc.scalar.copy(out=result[:, :, cols], in_=sums)
-            (nc.scalar if start + width == S else nc.sync).dma_start(out=out_rows[:, :, start : start + width], in_=result[:])
-
-        def layer(h, cols, z):
-            made = products(h, cols, z)
-            result16 = rounded(*made)
-            stored(*made)
-            return result16
 
         def planes(start, width, result16):
             js = slice(start, start + width)
             nc.vector.quantize_mx(out=out_codes[:, js].bitcast(FP8X4), scales=out_plane[:, js], in_=result16[:].rearrange("p j t -> p (j t)"))
-            if start + width >= S - 64:
-                done = slice(0 if start + width < S else start, start + width)
-                nc.sync.dma_start(out=out_words[:, done], in_=out_codes[:, done])
 
-        whole, low, high = slice(0, HALF), slice(0, 128), slice(128, 256)
-        for t, h in ((0, 0), (1, 0), (2, 0), (3, 0), (0, 1)):
-            gather(t, h)
-        q_sb.append(tile("q1", [PACK, HALF], F32))
-        nc.sync.dma_start(out=q_sb[1][:], in_=q_rows[:, :, HALF:])
-        w2_plane = deal(nc.vector, "w2_plane", w2_raw_plane, U8, 0, 4, "p t m")
-        soften([(0, 0, low), (0, 0, high)])
-        fetch(1, 1, "denom2_0_0_0")
-        soften([(1, 0, whole), (2, 0, whole)])
-        soften([(3, 0, whole), (0, 1, whole)])
-        fetch(2, 1, "denom2_3_0_0")
-        forces([(0, 0, low), (0, 0, high)])
-        subtract(1, 1, "poly0_0_0")
-        soften([(1, 1, whole)])
-        fetch(3, 1, "denom2_0_1_0")
-        forces([(1, 0, whole), (2, 0, whole)])
-        forces([(3, 0, whole), (0, 1, whole)], None, lambda: subtract(2, 1, "soft0_1"))
-        subtract(3, 1, "poly3_0_0")
-        soften([(2, 1, low), (2, 1, high)])
-        soften([(3, 1, low), (3, 1, high)])
-        z = quantized(0, whole)
-        forces([(1, 1, low), (1, 1, high)])
-        made = products(0, whole, z)
-        stored(*made)
-        late = [rounded(*made)]
-        for cols in (low, slice(128, 192), slice(192, 256)):
-            forces([(2, 1, cols), (3, 1, cols)])
-            late.append(layer(1, cols, quantized(1, cols)))
-        out_codes = tile("out_codes", [S], I32, "force1")
-        for piece in late:
+        both, first, second = slice(0, 2), slice(0, 1), slice(1, 2)
+        for t, number in ((0, 5), (1, 6), (2, 0)):
+            gather(t, 0)
+            turn_over(t, 0, number)
+        for t in range(PACK):
+            nc.vector.tensor_copy(out=y_own[t, 1][:], in_=y_window[t][:, halves[1]])
+        gather(0, 1, "d1_0")
+        gather(1, 1, "d2_0")
+        pairs = [[(0, 0, both), (1, 0, both)], [(2, 0, both), (3, 0, both)], [(0, 1, both), (1, 1, both)]]
+        soften(pairs[0], None, lambda: fetch(3, 0, 1))
+        turn_over(0, 1, 2)
+        turn_over(1, 1, 3)
+        gather(2, 1, "y_own0_1")
+        gather(3, 1, "y_own1_1")
+        strengths([(0, 0), (1, 0)], 7)
+        strengths([(2, 0), (3, 0)], 4)
+        soften(pairs[1])
+        w2_plane = deal("w2_plane", w2_raw_plane, U8, 0, 4, "p t m")
+        factors(pairs[0])
+        strengths([(0, 1), (1, 1)], 7)
+        turn_over(2, 1, 5)
+        turn_over(3, 1, 6)
+        forces(nc.gpsimd, pairs[0])
+        soften(pairs[2])
+        factors(pairs[1])
+        forces(nc.gpsimd, pairs[1])
+        strengths([(2, 1), (3, 1)], 4)
+        z_banks = {(0, c): bank("z_bank0_%d" % c, c) for c in range(2)}
+        for t in range(PACK):
+            for c in range(2):
+                turn_back(z_banks[0, c], t, 0, c)
+        factors(pairs[2])
+        forces(nc.gpsimd, pairs[2])
+        z_banks[1, 0] = bank("z_bank1_0", 2)
+        z_banks[1, 1] = bank("z_bank1_1", 3)
+        for t in range(2):
+            for c in range(2):
+                turn_back(z_banks[1, c], t, 1, c)
+        last = [[(2, 1, cs), (3, 1, cs)] for cs in (first, second)]
+        for c in range(2):
+            soften(last[c])
+        for c in range(2):
+            factors(last[c])
+        z16 = [weighted(P * c, P, z_banks[0, c], ("soft2_1_1", "soft3_1_1")[c]) for c in range(2)]
+
+        def stored(queue, start, parts):
+            width = sum(part.shape[2] for part in parts)
+            result = tile("result%d" % start, [PACK, width], F32)
+            at = 0
+            for part in parts:
+                nc.scalar.copy(out=result[:, :, at : at + part.shape[2]], in_=part)
+                at = at + part.shape[2]
+            queue.dma_start(out=out_rows[:, :, start : start + width], in_=result[:])
+
+        sums = layer(0, P, quantized(0, P, z16[0]), 7)
+        stored(nc.sync, 0, [sums])
+        late = [rounded(nc.scalar.copy, 0, P, sums)]
+        last_forces = tile("last_forces", [2, 2, HALF], F32, "gain0")
+        for c in range(2):
+            forces(nc.vector, last[c], [last_forces[:, c, i, :] for i in range(2)])
+            for t in (2, 3):
+                turn_back(z_banks[1, c], t, 1, c)
+        sums = layer(P, P, quantized(P, P, z16[1], "m3_1_1"), 0)
+        stored(nc.sync, P, [sums])
+        late.append(rounded(nc.scalar.copy, P, P, sums))
+        pieces = ((256, P, 1), (384, 64, 4), (448, 64, 5))
+        z16 = [weighted(start, width, z_banks[1, (start - HALF) // P]) for start, width, number in pieces[:2]]
+        z = [quantized(256, P, z16[0])]
+        z16.append(weighted(448, 64, z_banks[1, 1]))
+        z = z + [quantized(384, 64, z16[1]), quantized(448, 64, z16[2])]
+        sums = [layer(start, width, made, number) for (start, width, number), made in zip(pieces, z)]
+        late.append(rounded(nc.scalar.copy, 256, P, sums[0]))
+        late.append(rounded(nc.vector.tensor_copy, 384, 64, sums[1]))
+        late.append(rounded(nc.vector.tensor_copy, 448, 64, sums[2]))
+        stored(nc.sync, 256, sums[:1])
+        for piece in late[:2]:
             planes(*piece)
+        nc.sync.dma_start(out=out_words[:, :HALF], in_=out_codes[:, :HALF])
+        for piece in late[2:]:
+            planes(*piece)
+        nc.sync.dma_start(out=out_words[:, HALF:], in_=out_codes[:, HALF:])
+        stored(nc.scalar, 384, sums[1:])
         for quad in range(4):
             (nc.sync if quad < 2 else nc.scalar).dma_start(out=out_2[0, 4 * quad : 4 * quad + 4, :].bitcast(I32), in_=out_plane[32 * quad : 32 * quad + 4, :].bitcast(I32))

@@ -114,18 +114,19 @@ def tile_picked_ljpot_none_po_kernel(
         y_window = [tile("y_window%d" % t, [S], F32) for t in range(PACK)]
         y_own = {(t, h): tile("y_own%d_%d" % (t, h), [HALF], F32) for t in range(PACK) for h in range(2) if (t, h) != (3, 0)}
         halves = [slice(0, HALF), slice(HALF, S)]
-        y_banks = [bank("y%d" % n, n) for n in range(5)]
-        for h in range(2):
-            product(y_banks[h][:, :HALF], w1_codes[0], w1_plane[0], x_codes[:, halves[h]], x_picked_plane[:, halves[h]])
-        for t in range(1, PACK):
-            product(y_banks[t + 1][:], w1_codes[t], w1_plane[t], x_codes[:], x_picked_plane[:])
-        nc.scalar.copy(out=y_window[0][:, halves[0]], in_=y_banks[0][:, :HALF])
-        nc.scalar.copy(out=y_own[0, 0][:], in_=y_banks[0][:, :HALF])
-        nc.vector.tensor_copy(out=y_window[0][:, halves[1]], in_=y_banks[1][:, :HALF])
-        for t in range(1, PACK):
-            nc.scalar.copy(out=y_window[t][:], in_=y_banks[t + 1][:])
-            if t < PACK - 1:
-                nc.scalar.copy(out=y_own[t, 0][:], in_=y_banks[t + 1][:, :HALF])
+        y_banks = [bank("y%d" % n, n) for n in range(6)]
+        for t in range(2):
+            for h in range(2):
+                product(y_banks[2 * t + h][:, :HALF], w1_codes[t], w1_plane[t], x_codes[:, halves[h]], x_picked_plane[:, halves[h]])
+        for t in range(2, PACK):
+            product(y_banks[t + 2][:], w1_codes[t], w1_plane[t], x_codes[:], x_picked_plane[:])
+        for t in range(2):
+            nc.scalar.copy(out=y_window[t][:, halves[0]], in_=y_banks[2 * t][:, :HALF])
+            nc.scalar.copy(out=y_own[t, 0][:], in_=y_banks[2 * t][:, :HALF])
+            (nc.scalar.copy if t else nc.vector.tensor_copy)(out=y_window[t][:, halves[1]], in_=y_banks[2 * t + 1][:, :HALF])
+        nc.scalar.copy(out=y_window[2][:], in_=y_banks[4][:])
+        nc.scalar.copy(out=y_own[2, 0][:], in_=y_banks[4][:, :HALF])
+        nc.scalar.copy(out=y_window[3][:], in_=y_banks[5][:])
 
         lists = (p1_sb, p2_sb)
         d_bank, q_bank, soft, s, m, force = {}, {}, {}, {}, {}, {}
@@ -135,8 +136,7 @@ def tile_picked_ljpot_none_po_kernel(
 
         d = {}
 
-        def gather(t, h, tag=None):
-            d[t, h] = tile("d%d_%d" % (t, h), [2, HALF], F32, tag)
+        def gather(t, h):
             for k in range(2):
                 nc.vector.tensor_tensor(d[t, h][:, k, :], y_window[t][:].indirect(lists[k][:, 16 * h : 16 * (h + 1)]), y_own[t, h][:], SUBTRACT)
 
@@ -153,9 +153,10 @@ def tile_picked_ljpot_none_po_kernel(
             d_bank[t, h] = bank("d_bank%d_%d" % (t, h), number)
             for k in range(2):
                 for c in range(2):
-                    out = blocks(d_bank[t, h][:])[:, c, k, :]
-                    turn(out, y_window[t][:, HALF * h + P * c : HALF * h + P * (c + 1)], True, False)
-                    turn(out, fetched[:, k, P * c : P * (c + 1)], False, True)
+                    turn(blocks(d_bank[t, h][:])[:, c, k, :], y_window[t][:, HALF * h + P * c : HALF * h + P * (c + 1)], k + c == 0, False)
+            for k in range(2):
+                for c in range(2):
+                    turn(blocks(d_bank[t, h][:])[:, c, k, :], fetched[:, k, P * c : P * (c + 1)], False, k + c == 2)
 
         def strengths(units, number):
             held = bank("q_bank%d_%d" % units[0], number)
@@ -186,16 +187,19 @@ def tile_picked_ljpot_none_po_kernel(
             for i, (t, h, cs) in enumerate(items):
                 nc.scalar.activation(out=soft[t, h, cs.start][:], in_=denom2[i][:], func=ACT.Abs_reciprocal_sqrt)
 
-        def factors(items):
+        def factors(items, split=False):
             for item, made, other in zip(items, fresh("s", items), fresh("m", items)):
                 s[item[0], item[1], item[2].start] = made
                 m[item[0], item[1], item[2].start] = other
-            for t, h, cs in items:
-                n = cs.stop - cs.start
-                shaped = lambda view: view.rearrange("j (c k p) -> j c k p", c=n, k=2)
-                nc.vector.tensor_tensor(shaped(s[t, h, cs.start][:]), shaped(soft[t, h, cs.start][:]), q_bank[t, h][:, cs, :].unsqueeze(2).to_broadcast([P, n, 2, P]), MULT)
-            for t, h, cs in items:
-                nc.vector.scalar_tensor_tensor(m[t, h, cs.start][:], s[t, h, cs.start][:], 1.0, d_bank[t, h][:, span(cs)], SUBTRACT, MULT)
+            parts = [(t, h, cs, part) for t, h, cs in items for part in ([slice(c, c + 1) for c in range(cs.start, cs.stop)] if split else [cs])]
+            for t, h, cs, part in parts:
+                n = part.stop - part.start
+                inside = span(slice(part.start - cs.start, part.stop - cs.start))
+                shaped = lambda view: view[:, inside].rearrange("j (c k p) -> j c k p", c=n, k=2)
+                nc.vector.tensor_tensor(shaped(s[t, h, cs.start]), shaped(soft[t, h, cs.start]), q_bank[t, h][:, part, :].unsqueeze(2).to_broadcast([P, n, 2, P]), MULT)
+            for t, h, cs, part in parts:
+                inside = span(slice(part.start - cs.start, part.stop - cs.start))
+                nc.vector.scalar_tensor_tensor(m[t, h, cs.start][:, inside], s[t, h, cs.start][:, inside], 1.0, d_bank[t, h][:, span(part)], SUBTRACT, MULT)
 
         def forces(engine, items, tiles=None):
             tiles = tiles or [made[:] for made in fresh("force", items)]
@@ -212,10 +216,6 @@ def tile_picked_ljpot_none_po_kernel(
         out_codes = tile("out_codes", [S], I32)
         out_rows = out_0.rearrange("(p t) j -> p t j", t=PACK)
         out_words = words_view(out_1)
-
-        gain = [tile("gain0", [PACK], F32), gn_sb]
-        nc.gpsimd.tensor_copy(out=gain[0][:, 0:3], in_=gn_sb[:, 0:3])
-        nc.gpsimd.tensor_scalar(out=gain[0][:, 3:4], in0=gn_sb[:, 3:4], scalar1=-1.0, scalar2=0.0, op0=MULT, op1=ADD)
 
         def weighted(start, width, z_bank, tag=None):
             cols = slice(start % P, start % P + width)
@@ -246,32 +246,37 @@ def tile_picked_ljpot_none_po_kernel(
             nc.vector.quantize_mx(out=out_codes[:, js].bitcast(FP8X4), scales=out_plane[:, js], in_=result16[:].rearrange("p j t -> p (j t)"))
 
         both, first, second = slice(0, 2), slice(0, 1), slice(1, 2)
-        for t, number in ((0, 5), (1, 6), (2, 0)):
+        for t, number in ((0, 6), (1, 7), (2, 0)):
+            d[t, 0] = tile("d%d_0" % t, [2, HALF], F32)
             gather(t, 0)
             turn_over(t, 0, number)
         for t in range(PACK):
             nc.vector.tensor_copy(out=y_own[t, 1][:], in_=y_window[t][:, halves[1]])
-        gather(0, 1, "d1_0")
-        gather(1, 1, "d2_0")
+        d_second = tile("d_second", [PACK, 2, HALF], F32, "d1_0")
+        for t in range(PACK):
+            d[t, 1] = d_second[:, t]
+            gather(t, 1)
         pairs = [[(0, 0, both), (1, 0, both)], [(2, 0, both), (3, 0, both)], [(0, 1, both), (1, 1, both)]]
         soften(pairs[0], None, lambda: fetch(3, 0, 1))
         turn_over(0, 1, 2)
         turn_over(1, 1, 3)
-        gather(2, 1, "y_own0_1")
-        gather(3, 1, "y_own1_1")
-        strengths([(0, 0), (1, 0)], 7)
-        strengths([(2, 0), (3, 0)], 4)
+        gain = [tile("gain0", [PACK], F32, "y_own3_1"), gn_sb]
+        nc.gpsimd.tensor_copy(out=gain[0][:, 0:3], in_=gn_sb[:, 0:3])
+        nc.gpsimd.tensor_scalar(out=gain[0][:, 3:4], in0=gn_sb[:, 3:4], scalar1=-1.0, scalar2=0.0, op0=MULT, op1=ADD)
+        strengths([(0, 0), (1, 0)], 4)
+        strengths([(2, 0), (3, 0)], 5)
         soften(pairs[1])
         w2_plane = deal("w2_plane", w2_raw_plane, U8, 0, 4, "p t m")
-        factors(pairs[0])
-        strengths([(0, 1), (1, 1)], 7)
-        turn_over(2, 1, 5)
-        turn_over(3, 1, 6)
+        for item in pairs[0]:
+            factors([item], True)
+        strengths([(0, 1), (1, 1)], 4)
+        turn_over(2, 1, 6)
+        turn_over(3, 1, 7)
         forces(nc.gpsimd, pairs[0])
         soften(pairs[2])
         factors(pairs[1])
         forces(nc.gpsimd, pairs[1])
-        strengths([(2, 1), (3, 1)], 4)
+        strengths([(2, 1), (3, 1)], 5)
         z_banks = {(0, c): bank("z_bank0_%d" % c, c) for c in range(2)}
         for t in range(PACK):
             for c in range(2):
@@ -286,9 +291,11 @@ def tile_picked_ljpot_none_po_kernel(
         last = [[(2, 1, cs), (3, 1, cs)] for cs in (first, second)]
         for c in range(2):
             soften(last[c])
-        for c in range(2):
-            factors(last[c])
-        z16 = [weighted(P * c, P, z_banks[0, c], ("soft2_1_1", "soft3_1_1")[c]) for c in range(2)]
+        factors(last[0])
+        z16 = [weighted(0, P, z_banks[0, 0], "soft2_1_0")]
+        factors(last[1])
+        z = quantized(0, P, z16[0], "soft3_1_1")
+        z16.append(weighted(P, P, z_banks[0, 1], "soft2_1_1"))
 
         def stored(queue, start, parts):
             width = sum(part.shape[2] for part in parts)
@@ -299,10 +306,10 @@ def tile_picked_ljpot_none_po_kernel(
                 at = at + part.shape[2]
             queue.dma_start(out=out_rows[:, :, start : start + width], in_=result[:])
 
-        sums = layer(0, P, quantized(0, P, z16[0]), 7)
+        sums = layer(0, P, z, 4)
         stored(nc.sync, 0, [sums])
         late = [rounded(nc.scalar.copy, 0, P, sums)]
-        last_forces = tile("last_forces", [2, 2, HALF], F32, "gain0")
+        last_forces = tile("last_forces", [2, 2, HALF], F32, "soft2_1_0")
         for c in range(2):
             forces(nc.vector, last[c], [last_forces[:, c, i, :] for i in range(2)])
             for t in (2, 3):
@@ -310,7 +317,7 @@ def tile_picked_ljpot_none_po_kernel(
         sums = layer(P, P, quantized(P, P, z16[1], "m3_1_1"), 0)
         stored(nc.sync, P, [sums])
         late.append(rounded(nc.scalar.copy, P, P, sums))
-        pieces = ((256, P, 1), (384, 64, 4), (448, 64, 5))
+        pieces = ((256, P, 1), (384, 64, 5), (448, 64, 6))
         z16 = [weighted(start, width, z_banks[1, (start - HALF) // P]) for start, width, number in pieces[:2]]
         z = [quantized(256, P, z16[0])]
         z16.append(weighted(448, 64, z_banks[1, 1]))

@@ -112,7 +112,7 @@ def tile_picked_ljpot_none_po_kernel(
         w2_codes = deal("w2_codes", w2_raw, U32, 0, 4, "p m t", "w1_raw_plane")
 
         y_window = [tile("y_window%d" % t, [S], F32) for t in range(PACK)]
-        y_own = {(t, h): tile("y_own%d_%d" % (t, h), [HALF], F32) for t in range(PACK) for h in range(2) if (t, h) != (3, 0)}
+        y_own = {(t, 0): tile("y_own%d" % t, [HALF], F32) for t in range(2)}
         halves = [slice(0, HALF), slice(HALF, S)]
         y_banks = [bank("y%d" % n, n) for n in range(6)]
         for t in range(2):
@@ -125,7 +125,6 @@ def tile_picked_ljpot_none_po_kernel(
             nc.scalar.copy(out=y_own[t, 0][:], in_=y_banks[2 * t][:, :HALF])
             (nc.scalar.copy if t else nc.vector.tensor_copy)(out=y_window[t][:, halves[1]], in_=y_banks[2 * t + 1][:, :HALF])
         nc.scalar.copy(out=y_window[2][:], in_=y_banks[4][:])
-        nc.scalar.copy(out=y_own[2, 0][:], in_=y_banks[4][:, :HALF])
         nc.scalar.copy(out=y_window[3][:], in_=y_banks[5][:])
 
         lists = (p1_sb, p2_sb)
@@ -138,25 +137,23 @@ def tile_picked_ljpot_none_po_kernel(
 
         def gather(t, h):
             for k in range(2):
-                nc.vector.tensor_tensor(d[t, h][:, k, :], y_window[t][:].indirect(lists[k][:, 16 * h : 16 * (h + 1)]), y_own[t, h][:], SUBTRACT)
+                partners = y_window[t][:].indirect(lists[k][:, 16 * h : 16 * (h + 1)])
+                if (t, h) in y_own:
+                    nc.vector.tensor_tensor(d[t, h][:, k, :], partners, y_own[t, h][:], SUBTRACT)
+                elif (t, h) == (3, 0):
+                    nc.scalar.activation(out=d[t, h][:, k, :], in_=partners, func=ACT.Copy, scale=-1.0)
+                else:
+                    nc.vector.tensor_scalar(out=d[t, h][:, k, :], in0=partners, scalar1=-1.0, scalar2=0.0, op0=MULT, op1=ADD)
 
         def turn_over(t, h, number):
             d_bank[t, h] = bank("d_bank%d_%d" % (t, h), number)
-            for k in range(2):
-                for c in range(2):
-                    turn(blocks(d_bank[t, h][:])[:, c, k, :], d[t, h][:, k, P * c : P * (c + 1)])
-
-        def fetch(t, h, number, tag=None):
-            fetched = tile("fetched%d_%d" % (t, h), [2, HALF], F32, tag)
-            for k in range(2):
-                nc.scalar.activation(out=fetched[:, k, :], in_=y_window[t][:].indirect(lists[k][:, 16 * h : 16 * (h + 1)]), func=ACT.Copy, scale=-1.0)
-            d_bank[t, h] = bank("d_bank%d_%d" % (t, h), number)
-            for k in range(2):
+            fused = (t, h) in y_own
+            for k in range(0 if fused else 2):
                 for c in range(2):
                     turn(blocks(d_bank[t, h][:])[:, c, k, :], y_window[t][:, HALF * h + P * c : HALF * h + P * (c + 1)], k + c == 0, False)
             for k in range(2):
                 for c in range(2):
-                    turn(blocks(d_bank[t, h][:])[:, c, k, :], fetched[:, k, P * c : P * (c + 1)], False, k + c == 2)
+                    turn(blocks(d_bank[t, h][:])[:, c, k, :], d[t, h][:, k, P * c : P * (c + 1)], fused, fused or k + c == 2)
 
         def strengths(units, number):
             held = bank("q_bank%d_%d" % units[0], number)
@@ -217,12 +214,9 @@ def tile_picked_ljpot_none_po_kernel(
         out_rows = out_0.rearrange("(p t) j -> p t j", t=PACK)
         out_words = words_view(out_1)
 
-        def weighted(start, width, z_bank, tag=None):
-            cols = slice(start % P, start % P + width)
-            z16 = tile("z16_%d" % start, [width, PACK], BF16, tag)
-            sums = z_bank[:].rearrange("p (t j) -> p j t", t=PACK)[:, cols, :]
-            nc.vector.tensor_tensor(z16[:], sums, gain[start // HALF][:].unsqueeze(1).to_broadcast([P, width, PACK]), MULT)
-            return z16
+        def weighted(z16, h, z_bank):
+            sums = z_bank[:].rearrange("p (t j) -> p j t", t=PACK)
+            nc.vector.tensor_tensor(z16, sums, gain[h][:].unsqueeze(1).to_broadcast([P, P, PACK]), MULT)
 
         def quantized(start, width, z16, tag=None):
             z_codes = tile("z_codes%d" % start, [width], I32, tag)
@@ -230,16 +224,17 @@ def tile_picked_ljpot_none_po_kernel(
             nc.vector.quantize_mx(out=z_codes[:].bitcast(FP8X4), scales=z_plane[:], in_=z16[:].rearrange("p j t -> p (j t)"))
             return z_codes, z_plane
 
-        def layer(start, width, z, number):
-            sums = bank("out_bank%d" % start, number)[:, : PACK * width].rearrange("p (t j) -> p t j", t=PACK)
+        def layer(start, z, number):
+            sums = bank("out_bank%d" % start, number)[:].rearrange("p (t j) -> p t j", t=PACK)
             for t in range(PACK):
-                product(sums[:, t, :], w2_codes[t], w2_plane[t], z[0][:], z[1][:])
+                product(sums[:, t, :], w2_codes[t], w2_plane[t], z[0], z[1])
             return sums
 
-        def rounded(engine_copy, start, width, sums):
-            result16 = tile("result16_%d" % start, [width, PACK], BF16)
-            engine_copy(out=result16[:], in_=sums.rearrange("p t j -> p j t"))
-            return start, width, result16
+        def stored(queue, start, sums):
+            result = tile("result%d" % start, [PACK, P], F32)
+            nc.scalar.copy(out=result[:], in_=sums)
+            queue.dma_start(out=out_rows[:, :, start : start + P], in_=result[:])
+            return result
 
         def planes(start, width, result16):
             js = slice(start, start + width)
@@ -250,31 +245,33 @@ def tile_picked_ljpot_none_po_kernel(
             d[t, 0] = tile("d%d_0" % t, [2, HALF], F32)
             gather(t, 0)
             turn_over(t, 0, number)
-        for t in range(PACK):
-            nc.vector.tensor_copy(out=y_own[t, 1][:], in_=y_window[t][:, halves[1]])
         d_second = tile("d_second", [PACK, 2, HALF], F32, "d1_0")
         for t in range(PACK):
             d[t, 1] = d_second[:, t]
             gather(t, 1)
         pairs = [[(0, 0, both), (1, 0, both)], [(2, 0, both), (3, 0, both)], [(0, 1, both), (1, 1, both)]]
-        soften(pairs[0], None, lambda: fetch(3, 0, 1))
+        d[3, 0] = tile("d3_0", [2, HALF], F32)
+        soften(pairs[0], None, lambda: gather(3, 0))
+        turn_over(3, 0, 1)
         turn_over(0, 1, 2)
         turn_over(1, 1, 3)
-        gain = [tile("gain0", [PACK], F32, "y_own3_1"), gn_sb]
-        nc.gpsimd.tensor_copy(out=gain[0][:, 0:3], in_=gn_sb[:, 0:3])
-        nc.gpsimd.tensor_scalar(out=gain[0][:, 3:4], in0=gn_sb[:, 3:4], scalar1=-1.0, scalar2=0.0, op0=MULT, op1=ADD)
         strengths([(0, 0), (1, 0)], 4)
         strengths([(2, 0), (3, 0)], 5)
         soften(pairs[1])
         w2_plane = deal("w2_plane", w2_raw_plane, U8, 0, 4, "p t m")
         for item in pairs[0]:
             factors([item], True)
+        gain = [tile("gain0", [PACK], F32, "y_own0"), tile("gain1", [PACK], F32, "y_own1")]
+        nc.scalar.copy(out=gain[0][:, 0:2], in_=gn_sb[:, 0:2])
+        nc.scalar.activation(out=gain[0][:, 2:4], in_=gn_sb[:, 2:4], func=ACT.Copy, scale=-1.0)
+        nc.scalar.activation(out=gain[1][:], in_=gn_sb[:], func=ACT.Copy, scale=-1.0)
         strengths([(0, 1), (1, 1)], 4)
         turn_over(2, 1, 6)
         turn_over(3, 1, 7)
         forces(nc.gpsimd, pairs[0])
         soften(pairs[2])
-        factors(pairs[1])
+        for item in pairs[1]:
+            factors([item], True)
         forces(nc.gpsimd, pairs[1])
         strengths([(2, 1), (3, 1)], 5)
         z_banks = {(0, c): bank("z_bank0_%d" % c, c) for c in range(2)}
@@ -291,48 +288,36 @@ def tile_picked_ljpot_none_po_kernel(
         last = [[(2, 1, cs), (3, 1, cs)] for cs in (first, second)]
         for c in range(2):
             soften(last[c])
-        factors(last[0])
-        z16 = [weighted(0, P, z_banks[0, 0], "soft2_1_0")]
-        factors(last[1])
-        z = quantized(0, P, z16[0], "soft3_1_1")
-        z16.append(weighted(P, P, z_banks[0, 1], "soft2_1_1"))
-
-        def stored(queue, start, parts):
-            width = sum(part.shape[2] for part in parts)
-            result = tile("result%d" % start, [PACK, width], F32)
-            at = 0
-            for part in parts:
-                nc.scalar.copy(out=result[:, :, at : at + part.shape[2]], in_=part)
-                at = at + part.shape[2]
-            queue.dma_start(out=out_rows[:, :, start : start + width], in_=result[:])
-
-        sums = layer(0, P, z, 4)
-        stored(nc.sync, 0, [sums])
-        late = [rounded(nc.scalar.copy, 0, P, sums)]
-        last_forces = tile("last_forces", [2, 2, HALF], F32, "soft2_1_0")
+        for c in range(2):
+            factors(last[c])
+        z16 = tile("z16_0", [HALF, PACK], BF16, "soft2_1_1")
+        for c in range(2):
+            weighted(z16[:, P * c : P * (c + 1), :], 0, z_banks[0, c])
+        last_forces = tile("last_forces", [2, 2, HALF], F32, "y_own0")
         for c in range(2):
             forces(nc.vector, last[c], [last_forces[:, c, i, :] for i in range(2)])
             for t in (2, 3):
                 turn_back(z_banks[1, c], t, 1, c)
-        sums = layer(P, P, quantized(P, P, z16[1], "m3_1_1"), 0)
-        stored(nc.sync, P, [sums])
-        late.append(rounded(nc.scalar.copy, P, P, sums))
-        pieces = ((256, P, 1), (384, 64, 5), (448, 64, 6))
-        z16 = [weighted(start, width, z_banks[1, (start - HALF) // P]) for start, width, number in pieces[:2]]
-        z = [quantized(256, P, z16[0])]
-        z16.append(weighted(448, 64, z_banks[1, 1]))
-        z = z + [quantized(384, 64, z16[1]), quantized(448, 64, z16[2])]
-        sums = [layer(start, width, made, number) for (start, width, number), made in zip(pieces, z)]
-        late.append(rounded(nc.scalar.copy, 256, P, sums[0]))
-        late.append(rounded(nc.vector.tensor_copy, 384, 64, sums[1]))
-        late.append(rounded(nc.vector.tensor_copy, 448, 64, sums[2]))
-        stored(nc.sync, 256, sums[:1])
-        for piece in late[:2]:
-            planes(*piece)
+        z_first = quantized(0, HALF, z16, "m2_1_1")
+        sums = [layer(P * c, [part[:, P * c : P * (c + 1)] for part in z_first], 4 + c) for c in range(2)]
+        z16 = [tile("z16_%d" % (HALF + P * c), [P, PACK], BF16) for c in range(2)]
+        for c in range(2):
+            weighted(z16[c][:], 1, z_banks[1, c])
+        for c in range(2):
+            sums.append(layer(HALF + P * c, [part[:] for part in quantized(HALF + P * c, P, z16[c])], c))
+        result16 = [tile("result16_%d" % c, [P, PACK], BF16) for c in range(4)]
+        for c in range(2):
+            result = stored(nc.sync, P * c, sums[c])
+            nc.vector.tensor_copy(out=result16[c][:].rearrange("p (c i) t -> p c t i", i=4), in_=result[:].rearrange("p t (c i) -> p c t i", i=4))
+        for c in range(2):
+            planes(P * c, P, result16[c])
         nc.sync.dma_start(out=out_words[:, :HALF], in_=out_codes[:, :HALF])
-        for piece in late[2:]:
-            planes(*piece)
+        nc.scalar.copy(out=result16[2][:], in_=sums[2].rearrange("p t j -> p j t"))
+        nc.vector.tensor_copy(out=result16[3][:], in_=sums[3].rearrange("p t j -> p j t"))
+        stored(nc.sync, HALF, sums[2])
+        for c in range(2, 4):
+            planes(P * c, P, result16[c])
         nc.sync.dma_start(out=out_words[:, HALF:], in_=out_codes[:, HALF:])
-        stored(nc.scalar, 384, sums[1:])
+        stored(nc.scalar, HALF + P, sums[3])
         for quad in range(4):
             (nc.sync if quad < 2 else nc.scalar).dma_start(out=out_2[0, 4 * quad : 4 * quad + 4, :].bitcast(I32), in_=out_plane[32 * quad : 32 * quad + 4, :].bitcast(I32))

@@ -100,7 +100,7 @@ def tile_picked_ljpot_none_po_kernel(
                 out=out, lhsT=codes.bitcast(FP8X4), lhsT_scale=plane, rhs=moving.bitcast(FP8X4), rhs_scale=moving_plane, start=True, stop=True
             )
 
-        x_picked_plane = tile("x_picked_plane", [S], U8, tag="w2_plane")
+        x_picked_plane = tile("x_picked_plane", [S], U8)
         nc.vector.tensor_copy(x_picked_plane[:], x_plane[:].indirect(offs_sb[:]))
         x_codes = tile("x_codes", [S], I32)
         for h in range(2):
@@ -112,7 +112,6 @@ def tile_picked_ljpot_none_po_kernel(
         w2_codes = deal("w2_codes", w2_raw, U32, 0, 4, "p m t", "w1_raw_plane")
 
         y_window = [tile("y_window%d" % t, [S], F32) for t in range(PACK)]
-        y_own = {(t, 0): tile("y_own%d" % t, [HALF], F32) for t in range(2)}
         halves = [slice(0, HALF), slice(HALF, S)]
         y_banks = [bank("y%d" % n, n) for n in range(6)]
         for t in range(2):
@@ -120,204 +119,239 @@ def tile_picked_ljpot_none_po_kernel(
                 product(y_banks[2 * t + h][:, :HALF], w1_codes[t], w1_plane[t], x_codes[:, halves[h]], x_picked_plane[:, halves[h]])
         for t in range(2, PACK):
             product(y_banks[t + 2][:], w1_codes[t], w1_plane[t], x_codes[:], x_picked_plane[:])
+        y_own = [tile("y_own%d" % t, [HALF], F32) for t in range(2)]
         for t in range(2):
             nc.scalar.copy(out=y_window[t][:, halves[0]], in_=y_banks[2 * t][:, :HALF])
-            nc.scalar.copy(out=y_own[t, 0][:], in_=y_banks[2 * t][:, :HALF])
+            nc.scalar.copy(out=y_own[t][:], in_=y_banks[2 * t][:, :HALF])
             (nc.scalar.copy if t else nc.vector.tensor_copy)(out=y_window[t][:, halves[1]], in_=y_banks[2 * t + 1][:, :HALF])
-        nc.scalar.copy(out=y_window[2][:], in_=y_banks[4][:])
-        nc.scalar.copy(out=y_window[3][:], in_=y_banks[5][:])
+        for t in range(2, PACK):
+            nc.scalar.copy(out=y_window[t][:], in_=y_banks[t + 2][:])
 
         lists = (p1_sb, p2_sb)
-        d_bank, q_bank, soft, s, m, force = {}, {}, {}, {}, {}, {}
+        fetched, d_bank, q_bank, d2, denom2, soft, s, m, force, z_bank = {}, {}, {}, {}, {}, {}, {}, {}, {}, {}
+        whole, first, second = slice(0, 2), slice(0, 1), slice(1, 2)
+        PIECE = 2 * P
 
-        def blocks(view):
-            return view.rearrange("j (c k p) -> j c k p", c=2, k=2)
+        units = [[(0, 0), (0, 1)], [(1, 0), (1, 1)]] + [[(t, c), (t + 1, c)] for t, c in ((2, 0), (2, 1), (0, 2), (2, 2), (0, 3), (2, 3))]
 
-        d = {}
+        def span(part):
+            return slice(PIECE * part.start, PIECE * part.stop)
 
-        def gather(t, h):
-            for k in range(2):
-                partners = y_window[t][:].indirect(lists[k][:, 16 * h : 16 * (h + 1)])
-                if (t, h) in y_own:
-                    nc.vector.tensor_tensor(d[t, h][:, k, :], partners, y_own[t, h][:], SUBTRACT)
-                elif (t, h) == (3, 0):
-                    nc.scalar.activation(out=d[t, h][:, k, :], in_=partners, func=ACT.Copy, scale=-1.0)
+        def fetch(engine, t, c, count, held, ks=(0, 1)):
+            for k in ks:
+                partners = y_window[t][:].indirect(lists[k][:, 8 * c : 8 * (c + count)])
+                if engine == "scalar":
+                    nc.scalar.activation(out=held[:, k, :], in_=partners, func=ACT.Copy, scale=-1.0)
+                elif engine == "vector":
+                    nc.vector.tensor_scalar(out=held[:, k, :], in0=partners, scalar1=-1.0, scalar2=0.0, op0=MULT, op1=ADD)
                 else:
-                    nc.vector.tensor_scalar(out=d[t, h][:, k, :], in0=partners, scalar1=-1.0, scalar2=0.0, op0=MULT, op1=ADD)
+                    nc.vector.tensor_tensor(held[:, k, :], partners, y_own[t][:], SUBTRACT)
+            for n in range(count):
+                fetched[t, c + n] = held[:, :, P * n : P * (n + 1)]
 
-        def turn_over(t, h, number):
-            d_bank[t, h] = bank("d_bank%d_%d" % (t, h), number)
-            fused = (t, h) in y_own
-            for k in range(0 if fused else 2):
-                for c in range(2):
-                    turn(blocks(d_bank[t, h][:])[:, c, k, :], y_window[t][:, HALF * h + P * c : HALF * h + P * (c + 1)], k + c == 0, False)
+        def piece(engine, t, c, tag=None):
+            fetch(engine, t, c, 1, tile("fetched%d_%d" % (t, c), [2, P], F32, tag))
+
+        def differences(u, number):
+            d_bank[u] = bank("d_bank%d" % u, number)
+            blocks = d_bank[u][:].rearrange("j (i k p) -> j i k p", i=2, k=2)
+            fused = u < 2
+            for i, (t, c) in enumerate([] if fused else units[u]):
+                for k in range(2):
+                    turn(blocks[:, i, k, :], y_window[t][:, P * c : P * (c + 1)], i + k == 0, False)
             for k in range(2):
-                for c in range(2):
-                    turn(blocks(d_bank[t, h][:])[:, c, k, :], d[t, h][:, k, P * c : P * (c + 1)], fused, fused or k + c == 2)
+                for i in range(2):
+                    turn(blocks[:, i, k, :], fetched[units[u][i]][:, k, :], fused, fused or i + k == 2)
 
-        def strengths(units, number):
-            held = bank("q_bank%d_%d" % units[0], number)
-            for i, (t, h) in enumerate(units):
-                q_bank[t, h] = held[:, HALF * i : HALF * (i + 1)].rearrange("j (c p) -> j c p", c=2)
-                for c in range(2):
-                    turn(q_bank[t, h][:, c, :], q_sb[h][:, t, P * c : P * (c + 1)])
+        def strengths(u, number):
+            held = bank("q_bank%d" % u, number)
+            for n, (t, c) in enumerate(units[u] + units[u + 1]):
+                q_bank[t, c] = held[:, P * n : P * (n + 1)]
+                turn(q_bank[t, c], q_sb[c // 2][:, t, P * (c % 2) : P * (c % 2 + 1)])
 
-        def label(name, t, h, cs):
-            return "%s%d_%d_%d" % (name, t, h, cs.start)
+        def square(u, parts=(whole,)):
+            d2[u] = tile("d2_%d" % u, [S], F32)
+            for part in parts:
+                nc.scalar.activation(out=d2[u][:, span(part)], in_=d_bank[u][:, span(part)], func=ACT.Square)
 
-        def span(cs):
-            return slice(HALF * cs.start, HALF * cs.stop)
+        def denominator(u, parts=(whole,)):
+            denom2[u] = tile("denom2_%d" % u, [S], F32)
+            for part in parts:
+                nc.scalar.activation(out=denom2[u][:, span(part)], in_=d2[u][:, span(part)], func=ACT.Square, bias=1.0)
 
-        def fresh(name, items, tags=None):
-            return [tile(label(name, t, h, cs), [HALF * (cs.stop - cs.start)], F32, tag) for (t, h, cs), tag in zip(items, tags or [None] * len(items))]
+        def root(u, parts=(whole,)):
+            soft[u] = tile("soft%d" % u, [S], F32)
+            for part in parts:
+                nc.scalar.activation(out=soft[u][:, span(part)], in_=denom2[u][:, span(part)], func=ACT.Abs_reciprocal_sqrt)
 
-        def soften(items, tags=None, between=None):
-            d2, denom2 = fresh("d2_", items, tags), fresh("denom2_", items)
-            for item, made in zip(items, fresh("soft", items)):
-                soft[item[0], item[1], item[2].start] = made
-            for i, (t, h, cs) in enumerate(items):
-                nc.scalar.activation(out=d2[i][:], in_=d_bank[t, h][:, span(cs)], func=ACT.Square)
-                if between and i == 0:
-                    between()
-            for i, (t, h, cs) in enumerate(items):
-                nc.scalar.activation(out=denom2[i][:], in_=d2[i][:], func=ACT.Square, bias=1.0)
-            for i, (t, h, cs) in enumerate(items):
-                nc.scalar.activation(out=soft[t, h, cs.start][:], in_=denom2[i][:], func=ACT.Abs_reciprocal_sqrt)
+        def factors(u):
+            s[u], m[u] = tile("s%d" % u, [S], F32), tile("m%d" % u, [S], F32)
+            for i, part in enumerate((first, second)):
+                paired = lambda view: view[:, span(part)].rearrange("j (k p) -> j k p", k=2)
+                nc.vector.tensor_tensor(paired(s[u]), paired(soft[u]), q_bank[units[u][i]].unsqueeze(1).to_broadcast([P, 2, P]), MULT)
+            for part in (first, second):
+                nc.vector.scalar_tensor_tensor(m[u][:, span(part)], s[u][:, span(part)], 1.0, d_bank[u][:, span(part)], SUBTRACT, MULT)
 
-        def factors(items, split=False):
-            for item, made, other in zip(items, fresh("s", items), fresh("m", items)):
-                s[item[0], item[1], item[2].start] = made
-                m[item[0], item[1], item[2].start] = other
-            parts = [(t, h, cs, part) for t, h, cs in items for part in ([slice(c, c + 1) for c in range(cs.start, cs.stop)] if split else [cs])]
-            for t, h, cs, part in parts:
-                n = part.stop - part.start
-                inside = span(slice(part.start - cs.start, part.stop - cs.start))
-                shaped = lambda view: view[:, inside].rearrange("j (c k p) -> j c k p", c=n, k=2)
-                nc.vector.tensor_tensor(shaped(s[t, h, cs.start]), shaped(soft[t, h, cs.start]), q_bank[t, h][:, part, :].unsqueeze(2).to_broadcast([P, n, 2, P]), MULT)
-            for t, h, cs, part in parts:
-                inside = span(slice(part.start - cs.start, part.stop - cs.start))
-                nc.vector.scalar_tensor_tensor(m[t, h, cs.start][:, inside], s[t, h, cs.start][:, inside], 1.0, d_bank[t, h][:, span(part)], SUBTRACT, MULT)
+        def forces(engine, u, part=whole):
+            if u not in force:
+                force[u] = tile("force%d" % u, [S], F32)
+            engine.tensor_tensor(force[u][:, span(part)], m[u][:, span(part)], s[u][:, span(part)], MULT)
 
-        def forces(engine, items, tiles=None):
-            tiles = tiles or [made[:] for made in fresh("force", items)]
-            for (t, h, cs), made in zip(items, tiles):
-                engine.tensor_tensor(made, m[t, h, cs.start][:], s[t, h, cs.start][:], MULT)
-                for c in range(cs.start, cs.stop):
-                    force[t, h, c] = made[:, HALF * (c - cs.start) : HALF * (c - cs.start + 1)]
-
-        def turn_back(z_bank, t, h, c):
-            for k in range(2):
-                turn(z_bank[:, P * t : P * (t + 1)], force[t, h, c][:, P * k : P * (k + 1)], k == 0, k == 1)
+        def turn_back(u):
+            for i, (t, c) in enumerate(units[u]):
+                for k in range(2):
+                    turn(z_bank[c][:, P * t : P * (t + 1)], force[u][:, PIECE * i + P * k : PIECE * i + P * (k + 1)], k == 0, k == 1)
 
         out_plane = tile("out_plane", [S], U8)
         out_codes = tile("out_codes", [S], I32)
         out_rows = out_0.rearrange("(p t) j -> p t j", t=PACK)
         out_words = words_view(out_1)
+        z16, z, sums, result, result16 = {}, {}, {}, {}, {}
 
-        def weighted(z16, h, z_bank):
-            sums = z_bank[:].rearrange("p (t j) -> p j t", t=PACK)
-            nc.vector.tensor_tensor(z16, sums, gain[h][:].unsqueeze(1).to_broadcast([P, P, PACK]), MULT)
+        def weighted(c, tag=None):
+            z16[c] = tile("z16_%d" % c, [P, PACK], BF16, tag)
+            turned = z_bank[c][:].rearrange("p (t j) -> p j t", t=PACK)
+            factor = gain if c < 2 else gn_sb
+            nc.vector.scalar_tensor_tensor(z16[c][:], turned, -1.0, factor[:].unsqueeze(1).to_broadcast([P, P, PACK]), MULT, MULT)
 
-        def quantized(start, width, z16, tag=None):
-            z_codes = tile("z_codes%d" % start, [width], I32, tag)
-            z_plane = tile("z_plane%d" % start, [width], U8)
-            nc.vector.quantize_mx(out=z_codes[:].bitcast(FP8X4), scales=z_plane[:], in_=z16[:].rearrange("p j t -> p (j t)"))
-            return z_codes, z_plane
+        def quantized(c, tag=None):
+            z[c] = (tile("z_codes%d" % c, [P], I32, tag), tile("z_plane%d" % c, [P], U8))
+            nc.vector.quantize_mx(out=z[c][0][:].bitcast(FP8X4), scales=z[c][1][:], in_=z16[c][:].rearrange("p j t -> p (j t)"))
 
-        def layer(start, z, number):
-            sums = bank("out_bank%d" % start, number)[:].rearrange("p (t j) -> p t j", t=PACK)
+        def layer(c, numbers):
+            count = PACK // len(numbers)
+            sums[c] = [bank("out_bank%d_%d" % (c, n), n)[:, : count * P].rearrange("p (t j) -> p t j", t=count) for n in numbers]
             for t in range(PACK):
-                product(sums[:, t, :], w2_codes[t], w2_plane[t], z[0], z[1])
-            return sums
+                product(sums[c][t // count][:, t % count, :], w2_codes[t], w2_plane[t], z[c][0][:], z[c][1][:])
 
-        def stored(queue, start, sums):
-            result = tile("result%d" % start, [PACK, P], F32)
-            nc.scalar.copy(out=result[:], in_=sums)
-            queue.dma_start(out=out_rows[:, :, start : start + P], in_=result[:])
-            return result
+        def stored(queue, c, tag=None):
+            result[c] = tile("result%d" % c, [PACK, P], F32, tag)
+            count = PACK // len(sums[c])
+            for n, part in enumerate(sums[c]):
+                nc.scalar.copy(out=result[c][:, count * n : count * (n + 1), :], in_=part)
+            queue.dma_start(out=out_rows[:, :, P * c : P * (c + 1)], in_=result[c][:])
 
-        def planes(start, width, result16):
-            js = slice(start, start + width)
-            nc.vector.quantize_mx(out=out_codes[:, js].bitcast(FP8X4), scales=out_plane[:, js], in_=result16[:].rearrange("p j t -> p (j t)"))
+        def rounded(c, engine, tag=None):
+            result16[c] = tile("result16_%d" % c, [P, PACK], BF16, tag)
+            if engine == "scalar":
+                nc.scalar.copy(out=result16[c][:], in_=sums[c][0].rearrange("p t j -> p j t"))
+            else:
+                nc.vector.tensor_copy(out=result16[c][:].rearrange("p (c i) t -> p c t i", i=4), in_=result[c][:].rearrange("p t (c i) -> p c t i", i=4))
 
-        both, first, second = slice(0, 2), slice(0, 1), slice(1, 2)
-        for t, number in ((0, 6), (1, 7), (2, 0)):
-            d[t, 0] = tile("d%d_0" % t, [2, HALF], F32)
-            gather(t, 0)
-            turn_over(t, 0, number)
-        d_second = tile("d_second", [PACK, 2, HALF], F32, "d1_0")
-        for t in range(PACK):
-            d[t, 1] = d_second[:, t]
-            gather(t, 1)
-        pairs = [[(0, 0, both), (1, 0, both)], [(2, 0, both), (3, 0, both)], [(0, 1, both), (1, 1, both)]]
-        d[3, 0] = tile("d3_0", [2, HALF], F32)
-        soften(pairs[0], None, lambda: gather(3, 0))
-        turn_over(3, 0, 1)
-        turn_over(0, 1, 2)
-        turn_over(1, 1, 3)
-        strengths([(0, 0), (1, 0)], 4)
-        strengths([(2, 0), (3, 0)], 5)
-        soften(pairs[1])
-        w2_plane = deal("w2_plane", w2_raw_plane, U8, 0, 4, "p t m")
-        for item in pairs[0]:
-            factors([item], True)
-        gain = [tile("gain0", [PACK], F32, "y_own0"), tile("gain1", [PACK], F32, "y_own1")]
-        nc.scalar.copy(out=gain[0][:, 0:2], in_=gn_sb[:, 0:2])
-        nc.scalar.activation(out=gain[0][:, 2:4], in_=gn_sb[:, 2:4], func=ACT.Copy, scale=-1.0)
-        nc.scalar.activation(out=gain[1][:], in_=gn_sb[:], func=ACT.Copy, scale=-1.0)
-        strengths([(0, 1), (1, 1)], 4)
-        turn_over(2, 1, 6)
-        turn_over(3, 1, 7)
-        forces(nc.gpsimd, pairs[0])
-        soften(pairs[2])
-        for item in pairs[1]:
-            factors([item], True)
-        forces(nc.gpsimd, pairs[1])
-        strengths([(2, 1), (3, 1)], 5)
-        z_banks = {(0, c): bank("z_bank0_%d" % c, c) for c in range(2)}
-        for t in range(PACK):
-            for c in range(2):
-                turn_back(z_banks[0, c], t, 0, c)
-        factors(pairs[2])
-        forces(nc.gpsimd, pairs[2])
-        z_banks[1, 0] = bank("z_bank1_0", 2)
-        z_banks[1, 1] = bank("z_bank1_1", 3)
+        def planes(c):
+            js = slice(P * c, P * (c + 1))
+            nc.vector.quantize_mx(out=out_codes[:, js].bitcast(FP8X4), scales=out_plane[:, js], in_=result16[c][:].rearrange("p j t -> p (j t)"))
+
+        first_half = [tile("fetched%d" % t, [2, HALF], F32) for t in range(2)]
         for t in range(2):
-            for c in range(2):
-                turn_back(z_banks[1, c], t, 1, c)
-        last = [[(2, 1, cs), (3, 1, cs)] for cs in (first, second)]
+            fetch("fused", t, 0, 2, first_half[t])
         for c in range(2):
-            soften(last[c])
-        for c in range(2):
-            factors(last[c])
-        z16 = tile("z16_0", [HALF, PACK], BF16, "soft2_1_1")
-        for c in range(2):
-            weighted(z16[:, P * c : P * (c + 1), :], 0, z_banks[0, c])
-        last_forces = tile("last_forces", [2, 2, HALF], F32, "y_own0")
-        for c in range(2):
-            forces(nc.vector, last[c], [last_forces[:, c, i, :] for i in range(2)])
-            for t in (2, 3):
-                turn_back(z_banks[1, c], t, 1, c)
-        z_first = quantized(0, HALF, z16, "m2_1_1")
-        sums = [layer(P * c, [part[:, P * c : P * (c + 1)] for part in z_first], 4 + c) for c in range(2)]
-        z16 = [tile("z16_%d" % (HALF + P * c), [P, PACK], BF16) for c in range(2)]
-        for c in range(2):
-            weighted(z16[c][:], 1, z_banks[1, c])
-        for c in range(2):
-            sums.append(layer(HALF + P * c, [part[:] for part in quantized(HALF + P * c, P, z16[c])], c))
-        result16 = [tile("result16_%d" % c, [P, PACK], BF16) for c in range(4)]
-        for c in range(2):
-            result = stored(nc.sync, P * c, sums[c])
-            nc.vector.tensor_copy(out=result16[c][:].rearrange("p (c i) t -> p c t i", i=4), in_=result[:].rearrange("p t (c i) -> p c t i", i=4))
-        for c in range(2):
-            planes(P * c, P, result16[c])
-        nc.sync.dma_start(out=out_words[:, :HALF], in_=out_codes[:, :HALF])
-        nc.scalar.copy(out=result16[2][:], in_=sums[2].rearrange("p t j -> p j t"))
-        nc.vector.tensor_copy(out=result16[3][:], in_=sums[3].rearrange("p t j -> p j t"))
-        stored(nc.sync, HALF, sums[2])
+            piece("vector", 3, c)
+        differences(0, 6)
+        differences(1, 7)
+        early = tile("fetched_early", [3, 2, P], F32, "fetched1")
+        for t in range(3):
+            fetch("vector", t, 2, 1, early[:, t])
+        gain = tile("gain", [PACK], F32, "y_own1")
+        nc.gpsimd.tensor_scalar(out=gain[:, 0:2], in0=gn_sb[:, 0:2], scalar1=-1.0, scalar2=0.0, op0=MULT, op1=ADD)
+        nc.gpsimd.tensor_scalar(out=gain[:, 2:4], in0=gn_sb[:, 2:4], scalar1=1.0, scalar2=0.0, op0=MULT, op1=ADD)
+        piece("scalar", 2, 0)
+        square(0)
+        piece("scalar", 2, 1)
+        strengths(0, 2)
+        differences(2, 0)
+        differences(3, 1)
+        strengths(2, 4)
+        differences(4, 3)
+        denominator(0)
+        square(1)
+        root(0)
+        factors(0)
+        piece("vector", 0, 3, "soft0")
+        forces(nc.gpsimd, 0)
+        denominator(1)
+        square(2)
+        root(1)
+        factors(1)
+        piece("vector", 1, 3, "soft1")
+        forces(nc.gpsimd, 1)
+        denominator(2)
+        square(3)
+        root(2)
+        piece("scalar", 3, 2, "d2_2")
+        differences(5, 5)
+        factors(2)
+        w2_plane = deal("w2_plane", w2_raw_plane, U8, 0, 4, "p t m", "soft2")
+        piece("vector", 2, 3, "denom2_2")
+        forces(nc.gpsimd, 2)
+        strengths(4, 2)
+        differences(6, 6)
+        z_bank[0] = bank("z_bank0", 7)
+        z_bank[1] = bank("z_bank1", 0)
+        turn_back(0)
+        turn_back(1)
+        turn_back(2)
+        denominator(3)
+        square(4)
+        root(3)
+        factors(3)
+        piece("vector", 3, 3, "soft3")
+        forces(nc.gpsimd, 3)
+        denominator(4)
+        square(5)
+        root(4)
+        factors(4)
+        weighted(0, "soft4")
+        forces(nc.gpsimd, 4)
+        differences(7, 1)
+        turn_back(3)
+        strengths(6, 4)
+        denominator(5)
+        square(6)
+        root(5)
+        factors(5)
+        quantized(0, "soft5")
+        weighted(1, "denom2_5")
+        forces(nc.gpsimd, 5)
+        layer(0, [3])
+        z_bank[2] = bank("z_bank2", 7)
+        turn_back(4)
+        turn_back(5)
+        denominator(6)
+        square(7)
+        root(6)
+        factors(6)
+        quantized(1, "soft6")
+        layer(1, [2])
+        forces(nc.gpsimd, 6, second)
+        denominator(7, (first, second))
+        root(7, (first, second))
+        factors(7)
+        forces(nc.vector, 6, first)
+        forces(nc.vector, 7, first)
+        forces(nc.vector, 7, second)
+        z_bank[3] = bank("z_bank3", 5)
+        turn_back(6)
+        turn_back(7)
+        weighted(2, "soft7")
+        stored(nc.sync, 0, "d2_7")
+        stored(nc.sync, 1)
+        rounded(0, "scalar", "denom2_7")
+        planes(0)
+        quantized(2)
+        rounded(1, "scalar", "soft7")
+        layer(2, [0])
+        weighted(3, "denom2_7")
+        quantized(3)
+        planes(1)
+        layer(3, [6, 4])
+        stored(nc.sync, 2)
+        stored(nc.scalar, 3)
         for c in range(2, 4):
-            planes(P * c, P, result16[c])
-        nc.sync.dma_start(out=out_words[:, HALF:], in_=out_codes[:, HALF:])
-        stored(nc.scalar, HALF + P, sums[3])
+            rounded(c, "vector")
+        planes(2)
+        nc.sync.dma_start(out=out_words[:, : 3 * P], in_=out_codes[:, : 3 * P])
+        planes(3)
+        nc.sync.dma_start(out=out_words[:, 3 * P :], in_=out_codes[:, 3 * P :])
         for quad in range(4):
             (nc.sync if quad < 2 else nc.scalar).dma_start(out=out_2[0, 4 * quad : 4 * quad + 4, :].bitcast(I32), in_=out_plane[32 * quad : 32 * quad + 4, :].bitcast(I32))

@@ -59,7 +59,7 @@ def tile_picked_ljpot_none_po_kernel(
         w2_raw_plane = tile("w2_raw_plane", [S], U8)
         gn_sb = tile("gn_sb", [PACK], F32)
         q_rows = q.rearrange("(p t) j -> p t j", t=PACK)
-        q_sb = [tile("q%d" % h, [PACK, HALF], F32) for h in range(2)]
+        q_sb = {(h, t): tile("q%d_%d" % (h, t), [2, HALF], F32) for h in range(2) for t in (0, 2)}
 
         x_rows = tile("x_rows", [T // 4], I32)
         for r in range(4):
@@ -72,19 +72,23 @@ def tile_picked_ljpot_none_po_kernel(
         nc.sync.dma_start(out=x_table[:], in_=words_view(x_words))
         load_plane(nc.sync, w1_raw_plane, w1_scales)
         nc.sync.dma_start(out=w1_raw[:], in_=words_view(w1_words))
-        nc.sync.dma_start(out=w2_raw[:], in_=words_view(w2_words))
+        nc.sync.dma_start(out=q_sb[0, 0][:], in_=q_rows[:, 0:2, :HALF])
         nc.sync.dma_start(p1_sb[:], p1)
         nc.sync.dma_start(p2_sb[:], p2)
-        load_plane(nc.sync, w2_raw_plane, w2_scales)
+        nc.sync.dma_start(out=w2_raw[:], in_=words_view(w2_words))
+        for h, t in ((0, 2), (1, 0), (1, 2)):
+            nc.sync.dma_start(out=q_sb[h, t][:], in_=q_rows[:, t : t + 2, HALF * h : HALF * (h + 1)])
         nc.sync.dma_start(out=gn_sb[:], in_=gn.rearrange("(p t) o -> p (t o)", t=PACK))
-        for h in range(2):
-            nc.sync.dma_start(out=q_sb[h][:], in_=q_rows[:, :, HALF * h : HALF * (h + 1)])
+        load_plane(nc.sync, w2_raw_plane, w2_scales)
 
         warm = tile("warm", [2], F32)
         nc.gpsimd.memset(warm[:, 0:1], 1.0)
         nc.scalar.activation(out=warm[:, 1:2], in_=warm[:, 0:1], func=ACT.Abs_reciprocal_sqrt)
         identity = tile("identity", [P], F32)
         make_identity(nc, identity[:])
+        signs = tile("signs", [PACK], F32)
+        nc.gpsimd.memset(signs[:, :3], -1.0)
+        nc.gpsimd.memset(signs[:, 3:], 1.0)
 
         def deal(name, raw, dtype, first, count, order, tag=None):
             dealt = tile(name, [count * P], I32 if dtype == U32 else U8, tag)
@@ -124,8 +128,13 @@ def tile_picked_ljpot_none_po_kernel(
             nc.scalar.copy(out=y_window[t][:, halves[0]], in_=y_banks[2 * t][:, :HALF])
             nc.scalar.copy(out=y_own[t][:], in_=y_banks[2 * t][:, :HALF])
             (nc.scalar.copy if t else nc.vector.tensor_copy)(out=y_window[t][:, halves[1]], in_=y_banks[2 * t + 1][:, :HALF])
-        for t in range(2, PACK):
-            nc.scalar.copy(out=y_window[t][:], in_=y_banks[t + 2][:])
+        y_own.append(tile("y_own2", [3 * P], F32))
+        nc.scalar.copy(out=y_window[2][:], in_=y_banks[4][:])
+        nc.scalar.copy(out=y_own[2][:], in_=y_banks[4][:, : 3 * P])
+        third = tile("y_third", [2, P], F32, "x_codes")
+        for t in range(2):
+            nc.scalar.copy(out=third[:, t, :], in_=y_banks[2 * t + 1][:, :P])
+        nc.scalar.copy(out=y_window[3][:], in_=y_banks[5][:])
 
         lists = (p1_sb, p2_sb)
         fetched, d_bank, q_bank, d2, denom2, soft, s, m, force, z_bank = {}, {}, {}, {}, {}, {}, {}, {}, {}, {}
@@ -134,10 +143,12 @@ def tile_picked_ljpot_none_po_kernel(
 
         units = [[(0, 0), (0, 1)], [(1, 0), (1, 1)]] + [[(t, c), (t + 1, c)] for t, c in ((2, 0), (2, 1), (0, 2), (2, 2), (0, 3), (2, 3))]
 
+        fused = set()
+
         def span(part):
             return slice(PIECE * part.start, PIECE * part.stop)
 
-        def fetch(engine, t, c, count, held, ks=(0, 1)):
+        def fetch(engine, t, c, count, held, ks=(0, 1), own=None):
             for k in ks:
                 partners = y_window[t][:].indirect(lists[k][:, 8 * c : 8 * (c + count)])
                 if engine == "scalar":
@@ -145,29 +156,33 @@ def tile_picked_ljpot_none_po_kernel(
                 elif engine == "vector":
                     nc.vector.tensor_scalar(out=held[:, k, :], in0=partners, scalar1=-1.0, scalar2=0.0, op0=MULT, op1=ADD)
                 else:
-                    nc.vector.tensor_tensor(held[:, k, :], partners, y_own[t][:], SUBTRACT)
+                    nc.vector.tensor_tensor(held[:, k, :], partners, own, SUBTRACT)
+                    for n in range(count):
+                        fused.add((t, c + n))
             for n in range(count):
                 fetched[t, c + n] = held[:, :, P * n : P * (n + 1)]
 
-        def piece(engine, t, c, tag=None):
-            fetch(engine, t, c, 1, tile("fetched%d_%d" % (t, c), [2, P], F32, tag))
+        def piece(engine, t, c, tag=None, ks=(0, 1)):
+            held = fetched[t, c] if (t, c) in fetched else tile("fetched%d_%d" % (t, c), [2, P], F32, tag)
+            fetch(engine, t, c, 1, held, ks)
 
         def differences(u, number):
             d_bank[u] = bank("d_bank%d" % u, number)
             blocks = d_bank[u][:].rearrange("j (i k p) -> j i k p", i=2, k=2)
-            fused = u < 2
-            for i, (t, c) in enumerate([] if fused else units[u]):
-                for k in range(2):
-                    turn(blocks[:, i, k, :], y_window[t][:, P * c : P * (c + 1)], i + k == 0, False)
-            for k in range(2):
-                for i in range(2):
-                    turn(blocks[:, i, k, :], fetched[units[u][i]][:, k, :], fused, fused or i + k == 2)
+            steps = []
+            for i, k in ((0, 0), (1, 0), (0, 1), (1, 1)) if u < 2 else ((0, 0), (0, 1), (1, 0), (1, 1)):
+                t, c = units[u][i]
+                steps.append((blocks[:, i, k, :], fetched[t, c][:, k, :]))
+                if (t, c) not in fused:
+                    steps.append((blocks[:, i, k, :], y_window[t][:, P * c : P * (c + 1)]))
+            for n, (out, block) in enumerate(steps):
+                turn(out, block, n == 0, n == len(steps) - 1)
 
         def strengths(u, number):
             held = bank("q_bank%d" % u, number)
+            q_bank[u], q_bank[u + 1] = held[:, :HALF], held[:, HALF:]
             for n, (t, c) in enumerate(units[u] + units[u + 1]):
-                q_bank[t, c] = held[:, P * n : P * (n + 1)]
-                turn(q_bank[t, c], q_sb[c // 2][:, t, P * (c % 2) : P * (c % 2 + 1)])
+                turn(held[:, P * n : P * (n + 1)], q_sb[c // 2, t - t % 2][:, t % 2, P * (c % 2) : P * (c % 2 + 1)])
 
         def square(u, parts=(whole,)):
             d2[u] = tile("d2_%d" % u, [S], F32)
@@ -184,12 +199,16 @@ def tile_picked_ljpot_none_po_kernel(
             for part in parts:
                 nc.scalar.activation(out=soft[u][:, span(part)], in_=denom2[u][:, span(part)], func=ACT.Abs_reciprocal_sqrt)
 
-        def factors(u):
+        def factors(u, between=None):
             s[u], m[u] = tile("s%d" % u, [S], F32), tile("m%d" % u, [S], F32)
-            for i, part in enumerate((first, second)):
-                paired = lambda view: view[:, span(part)].rearrange("j (k p) -> j k p", k=2)
-                nc.vector.tensor_tensor(paired(s[u]), paired(soft[u]), q_bank[units[u][i]].unsqueeze(1).to_broadcast([P, 2, P]), MULT)
-            for part in (first, second):
+            strength = q_bank[u].rearrange("j (i p) -> j i p", i=2).unsqueeze(2).to_broadcast([P, 2, 2, P])
+            paired = lambda view: view[:].rearrange("j (i k p) -> j i k p", i=2, k=2)
+            parts = (whole,) if between else (first, second)
+            for part in parts:
+                nc.vector.tensor_tensor(paired(s[u])[:, part], paired(soft[u])[:, part], strength[:, part], MULT)
+            if between:
+                between()
+            for part in parts:
                 nc.vector.scalar_tensor_tensor(m[u][:, span(part)], s[u][:, span(part)], 1.0, d_bank[u][:, span(part)], SUBTRACT, MULT)
 
         def forces(engine, u, part=whole):
@@ -197,8 +216,9 @@ def tile_picked_ljpot_none_po_kernel(
                 force[u] = tile("force%d" % u, [S], F32)
             engine.tensor_tensor(force[u][:, span(part)], m[u][:, span(part)], s[u][:, span(part)], MULT)
 
-        def turn_back(u):
-            for i, (t, c) in enumerate(units[u]):
+        def turn_back(u, order=(0, 1)):
+            for i in order:
+                t, c = units[u][i]
                 for k in range(2):
                     turn(z_bank[c][:, P * t : P * (t + 1)], force[u][:, PIECE * i + P * k : PIECE * i + P * (k + 1)], k == 0, k == 1)
 
@@ -211,8 +231,8 @@ def tile_picked_ljpot_none_po_kernel(
         def weighted(c, tag=None):
             z16[c] = tile("z16_%d" % c, [P, PACK], BF16, tag)
             turned = z_bank[c][:].rearrange("p (t j) -> p j t", t=PACK)
-            factor = gain if c < 2 else gn_sb
-            nc.vector.scalar_tensor_tensor(z16[c][:], turned, -1.0, factor[:].unsqueeze(1).to_broadcast([P, P, PACK]), MULT, MULT)
+            factor = gain[:] if c < 3 else gn_sb[:]
+            nc.vector.scalar_tensor_tensor(z16[c][:], turned, -1.0, factor.unsqueeze(1).to_broadcast([P, P, PACK]), MULT, MULT)
 
         def quantized(c, tag=None):
             z[c] = (tile("z_codes%d" % c, [P], I32, tag), tile("z_plane%d" % c, [P], U8))
@@ -244,30 +264,29 @@ def tile_picked_ljpot_none_po_kernel(
 
         first_half = [tile("fetched%d" % t, [2, HALF], F32) for t in range(2)]
         for t in range(2):
-            fetch("fused", t, 0, 2, first_half[t])
-        for c in range(2):
-            piece("vector", 3, c)
+            fetch("fused", t, 0, 2, first_half[t], own=y_own[t][:])
         differences(0, 6)
         differences(1, 7)
-        early = tile("fetched_early", [3, 2, P], F32, "fetched1")
-        for t in range(3):
-            fetch("vector", t, 2, 1, early[:, t])
-        gain = tile("gain", [PACK], F32, "y_own1")
-        nc.gpsimd.tensor_scalar(out=gain[:, 0:2], in0=gn_sb[:, 0:2], scalar1=-1.0, scalar2=0.0, op0=MULT, op1=ADD)
-        nc.gpsimd.tensor_scalar(out=gain[:, 2:4], in0=gn_sb[:, 2:4], scalar1=1.0, scalar2=0.0, op0=MULT, op1=ADD)
-        piece("scalar", 2, 0)
+        fetch("fused", 2, 0, 1, tile("fetched2_0", [2, P], F32), own=y_own[2][:, :P])
+        fetch("fused", 2, 1, 2, tile("fetched2_1", [2, HALF], F32), own=y_own[2][:, P:])
+        for t in range(2):
+            fetch("fused", t, 2, 1, tile("fetched%d_2" % t, [2, P], F32), own=third[:, t, :])
         square(0)
-        piece("scalar", 2, 1)
-        strengths(0, 2)
+        for c in range(2):
+            piece("scalar", 3, c)
+        strengths(0, 4)
         differences(2, 0)
-        differences(3, 1)
-        strengths(2, 4)
-        differences(4, 3)
         denominator(0)
+        piece("vector", 3, 2, "d2_0")
         square(1)
         root(0)
+        differences(3, 1)
+        differences(4, 3)
         factors(0)
         piece("vector", 0, 3, "soft0")
+        strengths(2, 6)
+        gain = tile("gain", [PACK], F32, "denom2_0")
+        nc.gpsimd.tensor_tensor(gain[:], gn_sb[:], signs[:], MULT)
         forces(nc.gpsimd, 0)
         denominator(1)
         square(2)
@@ -278,34 +297,35 @@ def tile_picked_ljpot_none_po_kernel(
         denominator(2)
         square(3)
         root(2)
-        piece("scalar", 3, 2, "d2_2")
         differences(5, 5)
         factors(2)
         w2_plane = deal("w2_plane", w2_raw_plane, U8, 0, 4, "p t m", "soft2")
         piece("vector", 2, 3, "denom2_2")
         forces(nc.gpsimd, 2)
-        strengths(4, 2)
-        differences(6, 6)
+        strengths(4, 4)
+        differences(6, 2)
         z_bank[0] = bank("z_bank0", 7)
-        z_bank[1] = bank("z_bank1", 0)
-        turn_back(0)
-        turn_back(1)
+        turn_back(0, (0,))
+        turn_back(1, (0,))
         turn_back(2)
         denominator(3)
         square(4)
         root(3)
         factors(3)
-        piece("vector", 3, 3, "soft3")
         forces(nc.gpsimd, 3)
         denominator(4)
         square(5)
         root(4)
+        piece("scalar", 3, 3, "d2_4")
         factors(4)
         weighted(0, "soft4")
         forces(nc.gpsimd, 4)
-        differences(7, 1)
+        differences(7, 0)
+        z_bank[1] = bank("z_bank1", 1)
+        turn_back(0, (1,))
+        turn_back(1, (1,))
         turn_back(3)
-        strengths(6, 4)
+        strengths(6, 6)
         denominator(5)
         square(6)
         root(5)
@@ -322,7 +342,7 @@ def tile_picked_ljpot_none_po_kernel(
         root(6)
         factors(6)
         quantized(1, "soft6")
-        layer(1, [2])
+        layer(1, [4])
         forces(nc.gpsimd, 6, second)
         denominator(7, (first, second))
         root(7, (first, second))
@@ -331,7 +351,7 @@ def tile_picked_ljpot_none_po_kernel(
         forces(nc.vector, 7, first)
         forces(nc.vector, 7, second)
         z_bank[3] = bank("z_bank3", 5)
-        turn_back(6)
+        turn_back(6, (1, 0))
         turn_back(7)
         weighted(2, "soft7")
         stored(nc.sync, 0, "d2_7")
@@ -340,11 +360,11 @@ def tile_picked_ljpot_none_po_kernel(
         planes(0)
         quantized(2)
         rounded(1, "scalar", "soft7")
-        layer(2, [0])
+        layer(2, [1])
         weighted(3, "denom2_7")
         quantized(3)
         planes(1)
-        layer(3, [6, 4])
+        layer(3, [2, 6])
         stored(nc.sync, 2)
         stored(nc.scalar, 3)
         for c in range(2, 4):

@@ -63,7 +63,7 @@ def tile_picked_ljpot_none_po_kernel(
 
         x_rows = tile("x_rows", [T // 4], I32)
         for r in range(4):
-            nc.sync.dma_start(out=x_rows[r:P:32, :], in_=x_scales[0].bitcast(I32)[r:16:4, :])
+            (nc.scalar if r % 2 else nc.sync).dma_start(out=x_rows[r:P:32, :], in_=x_scales[0].bitcast(I32)[r:16:4, :])
         nc.vector.memset(x_plane[:].bitcast(I32), 0)
         for quad in range(4):
             rows = slice(32 * quad, 32 * quad + 4)
@@ -90,10 +90,10 @@ def tile_picked_ljpot_none_po_kernel(
         nc.gpsimd.memset(signs[:, :3], -1.0)
         nc.gpsimd.memset(signs[:, 3:], 1.0)
 
-        def deal(name, raw, dtype, first, count, order, tag=None):
+        def deal(name, raw, dtype, first, count, order, tag=None, engine=nc.vector):
             dealt = tile(name, [count * P], I32 if dtype == U32 else U8, tag)
             source = raw[:].bitcast(dtype).rearrange("p (m t) -> p m t", t=PACK)[:, :, first : first + count]
-            nc.vector.tensor_copy(out=dealt[:].bitcast(dtype).rearrange("p (t m) -> " + order, t=count), in_=source.rearrange("p m t -> " + order))
+            engine.tensor_copy(out=dealt[:].bitcast(dtype).rearrange("p (t m) -> " + order, t=count), in_=source.rearrange("p m t -> " + order))
             return [dealt[:, P * t : P * (t + 1)] for t in range(count)]
 
         def turn(out, block, start=True, stop=True):
@@ -216,6 +216,11 @@ def tile_picked_ljpot_none_po_kernel(
                 force[u] = tile("force%d" % u, [S], F32)
             engine.tensor_tensor(force[u][:, span(part)], m[u][:, span(part)], s[u][:, span(part)], MULT)
 
+        def last_forces(u):
+            for k in range(2):
+                block = slice(PIECE + P * k, PIECE + P * (k + 1))
+                nc.vector.tensor_tensor(force[u][:, block], m[u][:, block], s[u][:, block], MULT)
+
         def turn_back(u, order=(0, 1)):
             for i in order:
                 t, c = units[u][i]
@@ -282,25 +287,25 @@ def tile_picked_ljpot_none_po_kernel(
         root(0)
         differences(3, 1)
         differences(4, 3)
-        factors(0)
-        piece("vector", 0, 3, "soft0")
+        factors(0, lambda: piece("vector", 0, 3, "denom2_0", (0,)))
+        piece("vector", 0, 3, ks=(1,))
         strengths(2, 6)
-        gain = tile("gain", [PACK], F32, "denom2_0")
-        nc.gpsimd.tensor_tensor(gain[:], gn_sb[:], signs[:], MULT)
-        forces(nc.gpsimd, 0)
         denominator(1)
+        w2_plane = deal("w2_plane", w2_raw_plane, U8, 0, 4, "p t m", "d2_1", nc.gpsimd)
+        forces(nc.gpsimd, 0)
         square(2)
         root(1)
-        factors(1)
-        piece("vector", 1, 3, "soft1")
+        factors(1, lambda: piece("vector", 1, 3, "denom2_1", (0,)))
+        piece("vector", 1, 3, ks=(1,))
         forces(nc.gpsimd, 1)
         denominator(2)
         square(3)
         root(2)
         differences(5, 5)
-        factors(2)
-        w2_plane = deal("w2_plane", w2_raw_plane, U8, 0, 4, "p t m", "soft2")
-        piece("vector", 2, 3, "denom2_2")
+        factors(2, lambda: piece("vector", 2, 3, "denom2_2", (0,)))
+        piece("vector", 2, 3, ks=(1,))
+        gain = tile("gain", [PACK], F32, "soft2")
+        nc.gpsimd.tensor_tensor(gain[:], gn_sb[:], signs[:], MULT)
         forces(nc.gpsimd, 2)
         strengths(4, 4)
         differences(6, 2)
@@ -311,12 +316,12 @@ def tile_picked_ljpot_none_po_kernel(
         denominator(3)
         square(4)
         root(3)
-        factors(3)
+        factors(3, lambda: piece("vector", 3, 3, "denom2_3", (0,)))
         forces(nc.gpsimd, 3)
         denominator(4)
         square(5)
         root(4)
-        piece("scalar", 3, 3, "d2_4")
+        piece("scalar", 3, 3, ks=(1,))
         factors(4)
         weighted(0, "soft4")
         forces(nc.gpsimd, 4)
@@ -349,7 +354,7 @@ def tile_picked_ljpot_none_po_kernel(
         factors(7)
         forces(nc.vector, 6, first)
         forces(nc.vector, 7, first)
-        forces(nc.vector, 7, second)
+        last_forces(7)
         z_bank[3] = bank("z_bank3", 5)
         turn_back(6, (1, 0))
         turn_back(7)
@@ -364,7 +369,7 @@ def tile_picked_ljpot_none_po_kernel(
         weighted(3, "denom2_7")
         quantized(3)
         planes(1)
-        layer(3, [2, 6])
+        layer(3, [2, 3, 7, 6])
         stored(nc.sync, 2)
         stored(nc.scalar, 3)
         for c in range(2, 4):

@@ -152,19 +152,18 @@ def tile_picked_ljpot_none_po_kernel(
             for k in ks:
                 partners = y_window[t][:].indirect(lists[k][:, 8 * c : 8 * (c + count)])
                 if engine == "scalar":
-                    nc.scalar.activation(out=held[:, k, :], in_=partners, func=ACT.Copy, scale=-1.0)
+                    nc.scalar.activation(out=held[:, k - ks[0], :], in_=partners, func=ACT.Copy, scale=-1.0)
                 elif engine == "vector":
-                    nc.vector.tensor_scalar(out=held[:, k, :], in0=partners, scalar1=-1.0, scalar2=0.0, op0=MULT, op1=ADD)
+                    nc.vector.tensor_scalar(out=held[:, k - ks[0], :], in0=partners, scalar1=-1.0, scalar2=0.0, op0=MULT, op1=ADD)
                 else:
-                    nc.vector.tensor_tensor(held[:, k, :], partners, own, SUBTRACT)
+                    nc.vector.tensor_tensor(held[:, k - ks[0], :], partners, own, SUBTRACT)
                     for n in range(count):
                         fused.add((t, c + n))
-            for n in range(count):
-                fetched[t, c + n] = held[:, :, P * n : P * (n + 1)]
+                for n in range(count):
+                    fetched[t, c + n, k] = held[:, k - ks[0], P * n : P * (n + 1)]
 
         def piece(engine, t, c, tag=None, ks=(0, 1)):
-            held = fetched[t, c] if (t, c) in fetched else tile("fetched%d_%d" % (t, c), [2, P], F32, tag)
-            fetch(engine, t, c, 1, held, ks)
+            fetch(engine, t, c, 1, tile("fetched%d_%d_%d" % (t, c, ks[0]), [len(ks), P], F32, tag), ks)
 
         def differences(u, number):
             d_bank[u] = bank("d_bank%d" % u, number)
@@ -172,7 +171,7 @@ def tile_picked_ljpot_none_po_kernel(
             steps = []
             for i, k in ((0, 0), (1, 0), (0, 1), (1, 1)) if u < 2 else ((0, 0), (0, 1), (1, 0), (1, 1)):
                 t, c = units[u][i]
-                steps.append((blocks[:, i, k, :], fetched[t, c][:, k, :]))
+                steps.append((blocks[:, i, k, :], fetched[t, c, k]))
                 if (t, c) not in fused:
                     steps.append((blocks[:, i, k, :], y_window[t][:, P * c : P * (c + 1)]))
             for n, (out, block) in enumerate(steps):
@@ -276,6 +275,8 @@ def tile_picked_ljpot_none_po_kernel(
         fetch("fused", 2, 1, 2, tile("fetched2_1", [2, HALF], F32), own=y_own[2][:, P:])
         for t in range(2):
             fetch("fused", t, 2, 1, tile("fetched%d_2" % t, [2, P], F32), own=third[:, t, :])
+        gain = tile("gain", [PACK], F32, "x_codes")
+        nc.gpsimd.tensor_tensor(gain[:], gn_sb[:], signs[:], MULT)
         square(0)
         for c in range(2):
             piece("scalar", 3, c)
@@ -288,7 +289,7 @@ def tile_picked_ljpot_none_po_kernel(
         differences(3, 1)
         differences(4, 3)
         factors(0, lambda: piece("vector", 0, 3, "denom2_0", (0,)))
-        piece("vector", 0, 3, ks=(1,))
+        piece("vector", 0, 3, "soft0", (1,))
         strengths(2, 6)
         denominator(1)
         w2_plane = deal("w2_plane", w2_raw_plane, U8, 0, 4, "p t m", "d2_1", nc.gpsimd)
@@ -296,16 +297,14 @@ def tile_picked_ljpot_none_po_kernel(
         square(2)
         root(1)
         factors(1, lambda: piece("vector", 1, 3, "denom2_1", (0,)))
-        piece("vector", 1, 3, ks=(1,))
+        piece("vector", 1, 3, "soft1", (1,))
         forces(nc.gpsimd, 1)
         denominator(2)
         square(3)
         root(2)
         differences(5, 5)
         factors(2, lambda: piece("vector", 2, 3, "denom2_2", (0,)))
-        piece("vector", 2, 3, ks=(1,))
-        gain = tile("gain", [PACK], F32, "soft2")
-        nc.gpsimd.tensor_tensor(gain[:], gn_sb[:], signs[:], MULT)
+        piece("vector", 2, 3, "soft2", (1,))
         forces(nc.gpsimd, 2)
         strengths(4, 4)
         differences(6, 2)
@@ -321,7 +320,7 @@ def tile_picked_ljpot_none_po_kernel(
         denominator(4)
         square(5)
         root(4)
-        piece("scalar", 3, 3, ks=(1,))
+        piece("scalar", 3, 3, "d2_4", (1,))
         factors(4)
         weighted(0, "soft4")
         forces(nc.gpsimd, 4)

@@ -81,14 +81,10 @@ def tile_picked_ljpot_none_po_kernel(
         nc.sync.dma_start(out=gn_sb[:], in_=gn.rearrange("(p t) o -> p (t o)", t=PACK))
         load_plane(nc.sync, w2_raw_plane, w2_scales)
 
-        warm = tile("warm", [2], F32)
-        nc.gpsimd.memset(warm[:, 0:1], 1.0)
-        nc.scalar.activation(out=warm[:, 1:2], in_=warm[:, 0:1], func=ACT.Abs_reciprocal_sqrt)
         identity = tile("identity", [P], F32)
         make_identity(nc, identity[:])
-        signs = tile("signs", [PACK], F32)
-        nc.gpsimd.memset(signs[:, :3], -1.0)
-        nc.gpsimd.memset(signs[:, 3:], 1.0)
+        warm = tile("warm", [1], F32)
+        nc.scalar.activation(out=warm[:], in_=identity[:, 0:1], func=ACT.Abs_reciprocal_sqrt, bias=1.0)
 
         def deal(name, raw, dtype, first, count, order, tag=None, engine=nc.vector):
             dealt = tile(name, [count * P], I32 if dtype == U32 else U8, tag)
@@ -276,7 +272,8 @@ def tile_picked_ljpot_none_po_kernel(
         for t in range(2):
             fetch("fused", t, 2, 1, tile("fetched%d_2" % t, [2, P], F32), own=third[:, t, :])
         gain = tile("gain", [PACK], F32, "x_codes")
-        nc.gpsimd.tensor_tensor(gain[:], gn_sb[:], signs[:], MULT)
+        for slabs, sign in ((slice(0, 3), -1.0), (slice(3, 4), 1.0)):
+            nc.gpsimd.tensor_scalar(out=gain[:, slabs], in0=gn_sb[:, slabs], scalar1=sign, scalar2=0.0, op0=MULT, op1=ADD)
         square(0)
         for c in range(2):
             piece("scalar", 3, c)

@@ -27,11 +27,10 @@ def words_view(words):
     return words[0].rearrange("p n t -> p (n t)").bitcast(I32)
 
 
-def load_plane(queue, plane, scales):
+def load_rows(queues, landing, scales):
     rows = scales[0].bitcast(I32)
-    for quad in range(4):
-        four = rows[4 * quad : 4 * quad + 4, :]
-        queue.dma_start(out=plane[32 * quad : 32 * quad + 32, :].bitcast(I32), in_=four.unsqueeze(0).to_broadcast([8, 4, four.shape[1]]))
+    for r in range(4):
+        queues[r % len(queues)].dma_start(out=landing[r:P:32, :], in_=rows[r:16:4, :])
 
 
 def tile_picked_ljpot_none_po_kernel(
@@ -62,15 +61,15 @@ def tile_picked_ljpot_none_po_kernel(
         q_sb = {(h, t): tile("q%d_%d" % (h, t), [2, HALF], F32) for h in range(2) for t in (0, 2)}
 
         x_rows = tile("x_rows", [T // 4], I32)
-        for r in range(4):
-            (nc.scalar if r % 2 else nc.sync).dma_start(out=x_rows[r:P:32, :], in_=x_scales[0].bitcast(I32)[r:16:4, :])
-        nc.vector.memset(x_plane[:].bitcast(I32), 0)
+        load_rows((nc.sync, nc.scalar), x_rows, x_scales)
+        for plane in (w1_raw_plane, w2_raw_plane, x_plane):
+            nc.vector.memset(plane[:].bitcast(I32), 0)
         for quad in range(4):
             rows = slice(32 * quad, 32 * quad + 4)
             nc.vector.tensor_copy(out=x_plane[rows, :].bitcast(I32), in_=x_rows[rows, :])
         nc.sync.dma_start(offs_sb[:], offs)
         nc.sync.dma_start(out=x_table[:], in_=words_view(x_words))
-        load_plane(nc.sync, w1_raw_plane, w1_scales)
+        load_rows((nc.sync,), w1_raw_plane[:].bitcast(I32), w1_scales)
         nc.sync.dma_start(out=w1_raw[:], in_=words_view(w1_words))
         nc.sync.dma_start(out=q_sb[0, 0][:], in_=q_rows[:, 0:2, :HALF])
         nc.sync.dma_start(p1_sb[:], p1)
@@ -79,7 +78,7 @@ def tile_picked_ljpot_none_po_kernel(
         for h, t in ((0, 2), (1, 0), (1, 2)):
             nc.sync.dma_start(out=q_sb[h, t][:], in_=q_rows[:, t : t + 2, HALF * h : HALF * (h + 1)])
         nc.sync.dma_start(out=gn_sb[:], in_=gn.rearrange("(p t) o -> p (t o)", t=PACK))
-        load_plane(nc.sync, w2_raw_plane, w2_scales)
+        load_rows((nc.sync,), w2_raw_plane[:].bitcast(I32), w2_scales)
 
         identity = tile("identity", [P], F32)
         make_identity(nc, identity[:])

@@ -61,7 +61,8 @@ def tile_picked_ljpot_none_po_kernel(
         q_sb = {(h, t): tile("q%d_%d" % (h, t), [2, HALF], F32) for h in range(2) for t in (0, 2)}
 
         x_rows = tile("x_rows", [T // 4], I32)
-        load_rows((nc.sync, nc.scalar), x_rows, x_scales)
+        for quad in range(4):
+            (nc.scalar if quad % 2 else nc.sync).dma_start(out=x_rows[32 * quad : 32 * quad + 4, :], in_=x_scales[0].bitcast(I32)[4 * quad : 4 * quad + 4, :])
         for plane in (w1_raw_plane, w2_raw_plane, x_plane):
             nc.vector.memset(plane[:].bitcast(I32), 0)
         for quad in range(4):

from contextlib import ExitStack

import concourse.mybir as mybir
from concourse.masks import make_identity

F32 = mybir.dt.float32
BF16 = mybir.dt.bfloat16
I32 = mybir.dt.int32
U32 = mybir.dt.uint32
U16 = mybir.dt.uint16
U8 = mybir.dt.uint8
FP8X4 = mybir.dt.float8_e4m3fn_x4
ACT = mybir.ActivationFunctionType
MULT = mybir.AluOpType.mult
ADD = mybir.AluOpType.add
SUBTRACT = mybir.AluOpType.subtract

P = 128
PACK = 4
T = 2048
S = 512
HALF = S // 2
FLOPS = 2 * 2 * 512 * 512 * 512


def words_view(words):
    return words[0].rearrange("p n t -> p (n t)").bitcast(I32)


def load_rows(queues, landing, scales):
    rows = scales[0].bitcast(I32)
    for r in range(4):
        queues[r % len(queues)].dma_start(out=landing[r:P:32, :], in_=rows[r:16:4, :])


def tile_picked_ljpot_none_po_kernel(
    tc, x_words, x_scales, w1_words, w1_scales, q, gn, w2_words, w2_scales, offs, p1, p2, out_0, out_1, out_2
):
    nc = tc.nc
    with ExitStack() as ctx:
        keep = ctx.enter_context(tc.tile_pool(name="keep", bufs=1))
        psum = ctx.enter_context(tc.psum_pool(name="psum", bufs=1))

        def tile(name, shape, dtype, tag=None):
            return keep.tile([P] + shape, dtype, name=name, tag=tag or name, align_bytes=64)

        def bank(name, number):
            return psum.tile([P, S], F32, name=name, tag="bank%d" % number)

        offs_sb = keep.tile([P, S // 16], U16, name="offs_sb")
        p1_sb = keep.tile([P, S // 16], U16, name="p1_sb")
        p2_sb = keep.tile([P, S // 16], U16, name="p2_sb")
        x_table = tile("x_table", [T], I32)
        x_plane = tile("x_plane", [T], U8)
        w1_raw = tile("w1_raw", [S], I32)
        w2_raw = tile("w2_raw", [S], I32)
        w1_raw_plane = tile("w1_raw_plane", [S], U8)
        w2_raw_plane = tile("w2_raw_plane", [S], U8)
        gn_sb = tile("gn_sb", [PACK], F32)
        q_rows = q.rearrange("(p t) j -> p t j", t=PACK)
        q_sb = {(h, t): tile("q%d_%d" % (h, t), [2, HALF], F32) for h in range(2) for t in (0, 2)}

        x_rows = tile("x_rows", [T // 4], I32)
        for quad in range(4):
            (nc.scalar if quad % 2 else nc.sync).dma_start(out=x_rows[32 * quad : 32 * quad + 4, :], in_=x_scales[0].bitcast(I32)[4 * quad : 4 * quad + 4, :])
        for plane in (w1_raw_plane, w2_raw_plane, x_plane):
            nc.vector.memset(plane[:].bitcast(I32), 0)
        for quad in range(4):
            rows = slice(32 * quad, 32 * quad + 4)
            nc.vector.tensor_copy(out=x_plane[rows, :].bitcast(I32), in_=x_rows[rows, :])
        nc.sync.dma_start(offs_sb[:], offs)
        nc.sync.dma_start(out=x_table[:], in_=words_view(x_words))
        load_rows((nc.sync,), w1_raw_plane[:].bitcast(I32), w1_scales)
        nc.sync.dma_start(out=w1_raw[:], in_=words_view(w1_words))
        nc.sync.dma_start(out=q_sb[0, 0][:], in_=q_rows[:, 0:2, :HALF])
        nc.sync.dma_start(p1_sb[:], p1)
        nc.sync.dma_start(p2_sb[:], p2)
        nc.sync.dma_start(out=w2_raw[:], in_=words_view(w2_words))
        for h, t in ((0, 2), (1, 0), (1, 2)):
            nc.sync.dma_start(out=q_sb[h, t][:], in_=q_rows[:, t : t + 2, HALF * h : HALF * (h + 1)])
        nc.sync.dma_start(out=gn_sb[:], in_=gn.rearrange("(p t) o -> p (t o)", t=PACK))
        load_rows((nc.sync,), w2_raw_plane[:].bitcast(I32), w2_scales)

        identity = tile("identity", [P], F32)
        make_identity(nc, identity[:])
        warm = tile("warm", [1], F32)
        nc.scalar.activation(out=warm[:], in_=identity[:, 0:1], func=ACT.Abs_reciprocal_sqrt, bias=1.0)

        def deal(name, raw, dtype, first, count, order, tag=None, engine=nc.vector):
            dealt = tile(name, [count * P], I32 if dtype == U32 else U8, tag)
            source = raw[:].bitcast(dtype).rearrange("p (m t) -> p m t", t=PACK)[:, :, first : first + count]
            engine.tensor_copy(out=dealt[:].bitcast(dtype).rearrange("p (t m) -> " + order, t=count), in_=source.rearrange("p m t -> " + order))
            return [dealt[:, P * t : P * (t + 1)] for t in range(count)]

        def turn(out, block, start=True, stop=True):
            nc.tensor.matmul(out=out, lhsT=block, rhs=identity[:], start=start, stop=stop, is_transpose=True)

        def product(out, codes, plane, moving, moving_plane):
            nc.tensor.matmul_mx(
                out=out, lhsT=codes.bitcast(FP8X4), lhsT_scale=plane, rhs=moving.bitcast(FP8X4), rhs_scale=moving_plane, start=True, stop=True
            )

        x_picked_plane = tile("x_picked_plane", [S], U8)
        nc.vector.tensor_copy(x_picked_plane[:], x_plane[:].indirect(offs_sb[:]))
        x_codes = tile("x_codes", [S], I32)
        for h in range(2):
            nc.vector.tensor_copy(x_codes[:, HALF * h : HALF * (h + 1)].bitcast(U32), x_table[:].bitcast(U32).indirect(offs_sb[:, 16 * h : 16 * (h + 1)]))
        w1_plane = deal("w1_plane0", w1_raw_plane, U8, 0, 1, "p t m")
        w1_codes = deal("w1_codes0", w1_raw, U32, 0, 1, "p m t")
        w1_codes = w1_codes + deal("w1_codes", w1_raw, U32, 1, 3, "p m t")
        w1_plane = w1_plane + deal("w1_plane", w1_raw_plane, U8, 1, 3, "p t m", "w1_raw")
        w2_codes = deal("w2_codes", w2_raw, U32, 0, 4, "p m t", "w1_raw_plane")

        y_window = [tile("y_window%d" % t, [S], F32) for t in range(PACK)]
        halves = [slice(0, HALF), slice(HALF, S)]
        y_banks = [bank("y%d" % n, n) for n in range(6)]
        for t in range(2):
            for h in range(2):
                product(y_banks[2 * t + h][:, :HALF], w1_codes[t], w1_plane[t], x_codes[:, halves[h]], x_picked_plane[:, halves[h]])
        for t in range(2, PACK):
            product(y_banks[t + 2][:], w1_codes[t], w1_plane[t], x_codes[:], x_picked_plane[:])
        y_own = [tile("y_own%d" % t, [HALF], F32) for t in range(2)]
        for t in range(2):
            nc.scalar.copy(out=y_window[t][:, halves[0]], in_=y_banks[2 * t][:, :HALF])
            nc.scalar.copy(out=y_own[t][:], in_=y_banks[2 * t][:, :HALF])
            (nc.scalar.copy if t else nc.vector.tensor_copy)(out=y_window[t][:, halves[1]], in_=y_banks[2 * t + 1][:, :HALF])
        y_own.append(tile("y_own2", [3 * P], F32))
        nc.scalar.copy(out=y_window[2][:], in_=y_banks[4][:])
        nc.scalar.copy(out=y_own[2][:], in_=y_banks[4][:, : 3 * P])
        third = tile("y_third", [2, P], F32, "x_codes")
        for t in range(2):
            nc.scalar.copy(out=third[:, t, :], in_=y_banks[2 * t + 1][:, :P])
        nc.scalar.copy(out=y_window[3][:], in_=y_banks[5][:])

        lists = (p1_sb, p2_sb)
        fetched, d_bank, q_bank, d2, denom2, soft, s, m, force, z_bank = {}, {}, {}, {}, {}, {}, {}, {}, {}, {}
        whole, first, second = slice(0, 2), slice(0, 1), slice(1, 2)
        PIECE = 2 * P

        units = [[(0, 0), (0, 1)], [(1, 0), (1, 1)]] + [[(t, c), (t + 1, c)] for t, c in ((2, 0), (2, 1), (0, 2), (2, 2), (0, 3), (2, 3))]

        fused = set()

        def span(part):
            return slice(PIECE * part.start, PIECE * part.stop)

        def fetch(engine, t, c, count, held, ks=(0, 1), own=None):
            for k in ks:
                partners = y_window[t][:].indirect(lists[k][:, 8 * c : 8 * (c + count)])
                if engine == "scalar":
                    nc.scalar.activation(out=held[:, k - ks[0], :], in_=partners, func=ACT.Copy, scale=-1.0)
                elif engine == "vector":
                    nc.vector.tensor_scalar(out=held[:, k - ks[0], :], in0=partners, scalar1=-1.0, scalar2=0.0, op0=MULT, op1=ADD)
                else:
                    nc.vector.tensor_tensor(held[:, k - ks[0], :], partners, own, SUBTRACT)
                    for n in range(count):
                        fused.add((t, c + n))
                for n in range(count):
                    fetched[t, c + n, k] = held[:, k - ks[0], P * n : P * (n + 1)]

        def piece(engine, t, c, tag=None, ks=(0, 1)):
            fetch(engine, t, c, 1, tile("fetched%d_%d_%d" % (t, c, ks[0]), [len(ks), P], F32, tag), ks)

        def differences(u, number):
            d_bank[u] = bank("d_bank%d" % u, number)
            blocks = d_bank[u][:].rearrange("j (i k p) -> j i k p", i=2, k=2)
            steps = []
            for i, k in ((0, 0), (1, 0), (0, 1), (1, 1)) if u < 2 else ((0, 0), (0, 1), (1, 0), (1, 1)):
                t, c = units[u][i]
                steps.append((blocks[:, i, k, :], fetched[t, c, k]))
                if (t, c) not in fused:
                    steps.append((blocks[:, i, k, :], y_window[t][:, P * c : P * (c + 1)]))
            for n, (out, block) in enumerate(steps):
                turn(out, block, n == 0, n == len(steps) - 1)

        def strengths(u, number):
            held = bank("q_bank%d" % u, number)
            q_bank[u], q_bank[u + 1] = held[:, :HALF], held[:, HALF:]
            for n, (t, c) in enumerate(units[u] + units[u + 1]):
                turn(held[:, P * n : P * (n + 1)], q_sb[c // 2, t - t % 2][:, t % 2, P * (c % 2) : P * (c % 2 + 1)])

        def square(u, parts=(whole,)):
            d2[u] = tile("d2_%d" % u, [S], F32)
            for part in parts:
                nc.scalar.activation(out=d2[u][:, span(part)], in_=d_bank[u][:, span(part)], func=ACT.Square)

        def denominator(u, parts=(whole,)):
            denom2[u] = tile("denom2_%d" % u, [S], F32)
            for part in parts:
                nc.scalar.activation(out=denom2[u][:, span(part)], in_=d2[u][:, span(part)], func=ACT.Square, bias=1.0)

        def root(u, parts=(whole,)):
            soft[u] = tile("soft%d" % u, [S], F32)
            for part in parts:
                nc.scalar.activation(out=soft[u][:, span(part)], in_=denom2[u][:, span(part)], func=ACT.Abs_reciprocal_sqrt)

        def factors(u, between=None):
            s[u], m[u] = tile("s%d" % u, [S], F32), tile("m%d" % u, [S], F32)
            strength = q_bank[u].rearrange("j (i p) -> j i p", i=2).unsqueeze(2).to_broadcast([P, 2, 2, P])
            paired = lambda view: view[:].rearrange("j (i k p) -> j i k p", i=2, k=2)
            parts = (whole,) if between else (first, second)
            for part in parts:
                nc.vector.tensor_tensor(paired(s[u])[:, part], paired(soft[u])[:, part], strength[:, part], MULT)
            if between:
                between()
            for part in parts:
                nc.vector.scalar_tensor_tensor(m[u][:, span(part)], s[u][:, span(part)], 1.0, d_bank[u][:, span(part)], SUBTRACT, MULT)

        def forces(engine, u, part=whole):
            if u not in force:
                force[u] = tile("force%d" % u, [S], F32)
            engine.tensor_tensor(force[u][:, span(part)], m[u][:, span(part)], s[u][:, span(part)], MULT)

        def last_forces(u):
            for k in range(2):
                block = slice(PIECE + P * k, PIECE + P * (k + 1))
                nc.vector.tensor_tensor(force[u][:, block], m[u][:, block], s[u][:, block], MULT)

        def turn_back(u, order=(0, 1)):
            for i in order:
                t, c = units[u][i]
                for k in range(2):
                    turn(z_bank[c][:, P * t : P * (t + 1)], force[u][:, PIECE * i + P * k : PIECE * i + P * (k + 1)], k == 0, k == 1)

        out_plane = tile("out_plane", [S], U8)
        out_codes = tile("out_codes", [S], I32)
        out_rows = out_0.rearrange("(p t) j -> p t j", t=PACK)
        out_words = words_view(out_1)
        z16, z, sums, result, result16 = {}, {}, {}, {}, {}

        def weighted(c, tag=None):
            z16[c] = tile("z16_%d" % c, [P, PACK], BF16, tag)
            turned = z_bank[c][:].rearrange("p (t j) -> p j t", t=PACK)
            factor = gain[:] if c < 3 else gn_sb[:]
            nc.vector.scalar_tensor_tensor(z16[c][:], turned, -1.0, factor.unsqueeze(1).to_broadcast([P, P, PACK]), MULT, MULT)

        def quantized(c, tag=None):
            z[c] = (tile("z_codes%d" % c, [P], I32, tag), tile("z_plane%d" % c, [P], U8))
            nc.vector.quantize_mx(out=z[c][0][:].bitcast(FP8X4), scales=z[c][1][:], in_=z16[c][:].rearrange("p j t -> p (j t)"))

        def layer(c, numbers):
            count = PACK // len(numbers)
            sums[c] = [bank("out_bank%d_%d" % (c, n), n)[:, : count * P].rearrange("p (t j) -> p t j", t=count) for n in numbers]
            for t in range(PACK):
                product(sums[c][t // count][:, t % count, :], w2_codes[t], w2_plane[t], z[c][0][:], z[c][1][:])

        def stored(queue, c, tag=None):
            result[c] = tile("result%d" % c, [PACK, P], F32, tag)
            count = PACK // len(sums[c])
            for n, part in enumerate(sums[c]):
                nc.scalar.copy(out=result[c][:, count * n : count * (n + 1), :], in_=part)
            queue.dma_start(out=out_rows[:, :, P * c : P * (c + 1)], in_=result[c][:])

        def rounded(c, engine, tag=None):
            result16[c] = tile("result16_%d" % c, [P, PACK], BF16, tag)
            if engine == "scalar":
                nc.scalar.copy(out=result16[c][:], in_=sums[c][0].rearrange("p t j -> p j t"))
            else:
                nc.vector.tensor_copy(out=result16[c][:].rearrange("p (c i) t -> p c t i", i=4), in_=result[c][:].rearrange("p t (c i) -> p c t i", i=4))

        def planes(c):
            js = slice(P * c, P * (c + 1))
            nc.vector.quantize_mx(out=out_codes[:, js].bitcast(FP8X4), scales=out_plane[:, js], in_=result16[c][:].rearrange("p j t -> p (j t)"))

        first_half = [tile("fetched%d" % t, [2, HALF], F32) for t in range(2)]
        for t in range(2):
            fetch("fused", t, 0, 2, first_half[t], own=y_own[t][:])
        differences(0, 6)
        differences(1, 7)
        fetch("fused", 2, 0, 1, tile("fetched2_0", [2, P], F32), own=y_own[2][:, :P])
        fetch("fused", 2, 1, 2, tile("fetched2_1", [2, HALF], F32), own=y_own[2][:, P:])
        for t in range(2):
            fetch("fused", t, 2, 1, tile("fetched%d_2" % t, [2, P], F32), own=third[:, t, :])
        gain = tile("gain", [PACK], F32, "x_codes")
        for slabs, sign in ((slice(0, 3), -1.0), (slice(3, 4), 1.0)):
            nc.gpsimd.tensor_scalar(out=gain[:, slabs], in0=gn_sb[:, slabs], scalar1=sign, scalar2=0.0, op0=MULT, op1=ADD)
        square(0)
        for c in range(2):
            piece("scalar", 3, c)
        strengths(0, 4)
        differences(2, 0)
        denominator(0)
        piece("vector", 3, 2, "d2_0")
        square(1)
        root(0)
        differences(3, 1)
        differences(4, 3)
        factors(0, lambda: piece("vector", 0, 3, "denom2_0", (0,)))
        piece("vector", 0, 3, "soft0", (1,))
        strengths(2, 6)
        denominator(1)
        w2_plane = deal("w2_plane", w2_raw_plane, U8, 0, 4, "p t m", "d2_1", nc.gpsimd)
        forces(nc.gpsimd, 0)
        square(2)
        root(1)
        factors(1, lambda: piece("vector", 1, 3, "denom2_1", (0,)))
        piece("vector", 1, 3, "soft1", (1,))
        forces(nc.gpsimd, 1)
        denominator(2)
        square(3)
        root(2)
        differences(5, 5)
        factors(2, lambda: piece("vector", 2, 3, "denom2_2", (0,)))
        piece("vector", 2, 3, "soft2", (1,))
        forces(nc.gpsimd, 2)
        strengths(4, 4)
        differences(6, 2)
        z_bank[0] = bank("z_bank0", 7)
        turn_back(0, (0,))
        turn_back(1, (0,))
        turn_back(2)
        denominator(3)
        square(4)
        root(3)
        factors(3, lambda: piece("vector", 3, 3, "denom2_3", (0,)))
        forces(nc.gpsimd, 3)
        denominator(4)
        square(5)
        root(4)
        piece("scalar", 3, 3, "d2_4", (1,))
        factors(4)
        weighted(0, "soft4")
        forces(nc.gpsimd, 4)
        differences(7, 0)
        z_bank[1] = bank("z_bank1", 1)
        turn_back(0, (1,))
        turn_back(1, (1,))
        turn_back(3)
        strengths(6, 6)
        denominator(5)
        square(6)
        root(5)
        factors(5)
        quantized(0, "soft5")
        weighted(1, "denom2_5")
        forces(nc.gpsimd, 5)
        layer(0, [3])
        z_bank[2] = bank("z_bank2", 7)
        turn_back(4)
        turn_back(5)
        denominator(6)
        square(7)
        root(6)
        factors(6)
        quantized(1, "soft6")
        layer(1, [4])
        forces(nc.gpsimd, 6, second)
        denominator(7, (first, second))
        root(7, (first, second))
        factors(7)
        forces(nc.vector, 6, first)
        forces(nc.vector, 7, first)
        last_forces(7)
        z_bank[3] = bank("z_bank3", 5)
        turn_back(6, (1, 0))
        turn_back(7)
        weighted(2, "soft7")
        stored(nc.sync, 0, "d2_7")
        stored(nc.sync, 1)
        rounded(0, "scalar", "denom2_7")
        planes(0)
        quantized(2)
        rounded(1, "scalar", "soft7")
        layer(2, [1])
        weighted(3, "denom2_7")
        quantized(3)
        planes(1)
        layer(3, [2, 3, 7, 6])
        stored(nc.sync, 2)
        stored(nc.scalar, 3)
        for c in range(2, 4):
            rounded(c, "vector")
        planes(2)
        nc.sync.dma_start(out=out_words[:, : 3 * P], in_=out_codes[:, : 3 * P])
        planes(3)
        nc.sync.dma_start(out=out_words[:, 3 * P :], in_=out_codes[:, 3 * P :])
        for quad in range(4):
            (nc.sync if quad < 2 else nc.scalar).dma_start(out=out_2[0, 4 * quad : 4 * quad + 4, :].bitcast(I32), in_=out_plane[32 * quad : 32 * quad + 4, :].bitcast(I32))
